import numpy as np, ml_dtypes
CORES = [13,21,141,149]
N = 4
BF = ml_dtypes.bfloat16
def gentries(a):
    return np.ascontiguousarray(a.reshape(8, 16, -1).transpose(0, 2, 1)).reshape(8, -1)
def gtable(e):
    e = np.asarray(e); return np.ascontiguousarray(e.reshape(8, -1, 16).transpose(0, 2, 1)).reshape(128, -1).astype(np.int32)
V, L, C, RO, MIN, SH = 960, 8, 5, 3, 3, 3
T = N * V; LN = L // N; H = T // C
def lists(rng):
    return np.argsort(rng.random((8, L, T)), axis=-1).reshape(8, L, C, H)
def turn(pm):
    hl = np.zeros((8, L, T), np.int64)
    np.put_along_axis(hl, pm.reshape(8, L, T), np.broadcast_to(np.tile(np.arange(H), C), (8, L, T)), 2)
    return hl
def parts(rng):
    s = rng.permutation(np.array([24, 48, 64, 96, 128, 160, 200, 256])); lo = rng.integers(0, (257 - s)[:, None], (8, 16))
    x = lo[:, :, None] + rng.integers(0, s[:, None, None], (8, 16, T))
    hits = lo[:, :, None, None] + rng.integers(0, s[:, None, None, None], (8, 16, L, H))
    th = (6 * s[:, None] * rng.random((8, T)) ** 2).astype(np.int64)
    return x, hits, lists(rng), th
def pack(x, hits, pm, th):
    hl = turn(pm).reshape(8, L, N, V).transpose(2, 0, 1, 3).reshape(N, 8, L * V)
    cl = pm.reshape(8, N, LN, C, H).transpose(1, 0, 3, 2, 4).reshape(N, 8, C * LN * H)
    return {"fx": np.ascontiguousarray(x.reshape(8, 16, N, V).transpose(2, 0, 1, 3)).reshape(N, 128, V).astype(np.float32).astype(BF),
            "hv": np.ascontiguousarray(hits.reshape(8, 16, N, LN * H).transpose(2, 0, 1, 3)).reshape(N, 128, LN * H).astype(np.float32).astype(BF),
            "hl": np.stack([gtable(a) for a in hl]), "cl": np.stack([gtable(a) for a in cl]),
            "th": np.ascontiguousarray(th.reshape(8, N, V).transpose(1, 0, 2)).astype(np.int32)}
def contest(x, hits, live, pm):
    out = []
    for l in range(L):
        best = np.full((8, H), 2 ** 24, np.int64)
        for c in range(C):
            t = pm[:, l, c]
            d = np.add.reduce(np.abs(hits[:, :, l] - np.take_along_axis(x, t[:, None, :], 2)), axis=1)
            best = np.minimum(best, np.where(np.take_along_axis(live[:, l], t, 1), d * 4096 + t, 2 ** 24))
        out.append(best & 4095)
    return np.stack(out, axis=1)
def apart(x, b, hl):
    who = np.stack([np.take_along_axis(b[:, l], hl[:, l], 1) for l in range(L)], axis=1)
    e = np.stack([np.add.reduce(np.abs(x - np.take_along_axis(x, who[:, l][:, None, :], 2)), axis=1) for l in range(L)], axis=1)
    return who, e
def classes(rng):
    p = C * np.argsort(rng.random((L, C, H)), axis=2) + np.arange(C)[None, :, None]
    return np.take_along_axis(p, np.argsort(rng.random((L, C, H)), axis=1), axis=1)
def far(rng):
    c = np.arange(T) % C; x = rng.integers(1, 129, (16, T)); x[:, c == 0] = 0
    top = 255 - (rng.random((16, T)) < rng.choice(np.array([0.0, 0.1, 0.3]), T)).astype(np.int64)
    hits = np.full((16, L, H), 255); hits[:, rng.integers(0, L)] = 0
    th = np.where(c == 1, np.add.reduce(top, axis=0) + rng.integers(0, 2, T), 4081)
    return np.where(c == 1, top, x), hits, classes(rng), th
def fall(rng):
    x = 50 * (np.arange(T) % C) + rng.integers(0, 16, (16, T))
    hits = 50 * (np.arange(L) % C)[None, :, None] + rng.integers(0, 16, (16, L, H))
    return x, hits, classes(rng)
def late(rng):
    c = np.arange(T) % C
    x = rng.integers(0, 4, (16, T)) + np.where(c == 0, 0, np.where(c == 1, 208, np.where(c == 2, 200, 100)))
    hits = rng.integers(0, 4, (16, L, H))
    if RO > 2: hits[:, rng.integers(0, L)] += 200
    th = np.where(c == 0, 4081, np.where(c == 1, rng.integers(177, 369, T), 0))
    return x, hits, classes(rng), th
def setup_inputs(rng):
    return pack(*parts(rng))
def setup_inputs_ties(rng):
    x, hits, pm, th = parts(rng); lo = rng.integers(0, 253, (8, 16))
    x = lo[:, :, None] + rng.integers(0, 3, (8, 16, T)); hits = lo[:, :, None, None] + rng.integers(0, 3, (8, 16, L, H))
    for g in (2, 5): x[g] = x[g][:, rng.integers(0, 8, T)]
    e = apart(x, contest(x, hits, np.ones((8, L, T), bool), pm), turn(pm))[1]
    at = np.take_along_axis(e, rng.integers(0, L, (8, 1, T)), 1)[:, 0] + rng.integers(0, 2, (8, T))
    th = np.where(rng.random((8, T)) < 0.5, at, rng.integers(0, 18, (8, T)))
    return pack(x, hits, pm, th)
def setup_inputs_counts(rng):
    x, hits, pm, th = parts(rng)
    w = np.take_along_axis(pm, rng.integers(0, C, (8, L, 1, H)), 2)[:, :, 0]
    hits = np.stack([x[g][:, w[g]] for g in range(8)])
    o = rng.permutation(8); share = np.zeros((8, 1)); share[o[:5], 0] = np.array([1.0, 0.0, 0.2, 0.5, 0.8])
    th = np.where(rng.random((8, T)) < share, 4081, 0)
    for g in o[5:7]: x[g], hits[g], pm[g] = fall(rng)
    th[o[5]] = 4081; th[o[6]] = np.where(np.arange(T) // V == rng.integers(0, N), 4081, 0)
    x[o[7]], hits[o[7]], pm[o[7]], th[o[7]] = late(rng)
    return pack(x, hits, pm, th)
def setup_inputs_ends(rng):
    x, hits, pm, th = parts(rng)
    x = 255 * rng.integers(0, 2, (8, 16, T)); hits = 255 * rng.integers(0, 2, (8, 16, L, H)); th = rng.choice(np.array([0, 1, 1800, 2040, 2041, 2295, 4080, 4081]), (8, T))
    p = np.ascontiguousarray(pm.reshape(8, L, T)); a, z = np.arange(C), T - 1 - np.arange(C)
    for g in range(8):
        for l, h, want in ((0, 0, z), (L - 1, H - 1, a)):
            for c in range(C):
                k = int(np.nonzero(p[g, l] == want[c])[0][0]); m = c * H + h; was = int(p[g, l, m])
                p[g, l, m] = int(want[c]); p[g, l, k] = was if k != m else int(want[c])
    x[:, :, z] = 0; hits[:, :, 0, 0] = 255; x[:, :, a] = 255; hits[:, :, L - 1, H - 1] = 0
    for t in (z, a): th[:, t] = (np.arange(8) & 1)[:, None]
    p = p.reshape(8, L, C, H); o = rng.permutation(8)
    for g in o[:2]: x[g], hits[g], p[g], th[g] = far(rng)
    x[o[1]] = 255 - x[o[1]]; hits[o[1]] = 255 - hits[o[1]]
    g = int(o[2]); hits[g] = 0; x[g] = 255 - (rng.random((16, T)) < 0.08).astype(np.int64)
    x[g, rng.integers(0, 16, T // 8), rng.permutation(T)[:T // 8]] = 0
    th[g] = rng.choice(np.array([0, 1, 2, 3, 255, 256]), T)
    return pack(x, hits, p, th)
def setup_inputs_alike(rng):
    x, hits, pm, th = parts(rng); pm = np.ascontiguousarray(pm)
    pm[0] = np.arange(T).reshape(C, H); pm[1] = (np.arange(T).reshape(H, C)[:, ::-1]).T; pm[3] = pm[3, 0]; pm[4] = np.arange(T)[::-1].reshape(C, H)
    for g in (0, 4, 6): x[g] = np.tile(x[g][:, :V], (1, N))
    for g in (0, 5): th[g] = rng.integers(0, 2, T)
    x[5] = x[5][:, rng.integers(0, 4, T)]; hits[7] = hits[7][:, :, :1]
    return pack(x, hits, pm, th)
def setup_inputs_spread(rng):
    x, hits, pm, th = parts(rng)
    x = (np.exp2(8 * rng.random((8, 1, T))) * rng.random((8, 16, T))).astype(np.int64)
    hits = (np.exp2(8 * rng.random((8, 1, L, H))) * rng.random((8, 16, L, H))).astype(np.int64)
    th = np.minimum(np.exp2(12 * rng.random((8, T))).astype(np.int64) - 1, 4081)
    return pack(x, hits, pm, th)
def claims(hl, cl):
    a = np.stack([gentries(q) for q in hl]).astype(np.int64).reshape(N, 8, L, V).transpose(1, 2, 0, 3).reshape(8, L, T)
    b = np.stack([gentries(q) for q in cl]).astype(np.int64).reshape(N, 8, C, LN, H).transpose(1, 0, 3, 2, 4).reshape(8, L, C, H)
    return a, b
def check_inputs(d):
    bad = []
    for k in ("fx", "hv"):
        v = d[k].astype(np.float32)
        if not np.all((v >= 0) & (v <= 255) & (v == np.floor(v))): bad.append("whole numbers of " + k)
    for k, hi in (("hl", H - 1), ("cl", T - 1), ("th", 4081)):
        if np.min(d[k]) < 0 or np.max(d[k]) > hi: bad.append("range of " + k)
    if not bad:
        a, b = claims(d["hl"], d["cl"]); b = b.reshape(8, L, T)
        if not np.all(np.sort(b, axis=-1) == np.arange(T)) or not np.all(np.take_along_axis(a, b, 2) == np.tile(np.arange(H), C)): bad.append("claimants of the hits")
    return bad
def reference(fx, hv, hl, cl, th):
    x = fx.astype(np.float32).astype(np.int64).reshape(N, 8, 16, V).transpose(1, 2, 0, 3).reshape(8, 16, T)
    hits = hv.astype(np.float32).astype(np.int64).reshape(N, 8, 16, LN * H).transpose(1, 2, 0, 3).reshape(8, 16, L, H)
    mine, pm = claims(hl, cl); t = th.astype(np.int64).transpose(1, 0, 2).reshape(8, 1, T)
    live = np.ones((8, L, T), bool)
    for rnd in range(RO):
        b = contest(x, hits, live, pm); who, e = apart(x, b, mine)
        live = live & ((who == np.arange(T)) | (e >= t))
        n = np.add.reduce(live.astype(np.int64), axis=1)
        live = live & (n >= MIN)[:, None, :]; n = np.where(n >= MIN, n, 0)
        tot = (L - n)[:, None, :] * x
        for l in range(L): tot = tot + live[:, l][:, None, :] * np.take_along_axis(hits[:, :, l], mine[:, l][:, None, :], 2)
        x = tot >> SH
    return {"yx": np.ascontiguousarray(x.reshape(8, 16, N, V).transpose(2, 0, 1, 3)).reshape(N, 128, V).astype(np.float32).astype(BF),
            "yl": np.ascontiguousarray(live.reshape(8, L, N, V).transpose(2, 0, 1, 3)).reshape(N, 8, L * V).astype(np.float32).astype(BF)}

@@ -1,0 +1,703 @@
+from concourse.bass import DstId, RemoteDMATransfer
+from concourse.mybir import AluOpType, ActivationFunctionType
+
+N, V, HQ, C, RO = 4, 960, 1536, 5, 3
+NT = N * V
+XB, IB, OB = 624, 256, 360
+PAD = 16
+BLK = PAD + NT
+H0 = RO * BLK
+BIG = 2.0 ** 23
+K = 32768.0
+OFF = -1.5 * K
+CFG = {"chunks": [(0, 48), (48, 72), (72, 96)],
+       "p5v": [(1, 3)], "p5l": [(1, 2), (1, 3)], "big": 2, "thv": 2,
+       "g": 1.5, "hop": 140.0, "pe": 0.42, "direct": 9000.0, "relayed": 12500.0,
+       "its": 8000, "seed": 1, "temp": 100.0, "moves": 3, "noise": 8000.0, "gap": 0.3, "eq0": 21.0, "tth": (4.0, 12.0)}
+CYC, T_DMA = 0.83, 2200.0
+
+F32, BF, I32, U16 = "float32", "bfloat16", "int32", "uint16"
+SCRATCH = {
+    "sx": ("dram", [N, 128, 240], BF), "sh": ("dram", [N, 128, 384], BF), "sc": ("dram", [N, 128, 120], I32),
+    "sl": ("dram", [N, 128, 120], I32), "st": ("dram", [N, 128, 15], I32),
+    "rx": ("dram", [128, 240], BF), "rh": ("dram", [128, 384], BF), "rc": ("dram", [128, 120], I32),
+    "ro": ("dram", [128, OB], BF), "lth": ("dram", [2, N, 128, 15], BF),
+    "m1": ("sbuf", [128, 2, 96], F32),
+}
+for _names, _shape, _dt in (
+        ("lb", [N * XB], BF), ("li", [N * IB], I32), ("lh ll", [N * IB], BF), ("lo res", [N * OB], BF), ("win", [H0 + HQ], F32),
+        ("dd ab eq g5", [7680], BF), ("db", [HQ], BF), ("iot", [NT], F32), ("thw", [NT], BF), ("m2", [96], F32),
+        ("mi ma", [96], I32), ("bi", [96], U16), ("cu hw ix", [480], U16), ("idw", [768], F32), ("ihi ilo", [768], BF),
+        ("ww0 ww1", [384], F32), ("hli hls", [480], I32), ("xf", [V], F32), ("al0 al1 als alt", [240], F32),
+        ("cx", [176], F32), ("cx2 cx3", [128], F32), ("pc", [2], I32), ("pi", [8], I32), ("pf tg cc", [16], F32),
+        ("tf tf0 tf48", [4], F32), ("tj tj0", [8], F32), ("me", [132], BF), ("mf", [4 * 176], BF), ("mr", [4 * 128], BF),
+        ("mg", [8 * 136], BF), ("clf thc key", [C, 96], F32), ("nb nl fl chi clo thi tlo", [C, 96], BF),
+        ("ki si0 hp0 hp1 hp2 sfp home al2 t1 t2", [480], F32), ("mz shi slo fb fc", [480], BF), ("mcb mck mch", [144], BF),
+        ("mi1 mni mn2 mnb mi4 mi8 mon msum monp monk mo8 mo8p mp", [128], BF)):
+    for _n in _names.split():
+        SCRATCH[_n] = ("sbuf", [128] + _shape, _dt)
+for _k in range(8):
+    SCRATCH["ps%d" % _k] = ("psum", [128, 512], F32)
+
+SEMAPHORES = (["eV", "eA", "eP", "eG", "sent", "rin1", "rin2", "rout"]
+              + ["a%s%d" % (k, s) for k in "xhclo" for s in range(N)] + ["d%d" % k for k in range(52)])
+
+
+def _mask(engines):
+    return sum(1 << e for e in engines)
+
+
+def _relays(T, topo):
+    plan = {}
+    for s, cs in enumerate(T.cores):
+        far = [d for d, cd in enumerate(T.cores) if d != s and not topo.may_write(cs, cd)]
+        free = sorted((c for c in topo.cores_of(cs) if T.rank_of(c) is None), key=lambda c: (topo.die(c) != topo.die(cs), c))
+        got = {d: [] for d in far}
+        for _ in range(2):
+            for d in far:
+                c = [c for c in free if topo.may_write(c, T.cores[d])][0]
+                free.remove(c)
+                got[d].append(c)
+        for d in far:
+            plan[(s, d)] = tuple(got[d])
+    return plan
+
+
+def _lanes(T, topo, plan, s):
+    far = [d for d in range(N) if (s, d) in plan]
+    near = [d for d in range(N) if d != s and d not in far][0]
+    off = topo.engines(T.cores[s], T.cores[near])
+    rest = [e for e in topo.engines(T.cores[s], plan[(s, far[0])][0]) if e not in off]
+    h, q = len(rest) // 2, len(off) // 4
+    lanes = {("x", near): off[2 * q:3 * q], ("c", near): off[3 * q:], ("h", near): off, ("l", near): off, ("t", near): off[:1]}
+    for j, d in enumerate(far):
+        lanes["x", d] = lanes["h", d] = lanes["l", d] = rest[j * h:(j + 1) * h]
+        lanes["c", d] = off[j * q:(j + 1) * q]
+        lanes["t", d] = rest[j * h:j * h + 1]
+    return lanes
+
+
+def _slot(T, piece, s):
+    buf, c0, c1 = {"x": ("lb", 0, 240), "h": ("lb", 240, XB), "c": ("li", 0, 120), "l": ("li", 120, 240), "t": ("li", 240, 255),
+                   "lt": ("li", 120, 255)}[piece]
+    w = XB if buf == "lb" else IB
+    return T[buf][:, s * w + c0:s * w + c1]
+
+
+def _relay_program(g, core, T, topo, plan):
+    for (s, d), pair in plan.items():
+        if core not in pair:
+            continue
+        lanes = _lanes(T, topo, plan, s)
+        out = topo.engines(core, T.cores[d])
+        rid, pid = topo.addr(T.cores[d], core)
+        if core == pair[0]:
+            steps = [(T.sem.rin1, len(lanes["x", d]), _slot(T, "x", s), T.rx[:], "ax"),
+                     (T.sem.rin2, len(lanes["h", d]), _slot(T, "h", s), T.rh[:], "ah"),
+                     (T.sem.rout, len(topo.engines(T.cores[s], core)), T.lo[:, s * OB:(s + 1) * OB], T.ro[:], "ao")]
+        else:
+            steps = [(T.sem.rin1, len(lanes["c", d]), _slot(T, "c", s), T.rc[:], "ac"),
+                     (T.sem.rin2, len(lanes["l", d]) + len(lanes["t", d]), _slot(T, "lt", s), _slot(T, "lt", s), "al")]
+        for sem, n, land, src, name in steps:
+            g.wait_ge(sem, n)
+            g.remote_dma(land, src, T.sem["%s%d" % (name, s)], T.sem.sent, pid, rid, _mask(out))
+        g.wait_ge(T.sem.sent, len(steps) * len(out))
+
+
+_ORDERS = {}
+
+
+def _place(seq, alts, before, first):
+    hop, n = CFG["hop"], len(alts)
+    b0, b1 = {e: [] for e in "VAPGS"}, {e: [] for e in "VAPGS"}
+    start, end, eng = [0.0] * n, [0.0] * n, [None] * n
+    for k in seq:
+        best = None
+        for e, cost in alts[k]:
+            t = first[k]
+            for d, raw, wait in before[k]:
+                u = end[d] + wait + (hop if raw or eng[d] != e else 0.0)
+                if u > t:
+                    t = u
+            j = 0
+            if e != "X":
+                s0, s1 = b0[e], b1[e]
+                j = len(s0)
+                while j > 0 and s1[j - 1] > t:
+                    j -= 1
+                while j < len(s0) and s0[j] < t + cost:
+                    if s1[j] > t:
+                        t = s1[j]
+                    j += 1
+            if best is None or t + cost < best[0]:
+                best = (t + cost, t, e, j)
+        end[k], start[k], eng[k], j = best
+        if eng[k] != "X":
+            b0[eng[k]].insert(j, start[k])
+            b1[eng[k]].insert(j, end[k])
+    return start, end, eng
+
+
+def _schedule(ops):
+    n = len(ops)
+    key = tuple(tuple(sorted(o["deps"].items())) for o in ops)
+    if key not in _ORDERS:
+        above, pred, succ = [0] * n, [], [[] for _ in range(n)]
+        lat = [o["lat"] for o in ops]
+        for k, o in enumerate(ops):
+            far = 0
+            for d in o["deps"]:
+                far |= above[d]
+            pred.append([(d, raw, lat[d]) for d, raw in o["deps"].items() if not far >> d & 1])
+            above[k] = far | sum(1 << d for d, _, _ in pred[k])
+            for d, raw, _ in pred[k]:
+                succ[d].append((k, raw, lat[d]))
+        alts = [[(e, c) for e, (_, c) in o["alts"].items()] for o in ops]
+        zero, prio = [0.0] * n, [o["prio"] for o in ops]
+        best, top, seed = None, None, [CFG["seed"]]
+
+        def rand():
+            seed[0] = (seed[0] * 1103515245 + 12345) % 2147483648
+            return seed[0] / 2147483648.0
+        pri = [o["at"] for o in ops]
+        for it in range(CFG["its"]):
+            for k in range(n):
+                for d, _, _ in pred[k]:
+                    if pri[d] >= pri[k]:
+                        pri[k] = pri[d] + 1e-6
+            start, end, eng = _place(sorted(range(n), key=lambda k: pri[k]), alts, pred, zero)
+            span = max(end[k] + lat[k] for k in range(n))
+            if best is None or span <= best[0] + CFG["temp"] * rand() * (1.0 - it / CFG["its"]):
+                best = (span, start, end, eng)
+                if top is None or span < top[0]:
+                    top = best
+            if it % 50 == 49:
+                fixed = [[x for x in alts[k] if x[0] == best[3][k]] for k in range(n)]
+                _, late, _ = _place(sorted(range(n), key=lambda k: (-best[2][k], -k)), fixed, succ, prio)
+                pri = [-x for x in late]
+            else:
+                pri, moved = list(best[1]), []
+                for _ in range(1 + int(CFG["moves"] * rand())):
+                    k = int(rand() * n)
+                    pri[k] += CFG["noise"] * (rand() - 0.5) * rand()
+                    moved.append(k)
+                if rand() < 0.5:
+                    for k in range(max(moved), -1, -1):
+                        for d, _, _ in pred[k]:
+                            if pri[d] >= pri[k]:
+                                pri[d] = pri[k] - 1e-3
+        _, start, end, eng = top
+        _ORDERS[key] = (eng, {e: sorted((k for k in range(n) if eng[k] == e), key=lambda k: (start[k], k)) for e in "VAPGSX"}, top[0])
+    return _ORDERS[key]
+
+
+def _emit(ops, queues, T):
+    n = len(ops)
+    eng, order, _ = _schedule(ops)
+    pos = {}
+    for e in order:
+        for j, k in enumerate(order[e]):
+            pos[k] = j
+    waits = [[] for _ in range(n)]
+    marked = set()
+    for e in "VAPGS":
+        seen = {}
+        for k in order[e]:
+            need = {}
+            for d, raw in ops[k]["deps"].items():
+                if ops[d]["sem"] is not None:
+                    if d not in seen:
+                        seen[d] = 1
+                        waits[k].append(("sem", d))
+                elif eng[d] != e or raw or ops[k]["sem"] is not None:
+                    need[eng[d]] = max(need.get(eng[d], -1), pos[d])
+            for f, j in need.items():
+                if seen.get(f, -1) < j:
+                    seen[f] = j
+                    waits[k].append(("eng", order[f][j]))
+                    marked.add(order[f][j])
+    count = {}
+    for e in "VAPG":
+        c = 0
+        for k in order[e]:
+            if k in marked:
+                c += 1
+                count[k] = c
+    for e in "VAPGS":
+        q = queues[e]
+        for k in order[e]:
+            for kind, d in waits[k]:
+                if kind == "sem":
+                    q.wait_ge(T.sem[ops[d]["sem"][0]], ops[d]["sem"][1])
+                else:
+                    q.wait_ge(T.sem["e" + eng[d]], count[d])
+            ins = ops[k]["alts"][e][0](q)
+            if k in marked:
+                ins.then_inc(T.sem["e" + e], 1)
+            elif ops[k]["dma"]:
+                ins.then_inc(T.sem[ops[k]["sem"][0]], 16)
+    waited = set(d for w in waits for kind, d in w if kind == "sem")
+    return [ops[k]["sem"] for k in range(n) if ops[k]["dma"] and k not in waited]
+
+
+def rank_program(g, core, T, topo):
+    plan = _relays(T, topo)
+    me = T.rank_of(core)
+    if me is None:
+        _relay_program(g, core, T, topo, plan)
+        return
+    A, F = AluOpType, ActivationFunctionType
+    GATH, CHUNKS = CFG["g"], CFG["chunks"]
+    ops, log, ndma, sent, at = [], {}, [0], [0], [-100.0]
+    far = [d for d in range(N) if (me, d) in plan]
+    near = [d for d in range(N) if d != me and d not in far]
+    dests = far + near + [me]
+
+    def op(alts, reads, writes, lat=0.0, prio=0.0, sem=None, dma=False):
+        k, deps = len(ops), {}
+        for acc, isw in ((reads, False), (writes, True)):
+            for r in acc:
+                name, lo, hi = r if isinstance(r, tuple) else (r, 0, 1 << 30)
+                bank = name.startswith("ps")
+                w = isw or bank
+                old = log.setdefault(name, [])
+                for (d, a, b, dw) in old:
+                    if d != k and a < hi and lo < b and (w or dw):
+                        deps[d] = deps.get(d, False) or (dw and not isw and not bank)
+                if w:
+                    old[:] = [x for x in old if not (lo <= x[1] and x[2] <= hi)]
+                old.append((k, lo, hi, w))
+        ops.append({"alts": alts, "deps": deps, "lat": lat, "prio": prio, "sem": sem, "dma": dma, "at": at[0] + 1e-4 * k})
+
+    def vc(n, f=1.0):
+        return 60.0 + max(64.0, n * f) * CYC
+
+    def tt(out, a, b, o, n, reads, writes, f=2.0):
+        op({"V": (lambda q: q.tensor_tensor(out, a, b, o), vc(n, f))}, reads, writes)
+
+    def ts(out, a, s1, s2, o0, o1, n, reads, writes, f=1.0):
+        if o1 is None:
+            op({"V": (lambda q: q.tensor_scalar(out, a, s1, None, o0), vc(n, f))}, reads, writes)
+        else:
+            op({"V": (lambda q: q.tensor_scalar(out, a, s1, s2, o0, o1), vc(n, f))}, reads, writes)
+
+    def cp(out, a, n, reads, writes):
+        op({"V": (lambda q: q.tensor_copy(out, a), vc(n))}, reads, writes)
+
+    def lin(out, a, scale, col, n, reads, writes, f=1.0, on="A"):
+        bias = T.cc[:, col:col + 1]
+        alts = {"V": (lambda q: q.tensor_scalar(out, a, scale, bias, A.mult, A.add), vc(n, f)),
+                "A": (lambda q: q.activation(out, a, F.Identity, bias=bias, scale=scale), vc(n, f))}
+        op({e: alts[e] for e in on}, reads + ["cc"], writes)
+
+    def act(out, a, func, n, reads, writes, scale=None, col=None):
+        if col is None:
+            op({"A": (lambda q: q.activation(out, a, func), vc(n))}, reads, writes)
+        else:
+            op({"A": (lambda q: q.activation(out, a, func, bias=T.cc[:, col:col + 1], scale=scale), vc(n))}, reads + ["cc"], writes)
+
+    def fill(ap, val, n, writes):
+        op({"V": (lambda q: q.memset(ap, val), vc(n))}, [], writes)
+
+    def mm(group, reads, bank):
+        def run(q):
+            ins = None
+            for (o, l, r, st, sp, _) in group:
+                ins = q.matmul(o, l, r, st, sp)
+            return ins
+        op({"P": (run, 60.0 + sum(max(64, x[5]) for x in group) * CFG["pe"])}, reads, ["ps%d" % bank])
+
+    def dma(e, out, src, reads, writes, prio=0.0, lat=T_DMA):
+        name = "d%d" % ndma[0]
+        ndma[0] += 1
+        op({e: (lambda q: q.dma_start(out, src), 900.0 if e == "G" else 150.0)}, reads, writes, lat=lat, prio=prio,
+           sem=(name, 16), dma=True)
+
+    def iota(out, pattern, base, mult, n, writes, flag=True, prio=0.0):
+        if flag:
+            fn = lambda q: q.iota(out, pattern, base, mult, allow_small_or_imprecise_dtypes=True)
+        else:
+            fn = lambda q: q.iota(out, pattern, base, mult)
+        op({"G": (fn, 130.0 + 2 * n * CYC)}, [], writes, prio=prio)
+
+    def arrives(name, val, t, reads, writes):
+        op({"X": (None, t)}, reads, writes, sem=(name, val))
+
+    def ps(k):
+        return T["ps%d" % k]
+
+    top = 2e5
+    dma("S", T.sx[:], T.fx[:], [], ["sx"], prio=top + 200)
+    dma("A", T.sc[:], T.cl[:], [], ["sc"], prio=top + 200)
+    dma("S", T.sh[:], T.hv[:], [], ["sh"], prio=top + 100)
+    dma("A", T.sl[:], T.hl[:], [], ["sl"], prio=top)
+    dma("S", T.st[:], T.th[:], [], ["st"], prio=top)
+    iota(T.pc[:, 0:1], [[0, 1]], 0, 1, 1, ["call", "pc"], flag=False, prio=top)
+    iota(T.cx[:], [[1, 176]], 0, 0, 176, ["call", "cx"], prio=top)
+    iota(T.cx2[:], [[64, 2], [0, 4], [1, 16]], 0, 0, 128, ["call", "cx2"], prio=top)
+    lanes = _lanes(T, topo, plan, me)
+    for pieces in ("xc", "h", "l", "t"):
+        tr = []
+        for piece in pieces:
+            for d in far + near:
+                if d in near:
+                    c, land, rsem = T.cores[d], _slot(T, piece, me), T.sem["a%s%d" % ("l" if piece == "t" else piece, me)]
+                else:
+                    c = plan[(me, d)][piece in "clt"]
+                    land = T["r" + piece][:] if piece in "xhc" else _slot(T, piece, me)
+                    rsem = T.sem.rin1 if piece in "xc" else T.sem.rin2
+                rid, pid = topo.addr(c, core)
+                tr.append(RemoteDMATransfer(dst_ids=[DstId(rid=rid, pnc=pid)], dma_engine_mask=_mask(lanes[piece, d]),
+                                            remote_sem=rsem, src=T["s" + piece][d], dst=land))
+                sent[0] += len(lanes[piece, d])
+        op({"G": (lambda q, tr=tr: q.remote_dma_fused(tr, local_sem=T.sem.sent), 1000.0)}, ["s" + x for x in pieces], ["call"],
+           prio=top)
+    rows = slice(32 * me, 32 * me + 32)
+    for piece, src in (("x", T.fx[rows, :]), ("c", T.cl[rows, :]), ("h", T.hv[rows, :]), ("l", T.hl[rows, :]),
+                       ("t", T.th[2 * me:2 * me + 2, :])):
+        dma("S", _slot(T, piece, me), src, ["st"], [("L" + piece, me, me + 1)])
+    for s in near + far:
+        theirs = _lanes(T, topo, plan, s)
+        for piece, late in (("x", 0.0), ("c", 0.0), ("h", 1000.0), ("l", 2500.0)):
+            if s in near:
+                n_in = len(theirs[piece, me]) + (len(theirs["t", me]) if piece == "l" else 0)
+            else:
+                n_in = len(topo.engines(plan[(s, me)][piece in "cl"], core))
+            arrives("a%s%d" % (piece, s), n_in, CFG["direct" if s in near else "relayed"] + late, [],
+                    [("L" + x, s, s + 1) for x in ("lt" if piece == "l" else piece)])
+    sources = [me] + near + far
+    iota(T.cx3[:], [[64, 2], [0, 8], [1, 8]], 0, 0, 128, ["call", "cx3"])
+    iota(T.si0[:], [[960, 4], [0, 2], [16, 60]], PAD + int(OFF), 1, 480, ["call", "si0"])
+    iota(T.ki[:], [[0, 4], [768, 2], [0, 60]], BLK + int(OFF), 0, 480, ["call", "ki"])
+    for r in dests:
+        iota(T.iot[:, r * V:(r + 1) * V], [[1, V]], r * V + 16384, 0, V, ["call", ("iot", r, r + 1)])
+
+    CZ, CM, CN, CFL, CB, CR, CS, CL, CH, CK, CF = range(11)
+    for col, val in ((CZ, 0.0), (CM, BIG + 1), (CN, -BIG), (CFL, BIG - 0.5), (CB, 16384.0), (CR, float(BLK)), (CS, -OFF),
+                     (CL, -10.5 * K), (CH, 0.5), (CK, -K), (CF, -OFF - 8192.0)):
+        fill(T.cc[:, col:col + 1], val, 1, [("cc", col, col + 1)])
+    p = T.pc[:, 0:1]
+    PF64, PI, PG16, PI4, PA, PI8, PU, PJ, PP = range(9)
+    for col, sh, m in ((PF64, 0, 64), (PI, 0, 15), (PG16, 0, 112), (PI4, 2, 15), (PA, 0, 3), (PI8, 0, 7), (PU, 0, 1), (PJ, 1, 7)):
+        ts(T.pi[:, col:col + 1], p, sh, m, A.arith_shift_right, A.bitwise_and, 1, ["pc"], [("pi", col, col + 1)])
+    cp(T.pf[:, 0:8], T.pi[:], 8, ["pi"], [("pf", 0, 8)])
+    cp(T.pf[:, PP:PP + 1], p, 1, ["pc"], [("pf", PP, PP + 1)])
+
+    def pf(c):
+        return T.pf[:, c:c + 1]
+
+    def tg(c):
+        return T.tg[:, c:c + 1]
+    GCB, GON, GE, GO8, GF, GP, GG, GT = range(8)
+    ts(tg(GF), pf(PI4), pf(PF64), None, A.add, None, 1, ["pf"], [("tg", GF, GF + 1)])
+    ts(tg(GCB), pf(PG16), 15.0, None, A.add, None, 1, ["pf"], [("tg", GCB, GCB + 1)])
+    ts(tg(GON), pf(PI), pf(PF64), None, A.add, None, 1, ["pf"], [("tg", GON, GON + 1)])
+    ts(tg(GE), pf(PI), 4.0, pf(PF64), A.mult, A.add, 1, ["pf"], [("tg", GE, GE + 1)])
+    ts(tg(GO8), pf(PI8), pf(PF64), None, A.add, None, 1, ["pf"], [("tg", GO8, GO8 + 1)])
+    ts(tg(GP), pf(PA), 16.0, tg(GF), A.mult, A.add, 1, ["pf", ("tg", GF, GF + 1)], [("tg", GP, GP + 1)])
+    ts(tg(GG), pf(PU), 8.0, pf(PG16), A.add, A.add, 1, ["pf"], [("tg", GG, GG + 1)])
+    ts(tg(GT), tg(GE), 3.0, None, A.add, None, 1, [("tg", GE, GE + 1)], [("tg", GT, GT + 1)])
+    ts(T.tf0[:], T.cx[:, 0:4], pf(PA), 1000.0, A.not_equal, A.mult, 4, ["cx", "pf"], ["tf0"])
+    ts(T.tf[:], T.tf0[:], tg(GF), None, A.add, None, 4, ["tf0", ("tg", GF, GF + 1)], ["tf"])
+    ts(T.tf48[:], T.tf0[:], tg(GF), 48.0, A.add, A.add, 4, ["tf0", ("tg", GF, GF + 1)], ["tf48"])
+    ts(T.tj0[:], T.cx[:, 0:8], pf(PJ), 1000.0, A.not_equal, A.mult, 8, ["cx", "pf"], ["tj0"])
+    ts(T.tj[:], T.tj0[:], tg(GG), None, A.add, None, 8, ["tj0", ("tg", GG, GG + 1)], ["tj"])
+
+    def pick(out, cols, target, weight, n, reads, writes):
+        ts(out, cols, target, weight, A.is_equal, A.mult, n, reads, writes)
+    for a in range(4):
+        pick(T.mr[:, a * 128:(a + 1) * 128], T.cx2[:], T.tf[:, a:a + 1], 1.0, 128, ["cx2", "tf"], [("mr", a, a + 1)])
+        pick(T.mf[:, a * 176:(a + 1) * 176], T.cx[:], T.tf48[:, a:a + 1], 1.0, 176, ["cx", "tf48"], [("mf", a, a + 1)])
+    pick(T.mcb[:], T.cx[:, 0:144], tg(GCB), 1.0, 144, ["cx", "tg"], ["mcb"])
+    pick(T.mi1[:], T.cx[:, 0:128], pf(PP), 1.0, 128, ["cx", "pf"], ["mi1"])
+    pick(T.mon[:], T.cx2[:], tg(GON), 1.0, 128, ["cx2", "tg"], ["mon"])
+    pick(T.mo8[:], T.cx3[:], tg(GO8), 1.0, 128, ["cx3", "tg"], ["mo8"])
+    pick(T.me[:], T.cx[:, 0:132], tg(GT), 0.125, 132, ["cx", "tg"], ["me"])
+    pick(T.mp[:], T.cx[:, 0:128], tg(GP), 1.0, 128, ["cx", "tg"], ["mp"])
+    for jj in range(8):
+        pick(T.mg[:, jj * 136:(jj + 1) * 136], T.cx[:, 0:136], T.tj[:, jj:jj + 1], K, 136, ["cx", "tj"], [("mg", jj, jj + 1)])
+    lin(T.mck[:], T.mcb[:], 4096.0, CZ, 144, ["mcb"], ["mck"])
+    lin(T.mch[:], T.mcb[:], 16384.0, CZ, 144, ["mcb"], ["mch"])
+    for name, src, w in (("mni", "mi1", -1.0), ("mn2", "mi1", -2.0), ("mnb", "mi1", -BIG), ("mi4", "mi1", 4096.0),
+                         ("mi8", "mi1", 8.0), ("msum", "mon", 0.125), ("monk", "mon", K / 2)):
+        lin(T[name][:], T[src][:], w, CZ, 128, [src], [name])
+    tt(T.monp[:], T.mon[:], T.mi8[:], A.add, 128, ["mon", "mi8"], ["monp"])
+    tt(T.mo8p[:], T.mo8[:], T.mi8[:], A.add, 128, ["mo8", "mi8"], ["mo8p"])
+    fill(T.mz[:], 0.0, 240, ["mz"])
+    fill(T.fl[:], 1.0, 240, ["fl"])
+    for b in range(RO):
+        fill(T.win[:, b * BLK:b * BLK + PAD], BIG + 1153.0, 16, [("win", b * BLK, b * BLK + PAD)])
+    for hh in range(4):
+        fill(T.thw[:, hh * V:(hh + 1) * V], 0.0, V // 2, [("thz", hh, hh + 1)])
+
+    def cb(j, name="mcb"):
+        return T[name][:, 15 - j:143 - j]
+
+    def parts(s, c0, c1, names, tag):
+        a, b, rd = s * IB + c0, s * IB + c1, [("L" + x, s, s + 1) for x in names]
+        cp(T.lh[:, a:b], T.li[:, a:b], c1 - c0, rd, [("lh" + tag, s, s + 1)])
+        tt(T.ll[:, a:b], T.li[:, a:b], T.lh[:, a:b], A.subtract, c1 - c0, rd + [("lh" + tag, s, s + 1)], [("ll" + tag, s, s + 1)])
+
+    x0 = (RO - 1) * BLK + PAD
+    mm([(ps(6)[:, 0:480], T.mz[:, 0:128], T.mz[:, 0:480], True, False, 480)], ["mz"], 6)
+    for k, s in enumerate(sources):
+        lastsrc = k == N - 1
+        parts(s, 0, 120, "c", "c")
+        for hh in range(2):
+            mm([(ps(hh)[:, 240 * b:240 * b + 240], T.mr[:, (2 * hh + b) * 128:(2 * hh + b + 1) * 128],
+                 _slot(T, "x", s), True, True, 240) for b in range(2)], ["mr", ("Lx", s, s + 1)], hh)
+            c0 = x0 + s * V + 480 * hh
+            lin(T.win[:, c0:c0 + 480], ps(hh)[:, 0:480], 1.0, CM, 480, ["ps%d" % hh], [("win", c0, c0 + 480)], on="VA")
+        grp = []
+        for a in range(4):
+            w = T.mf[:, a * 176 + 48 - 16 * s:a * 176 + 176 - 16 * s]
+            grp.append((ps(6)[:, 120 * a:120 * a + 120], w, T.lh[:, s * IB:s * IB + 120], False, False, 120))
+            grp.append((ps(6)[:, 120 * a:120 * a + 120], w, T.ll[:, s * IB:s * IB + 120], False, lastsrc and a == 3, 120))
+        mm(grp, ["mf", ("lhc", s, s + 1), ("llc", s, s + 1)], 6)
+        for a in range(4):
+            w = T.mf[:, a * 176 + 48 - 16 * s:a * 176 + 176 - 16 * s]
+            mm([(ps(2 + a)[:, 0:384], w, _slot(T, "h", s), k == 0, lastsrc, 384)], ["mf", ("Lh", s, s + 1)], 2 + a)
+    cp(T.cu[:], ps(6)[:, 0:480], 480, ["ps6"], ["cu"])
+    for a in range(4):
+        c0 = H0 + 384 * a
+        lin(T.win[:, c0:c0 + 384], ps(2 + a)[:, 0:384], 1.0, CM, 384, ["ps%d" % (2 + a)], [("win", c0, c0 + 384)], on="VA")
+    lin(T.clf[:], ps(6)[:, 0:480], 1.0, CB, 480, ["ps6"], ["clf"])
+    lin(T.chi[:], T.clf[:], 1.0, CZ, 480, ["clf"], ["chi"])
+    tt(T.clo[:], T.clf[:], T.chi[:], A.subtract, 480, ["clf", "chi"], ["clo"])
+    at[0] = -1.0
+    for s in sources:
+        parts(s, 120, 255, "lt", "l")
+        for b, name in enumerate(("lh", "ll")):
+            dma("S", T.lth[b, s], T[name][:, s * IB + 240:s * IB + 255], [(name + "l", s, s + 1)], [("lth", 4 * b + s, 4 * b + s + 1)],
+                lat=3000.0)
+        mm([(ps(7)[:, 120 * s:120 * s + 120], T.mp[:], T.lh[:, s * IB + 120:s * IB + 240], True, False, 120),
+            (ps(7)[:, 120 * s:120 * s + 120], T.mp[:], T.ll[:, s * IB + 120:s * IB + 240], False, True, 120)],
+           ["mp", ("lhl", s, s + 1), ("lll", s, s + 1)], 7)
+    k = 0
+    for b in range(2):
+        for gq in range(8):
+            f = gq // 4
+            dma("S" if k % 3 else "G", T.thw[16 * gq + b:16 * gq + b + 1, :], T.lth[b, :, 64 * f:64 * f + 64, :],
+                [("lth", 4 * b, 4 * b + 4), "thz"], [("thw", k, k + 1)])
+            k += 1
+    at[0] = 2.0
+    cp(T.hli[:], ps(7)[:, 0:480], 480, ["ps7"], ["hli"])
+    tt(T.hp0[:], ps(7)[:, 0:480], T.ki[:], A.add, 480, ["ps7", "ki"], ["hp0"], f=1.0)
+    at[0] = 6.0
+    ts(T.hls[:], T.hli[:], 1, None, A.arith_shift_right, None, 480, ["hli"], ["hls"])
+    cp(T.hw[:], T.hls[:], 480, ["hls"], ["hw"])
+    ts(T.sfp[:], T.si0[:], pf(PG16), None, A.subtract, None, 480, ["si0", "pf"], ["sfp"])
+    lin(T.shi[:], T.sfp[:], 1.0, CZ, 480, ["sfp"], ["shi"])
+    tt(T.slo[:], T.sfp[:], T.shi[:], A.subtract, 480, ["sfp", "shi"], ["slo"])
+    lin(T.hp1[:], T.hp0[:], 1.0, CR, 480, ["hp0"], ["hp1"])
+    lin(T.hp2[:], T.hp1[:], 1.0, CR, 480, ["hp1"], ["hp2"])
+
+    def spread(srcs, m, reads, own=True):
+        grp = []
+        for jj in range(8):
+            for c in range(C):
+                for b, src in enumerate(srcs):
+                    grp.append((ps(5)[:, jj:384:8], T.mg[:, jj * 136 + 8 - 2 * c:jj * 136 + 136 - 2 * c],
+                                src[:, c, 48 * m:48 * m + 48], own and c == 0 and b == 0,
+                                (own or jj == 7) and c == C - 1 and b == len(srcs) - 1, 48))
+        for j in range(0, len(grp), 20):
+            mm(grp[j:j + 20], ["mg"] + reads, 5)
+
+    at[0] = 3.0
+    for m in range(2):
+        a, b = 384 * m, 384 * m + 384
+        spread([T.chi, T.clo], m, ["chi", "clo"])
+        lin(T.idw[:, a:b], ps(5)[:, 0:384], 1.0 / K, CZ, 384, ["ps5"], [("idw", m, m + 1)])
+        lin(T.ihi[:, a:b], T.idw[:, a:b], 1.0, CZ, 384, [("idw", m, m + 1)], [("ihi", m, m + 1)])
+        tt(T.ilo[:, a:b], T.idw[:, a:b], T.ihi[:, a:b], A.subtract, 384, [("idw", m, m + 1), ("ihi", m, m + 1)], [("ilo", m, m + 1)])
+    for m in range(2):
+        u0, u1 = 48 * m, 48 * m + 48
+        at[0] = CFG["tth"][m]
+        for c in range(C):
+            a = 3840 * m + 768 * c
+            lin(T.g5[:, a:a + 768], T.thw[:].indirect(T.cu[:, 96 * c + u0:96 * c + u1]), 1.0, CZ, 768,
+                ["thw", "thz", "cu"], [("g5", a, a + 768)], f=GATH, on="VA" if c >= CFG["thv"] else "A")
+        mm([(ps(6)[:, 0:240], cb(j), T.g5[:, 3840 * m + j:3840 * m + 3840:16], j == 0, j == 15, 240) for j in range(16)],
+           ["mcb", "g5" if m else ("g5", 0, 3840)], 6)
+        lin(T.thc[:, :, u0:u1], ps(6)[:, 0:240], 1.0, CZ, 240, ["ps6"], [("thc", u0, u1)])
+        lin(T.thi[:, :, u0:u1], T.thc[:, :, u0:u1], 1.0, CZ, 240, [("thc", u0, u1)], [("thi", u0, u1)])
+        tt(T.tlo[:, :, u0:u1], T.thc[:, :, u0:u1], T.thi[:, :, u0:u1], A.subtract, 240,
+           [("thc", u0, u1), ("thi", u0, u1)], [("tlo", u0, u1)])
+
+    diff = [0]
+    for rnd in range(RO):
+        blk = (RO - 1 - rnd) * BLK
+        xs = blk + PAD
+        xw, xr = T.win[:, xs:xs + NT], ("win", xs, xs + NT)
+        whole, wholer = T.win[:, blk:H0 + HQ], ("win", blk, H0 + HQ)
+        last, t0 = rnd == RO - 1, 100.0 * rnd
+        al, hp = "al%d" % rnd, "hp%d" % rnd
+
+        def claims(m, k, r):
+            o, u0, u1 = 1920 * k, 120 * r, 120 * r + 120
+            a, v0, v1 = o + V * m, u0 + 60 * m, u0 + 60 * m + 60
+            ur, vr = (lambda name: (name, u0, u1)), (lambda name: (name, v0, v1))
+            fbank, nbank = 4 + k % 2 if m else 6, 7 - k % 2
+            at[0] = t0 + (30.0 + 1.8 * k if m else CFG["eq0"] + 1.3 * k)
+            tt(T.eq[:, a:a + V], T["ww%d" % m][:].indirect(T.hw[:, v0:v1]), T.iot[:, r * V:(r + 1) * V],
+               A.is_equal, V, ["ww%d" % m, "hw", ("iot", r, r + 1)], [("eq", a, a + V)], f=GATH)
+            at[0] += 1.0
+            if last and m == 0:
+                return
+            if last:
+                mm([(ps(7)[:, 0:120], cb(j), T.eq[:, o + j:o + 1920:16], j == 0, j == 15, 120) for j in range(16)],
+                   ["mcb", ("eq", o, o + 1920)], 7)
+                lin(T.fb[:, u0:u1], ps(7)[:, 0:120], 1.0, CZ, 120, ["ps7"], [ur("fb")])
+                mm([(ps(5)[:, 60 * m1:60 * m1 + 60], T.monp[:] if m1 == m2 else T.mon[:], T.fb[:, u0 + 60 * m2:u0 + 60 * m2 + 60],
+                     m2 == 0, m2 == 1, 60) for m1 in range(2) for m2 in range(2)], ["mon", "monp", ur("fb")], 5)
+                act(T[al][:, u0:u1], ps(5)[:, 0:120], F.Relu, 120, ["ps5"], [ur(al)], scale=K, col=CL)
+                tt(T.t1[:, u0:u1], T[al][:, u0:u1], T.home[:, u0:u1], A.add, 120, [ur(al), "home"], [ur("t1")])
+                tt(T.t2[:, u0:u1], T.t1[:, u0:u1], T[hp][:, u0:u1], A.min, 120, [ur("t1"), hp], [ur("t2")])
+                ts(T.ix[:, u0:u1], T.t2[:, u0:u1], OFF, None, A.subtract, None, 120, [ur("t2")], [ur("ix")])
+            else:
+                out = ps(fbank)[:, 0:60]
+                mm([(out, T.mi1[:], T.shi[:, v0:v1], True, False, 60), (out, T.mi1[:], T.slo[:, v0:v1], False, False, 60)]
+                   + [(out, cb(j, "mch"), T.eq[:, a + j:a + V:16], False, j == 15, 60) for j in range(16)],
+                   ["mi1", "mch", "shi", "slo", ("eq", a, a + V)], fbank)
+                tt(T.t1[:, v0:v1], out, T[hp][:, v0:v1], A.min, 60, ["ps%d" % fbank, hp], [vr("t1")], f=1.0)
+                act(T.fb[:, v0:v1], out, F.Sign, 60, ["ps%d" % fbank], [vr("fb")], scale=1.0, col=CF)
+                if m == 0:
+                    ts(T.ix[:, v0:v1], T.t1[:, v0:v1], OFF, None, A.subtract, None, 60, [vr("t1")], [vr("ix")])
+                else:
+                    out = ps(nbank)[:, 0:60]
+                    mm([(out, T.monk[:], T.fb[:, u0 + 60 * m2:u0 + 60 * m2 + 60], m2 == 0, m2 == 1, 60) for m2 in range(2)],
+                       ["monk", ur("fb")], nbank)
+                    tt(T.t2[:, v0:v1], out, T.t1[:, v0:v1], A.min, 60, ["ps%d" % nbank, vr("t1")], [vr("t2")], f=1.0)
+                    act(T[al][:, 60 * r:60 * r + 60], out, F.Sign, 60, ["ps%d" % nbank], [(al, r, r + 1)], scale=1.0, col=CS)
+                    ts(T.ix[:, v0:v1], T.t2[:, v0:v1], OFF, None, A.subtract, None, 60, [vr("t2")], [vr("ix")])
+            n5 = V if k < CFG["big"] else 480
+            for m2 in (range(2) if last else [m]):
+                for b in range(0, V, n5):
+                    a, c0 = o + V * m2 + b, u0 + 60 * m2 + b // 16
+                    lin(T.g5[:, a:a + n5], whole.indirect(T.ix[:, c0:c0 + n5 // 16]), 1.0, CN, n5, [wholer, ("ix", c0, c0 + n5 // 16)],
+                        [("g5", a, a + n5)], f=GATH, on="VA" if (m2, k) in CFG["p5l" if last else "p5v"] else "A")
+
+        if last:
+            at[0] = t0 + 10.0
+            tt(T.als[:], T.al0[:], T.al1[:], A.add, 240, ["al0", "al1"], ["als"])
+            lin(T.alt[:], T.als[:], -BLK / 2.0, CR, 240, ["als"], ["alt"])
+            for r in dests:
+                for m in range(2):
+                    c0 = 120 * r + 60 * m
+                    tt(T.home[:, c0:c0 + 60], T.alt[:, 60 * r:60 * r + 60], T.sfp[:, c0:c0 + 60], A.add, 60, ["alt", "sfp"],
+                       [("home", c0, c0 + 60)])
+        for k, (w0, w1) in enumerate(CHUNKS):
+            wc, hc, h0, o, m = w1 - w0, 16 * (w1 - w0), 16 * w0, 80 * w0, w0 // 48
+            hits = T.win[:, H0 + h0:H0 + h0 + hc]
+            hr = ("win", H0 + h0, H0 + h0 + hc)
+            wr = lambda name: (name, w0, w1)
+            for c in range(C):
+                a, b = o + c * hc, o + (c + 1) * hc
+                at[0] = t0 + 14.0 * a / 7680
+                tt(T.dd[:, a:b], xw.indirect(T.cu[:, 96 * c + w0:96 * c + w1]), hits, A.subtract, hc, [xr, hr, "cu"],
+                   [("dd", a, b)], f=GATH)
+                act(T.ab[:, a:b], T.dd[:, a:b], F.Abs, hc, [("dd", a, b)], [("ab", a, b)])
+            te = t0 + 14.0 * (o + 5 * hc) / 7680
+            at[0] = te - 0.5
+            kd = 3 + 4 * (k % 2)
+            out = ps(kd)[:, 0:5 * wc]
+            mm([(out, T.mnb[:], T.fl[:, :, w0:w1], True, False, 5 * wc), (out, T.mi1[:], T.chi[:, :, w0:w1], False, False, 5 * wc),
+                (out, T.mi1[:], T.clo[:, :, w0:w1], False, False, 5 * wc)], ["mnb", "mi1", "chi", "clo", wr("fl")], kd)
+            mm([(out, cb(j, "mck"), T.ab[:, o + j:o + 5 * hc:16], False, j == 15, 5 * wc) for j in range(16)],
+               ["mck", ("ab", o, o + 5 * hc)], kd)
+            lin(T.key[:, :, w0:w1], out, 1.0, CN, 5 * wc, ["ps%d" % kd], [wr("key")])
+            at[0] = te + 0.8
+            tt(T.m1[:, :, w0:w1], T.key[:, 0:2, w0:w1], T.key[:, 2:4, w0:w1], A.min, 2 * wc, [wr("key")], [wr("m1")])
+            at[0] += CFG["gap"]
+            tt(T.m2[:, w0:w1], T.m1[:, 0, w0:w1], T.m1[:, 1, w0:w1], A.min, wc, [wr("m1")], [wr("m2")])
+            at[0] += CFG["gap"]
+            tt(T.mi[:, w0:w1], T.m2[:, w0:w1], T.key[:, 4, w0:w1], A.min, wc, [wr("m2"), wr("key")], [wr("mi")])
+            at[0] += CFG["gap"]
+            ts(T.ma[:, w0:w1], T.mi[:, w0:w1], 4095, None, A.bitwise_and, None, wc, [wr("mi")], [wr("ma")])
+            at[0] += CFG["gap"]
+            ts(T.bi[:, w0:w1], T.ma[:, w0:w1], float(NT - 1), None, A.min, None, wc, [wr("ma")], [wr("bi")])
+            at[0] += CFG["gap"]
+            tt(T.db[:, h0:h0 + hc], xw.indirect(T.bi[:, w0:w1]), hits, A.subtract, hc, [xr, hr, wr("bi")],
+               [("db", h0, h0 + hc)], f=GATH)
+            for a in range(0, 5 * hc, 512):
+                b = min(a + 512, 5 * hc)
+                bank = diff[0] % 3
+                diff[0] += 1
+                grp, u = [], a
+                while u < b:
+                    v = min(b, (u // hc + 1) * hc)
+                    grp.append((ps(bank)[:, u - a:v - a], T.mi1[:], T.dd[:, o + u:o + v], True, False, v - u))
+                    grp.append((ps(bank)[:, u - a:v - a], T.mni[:], T.db[:, h0 + u % hc:h0 + u % hc + v - u], False, True, v - u))
+                    u = v
+                mm(grp, ["mi1", "mni", ("dd", o + a, o + b), ("db", h0, h0 + hc)], bank)
+                act(T.ab[:, o + a:o + b], ps(bank)[:, 0:b - a], F.Abs, b - a, ["ps%d" % bank], [("ab", o + a, o + b)])
+            if w1 % 48 == 0:
+                at[0] += 0.5
+                u0, u1 = 48 * m, 48 * m + 48
+                for c in range(C):
+                    tt(T.nb[:, c, u0:u1], T.key[:, c, u0:u1], T.mi[:, u0:u1], A.is_le, 48, [("key", u0, u1), ("mi", u0, u1)],
+                       [("nb", 5 * m + c, 5 * m + c + 1)])
+                act(T.nl[:, :, u0:u1], T.key[:, :, u0:u1], F.Relu, 240, [("key", u0, u1)], [("nl", u0, u1)])
+                for (v0, v1) in CHUNKS:
+                    if v0 // 48 == m:
+                        vw, vo = v1 - v0, 80 * v0
+                        out = ps(4)[:, 5 * (v0 - u0):5 * (v1 - u0)]
+                        mm([(out, w, src[:, :, v0:v1], j == 0, False, 5 * vw) for j, (w, src) in
+                            enumerate(((T.mni[:], T.thi), (T.mni[:], T.tlo), (T.mn2[:], T.nl), (T.mi4[:], T.nb)))],
+                           ["mni", "mn2", "mi4", ("thi", v0, v1), ("tlo", v0, v1), ("nl", v0, v1), ("nb", 5 * m, 5 * m + 5)], 4)
+                        mm([(out, cb(j), T.ab[:, vo + j:vo + 80 * vw:16], False, j == 15, 5 * vw) for j in range(16)],
+                           ["mcb", ("ab", vo, vo + 80 * vw)], 4)
+                        act(T.fl[:, :, v0:v1], out, F.Sign, 5 * vw, ["ps4"], [("fl", v0, v1)], scale=1.0, col=CH)
+                mm([(ps(5)[:, 0:384], T.mi1[:], T.ihi[:, 384 * m:384 * m + 384], True, False, 384),
+                    (ps(5)[:, 0:384], T.mi1[:], T.ilo[:, 384 * m:384 * m + 384], False, False, 384)],
+                   ["mi1", ("ihi", m, m + 1), ("ilo", m, m + 1)], 5)
+                spread([T.fl], m, [("fl", u0, u1)], own=False)
+                lin(T["ww%d" % m][:], ps(5)[:, 0:384], 1.0, CK, 384, ["ps5"], ["ww%d" % m])
+                if m == 0:
+                    for k2, r in enumerate(dests):
+                        claims(0, k2, r)
+        for k, r in enumerate(dests):
+            o, u0, u1 = 1920 * k, 120 * r, 120 * r + 120
+            claims(1, k, r)
+            if not last:
+                for hh in range(2):
+                    bank, a = (2 * k + hh) % 4, o + 480 * hh
+                    mm([(ps(bank)[:, 0:480], T.msum[:], T.g5[:, a + V * m:a + V * m + 480], m == 0, m == 1, 480) for m in range(2)],
+                       ["msum"] + [("g5", a + V * m, a + V * m + 480) for m in range(2)], bank)
+                    c0 = xs - BLK + r * V + 480 * hh
+                    lin(T.win[:, c0:c0 + 480], ps(bank)[:, 0:480], 1.0 + 2.0 ** -12, CFL, 480, ["ps%d" % bank],
+                        [("win", c0, c0 + 480)], on="VA")
+                continue
+            mm([(ps(k)[:, 0:240], T.me[:, 3 - a:131 - a], T.g5[:, o + V * m + 240 * a:o + V * m + 240 * a + 240],
+                 a == 0 and m == 0, a == 3 and m == 1, 240) for a in range(4) for m in range(2)], ["me", ("g5", o, o + 1920)], k)
+            xf = T.xf[:, 240 * r:240 * r + 240]
+            lin(xf, ps(k)[:, 0:240], 1.0 + 2.0 ** -12, CFL, 240, ["ps%d" % k], [("xf", r, r + 1)], on="VA")
+            ts(T.res[:, OB * r:OB * r + 240], xf, BIG + 1, None, A.subtract, None, 240, [("xf", r, r + 1)], [("res", 2 * r, 2 * r + 1)])
+            mm([(ps(4)[:, 0:120], cb(j), T.eq[:, o + 120 * j:o + 120 * j + 120], j == 0, j == 15, 120) for j in range(16)],
+               ["mcb", ("eq", o, o + 1920)], 4)
+            lin(T.fc[:, u0:u1], ps(4)[:, 0:120], 1.0, CZ, 120, ["ps4"], [("fc", u0, u1)], on="VA")
+            mm([(ps(6)[:, 0:120], T.mo8p[:], T.fc[:, u0:u1], True, True, 120)], ["mo8p", ("fc", u0, u1)], 6)
+            ts(T.res[:, OB * r + 240:OB * r + OB], ps(6)[:, 0:120], 11.0, None, A.is_ge, None, 120, ["ps6"],
+               [("res", 2 * r + 1, 2 * r + 2)])
+            piece = T.res[:, OB * r:OB * r + OB]
+            if r == me:
+                dma("S", T.yx[32 * r:32 * r + 32, :], T.res[:, OB * r:OB * r + 240], [("res", 2 * r, 2 * r + 1)], [])
+                dma("S", T.yl[2 * r:2 * r + 2, :], T.res[:, OB * r + 240:OB * r + OB], [("res", 2 * r + 1, 2 * r + 2)], [])
+                continue
+            if r in far:
+                dst, land, rsem, tail, via = plan[(me, r)][0], T.ro[:], T.sem.rout, 6500.0, plan[(r, me)][0]
+            else:
+                dst, land, rsem, tail, via = T.cores[r], T.lo[:, me * OB:(me + 1) * OB], T.sem["ao%d" % me], 3500.0, T.cores[r]
+            on = topo.engines(core, dst)
+            rid, pid = topo.addr(dst, core)
+            sent[0] += len(on)
+            op({"G": (lambda q, land=land, piece=piece, rsem=rsem, pid=pid, rid=rid, on=on:
+                      q.remote_dma(land, piece, rsem, T.sem.sent, pid, rid, _mask(on)), 800.0)},
+               [("res", 2 * r, 2 * r + 2)], [])
+            arrives("ao%d" % r, len(topo.engines(via, core)), tail, [("res", 2 * r, 2 * r + 2)], [("lo", r, r + 1)])
+            dma("S", T.yx[32 * r:32 * r + 32, :], T.lo[:, OB * r:OB * r + 240], [("lo", r, r + 1)], [])
+            dma("S", T.yl[2 * r:2 * r + 2, :], T.lo[:, OB * r + 240:OB * r + OB], [("lo", r, r + 1)], [])
+
+    for sem in _emit(ops, {"V": g.vector, "A": g.scalar, "P": g.tensor, "G": g, "S": g.sync}, T):
+        g.wait_ge(T.sem[sem[0]], sem[1])
+    g.wait_ge(T.sem.sent, sent[0])

@@ -10,11 +10,9 @@ H0 = RO * BLK
 BIG = 2.0 ** 23
 K = 32768.0
 OFF = -1.5 * K
-CFG = {"chunks": [(0, 48), (48, 72), (72, 96)],
-       "p5v": [(1, 3)], "p5l": [(1, 2), (1, 3)], "big": 2, "thv": 2,
-       "g": 1.5, "hop": 140.0, "pe": 0.42, "direct": 9000.0, "relayed": 12500.0,
-       "its": 8000, "seed": 1, "temp": 100.0, "moves": 3, "noise": 8000.0, "gap": 0.3, "eq0": 21.0, "tth": (4.0, 12.0)}
-CYC, T_DMA = 0.83, 2200.0
+CHUNKS = [(0, 24), (24, 48), (48, 72), (72, 96)]
+CYC, PEC, GATH, HOP, LOOK, T_DMA, T_NEAR, T_FAR = 0.83, 0.42, 1.5, 140.0, 200.0, 2200.0, 9000.0, 12500.0
+CFG = {"seeds": (1, 2, 3), "gits": 200, "its": 7000}
 
 F32, BF, I32, U16 = "float32", "bfloat16", "int32", "uint16"
 SCRATCH = {
@@ -26,7 +24,7 @@ SCRATCH = {
 }
 for _names, _shape, _dt in (
         ("lb", [N * XB], BF), ("li", [N * IB], I32), ("lh ll", [N * IB], BF), ("lo res", [N * OB], BF), ("win", [H0 + HQ], F32),
-        ("dd ab eq g5", [7680], BF), ("db", [HQ], BF), ("iot", [NT], F32), ("thw", [NT], BF), ("m2", [96], F32),
+        ("dd ab eq g5", [7680], BF), ("db", [HQ], BF), ("hb", [384], BF), ("iot", [NT], F32), ("thw", [NT], BF), ("m2", [96], F32),
         ("mi ma", [96], I32), ("bi", [96], U16), ("cu hw ix", [480], U16), ("idw", [768], F32), ("ihi ilo", [768], BF),
         ("ww0 ww1", [384], F32), ("hli hls", [480], I32), ("xf", [V], F32), ("al0 al1 als alt", [240], F32),
         ("cx", [176], F32), ("cx2 cx3", [128], F32), ("pc", [2], I32), ("pi", [8], I32), ("pf tg cc", [16], F32),
@@ -108,7 +106,7 @@ _ORDERS = {}
 
 
 def _place(seq, alts, before, first):
-    hop, n = CFG["hop"], len(alts)
+    n = len(alts)
     b0, b1 = {e: [] for e in "VAPGS"}, {e: [] for e in "VAPGS"}
     start, end, eng = [0.0] * n, [0.0] * n, [None] * n
     for k in seq:
@@ -116,7 +114,7 @@ def _place(seq, alts, before, first):
         for e, cost in alts[k]:
             t = first[k]
             for d, raw, wait in before[k]:
-                u = end[d] + wait + (hop if raw or eng[d] != e else 0.0)
+                u = end[d] + wait + (HOP if raw or eng[d] != e else 0.0)
                 if u > t:
                     t = u
             j = 0
@@ -138,6 +136,28 @@ def _place(seq, alts, before, first):
     return start, end, eng
 
 
+def _greedy(alts, pred, succ, pri):
+    n = len(alts)
+    free = {e: 0.0 for e in "VAPGSX"}
+    start, end, eng, left = [0.0] * n, [0.0] * n, [None] * n, [len(p) for p in pred]
+    ready = [k for k in range(n) if not left[k]]
+    when = {k: {e: 0.0 for e, _ in alts[k]} for k in ready}
+    while ready:
+        t, e = min((max(when[k][e], free[e]), e != "A", e) for k in ready for e in when[k])[::2]
+        k = min((k for k in ready if e in when[k] and when[k][e] <= t + (LOOK if len(when[k]) == 1 else 0.0)), key=lambda k: pri[k])
+        ready.remove(k)
+        start[k], eng[k] = max(when[k][e], free[e]), e
+        end[k] = start[k] + dict(alts[k])[e]
+        if e != "X":
+            free[e] = end[k]
+        for s, _, _ in succ[k]:
+            left[s] -= 1
+            if not left[s]:
+                ready.append(s)
+                when[s] = {f: max(end[d] + w + (HOP if raw or eng[d] != f else 0.0) for d, raw, w in pred[s]) for f, _ in alts[s]}
+    return start, end
+
+
 def _schedule(ops):
     n = len(ops)
     key = tuple(tuple(sorted(o["deps"].items())) for o in ops)
@@ -154,38 +174,48 @@ def _schedule(ops):
                 succ[d].append((k, raw, lat[d]))
         alts = [[(e, c) for e, (_, c) in o["alts"].items()] for o in ops]
         zero, prio = [0.0] * n, [o["prio"] for o in ops]
-        best, top, seed = None, None, [CFG["seed"]]
+        top, seed, its = None, [0], CFG["its"]
 
         def rand():
             seed[0] = (seed[0] * 1103515245 + 12345) % 2147483648
             return seed[0] / 2147483648.0
-        pri = [o["at"] for o in ops]
-        for it in range(CFG["its"]):
-            for k in range(n):
-                for d, _, _ in pred[k]:
-                    if pri[d] >= pri[k]:
-                        pri[k] = pri[d] + 1e-6
-            start, end, eng = _place(sorted(range(n), key=lambda k: pri[k]), alts, pred, zero)
-            span = max(end[k] + lat[k] for k in range(n))
-            if best is None or span <= best[0] + CFG["temp"] * rand() * (1.0 - it / CFG["its"]):
-                best = (span, start, end, eng)
-                if top is None or span < top[0]:
-                    top = best
-            if it % 50 == 49:
-                fixed = [[x for x in alts[k] if x[0] == best[3][k]] for k in range(n)]
-                _, late, _ = _place(sorted(range(n), key=lambda k: (-best[2][k], -k)), fixed, succ, prio)
-                pri = [-x for x in late]
-            else:
-                pri, moved = list(best[1]), []
-                for _ in range(1 + int(CFG["moves"] * rand())):
-                    k = int(rand() * n)
-                    pri[k] += CFG["noise"] * (rand() - 0.5) * rand()
-                    moved.append(k)
-                if rand() < 0.5:
-                    for k in range(max(moved), -1, -1):
-                        for d, _, _ in pred[k]:
-                            if pri[d] >= pri[k]:
-                                pri[d] = pri[k] - 1e-3
+        for seed[0] in CFG["seeds"]:
+            best = keep = None
+            for it in range(CFG["gits"]):
+                pri = [o["at"] for o in ops] if keep is None else list(keep[1])
+                for _ in range(0 if keep is None else 4):
+                    pri[int(rand() * n)] += 6.0 * (rand() - 0.5)
+                start, end = _greedy(alts, pred, succ, pri)
+                span = max(end[k] + lat[k] for k in range(n))
+                if keep is None or span <= keep[0]:
+                    keep = (span, pri, start)
+            pri = list(keep[2])
+            for it in range(its):
+                for k in range(n):
+                    for d, _, _ in pred[k]:
+                        if pri[d] >= pri[k]:
+                            pri[k] = pri[d] + 1e-6
+                start, end, eng = _place(sorted(range(n), key=lambda k: pri[k]), alts, pred, zero)
+                span = max(end[k] + lat[k] for k in range(n))
+                if best is None or span <= best[0] + 100.0 * rand() * (1.0 - it / its):
+                    best = (span, start, end, eng)
+                    if top is None or span < top[0]:
+                        top = best
+                if it % 50 == 49:
+                    fixed = [[x for x in alts[k] if x[0] == best[3][k]] for k in range(n)]
+                    _, late, _ = _place(sorted(range(n), key=lambda k: (-best[2][k], -k)), fixed, succ, prio)
+                    pri = [-x for x in late]
+                else:
+                    pri, moved = list(best[1]), []
+                    for _ in range(1 + int(3 * rand())):
+                        k = int(rand() * n)
+                        pri[k] += 6000.0 * (rand() - 0.5) * rand()
+                        moved.append(k)
+                    if rand() < 0.5:
+                        for k in range(max(moved), -1, -1):
+                            for d, _, _ in pred[k]:
+                                if pri[d] >= pri[k]:
+                                    pri[d] = pri[k] - 1e-3
         _, start, end, eng = top
         _ORDERS[key] = (eng, {e: sorted((k for k in range(n) if eng[k] == e), key=lambda k: (start[k], k)) for e in "VAPGSX"}, top[0])
     return _ORDERS[key]
@@ -194,10 +224,7 @@ def _schedule(ops):
 def _emit(ops, queues, T):
     n = len(ops)
     eng, order, _ = _schedule(ops)
-    pos = {}
-    for e in order:
-        for j, k in enumerate(order[e]):
-            pos[k] = j
+    pos = {k: j for e in order for j, k in enumerate(order[e])}
     waits = [[] for _ in range(n)]
     marked = set()
     for e in "VAPGS":
@@ -216,13 +243,7 @@ def _emit(ops, queues, T):
                     seen[f] = j
                     waits[k].append(("eng", order[f][j]))
                     marked.add(order[f][j])
-    count = {}
-    for e in "VAPG":
-        c = 0
-        for k in order[e]:
-            if k in marked:
-                c += 1
-                count[k] = c
+    count = {k: j + 1 for e in "VAPG" for j, k in enumerate(x for x in order[e] if x in marked)}
     for e in "VAPGS":
         q = queues[e]
         for k in order[e]:
@@ -247,7 +268,6 @@ def rank_program(g, core, T, topo):
         _relay_program(g, core, T, topo, plan)
         return
     A, F = AluOpType, ActivationFunctionType
-    GATH, CHUNKS = CFG["g"], CFG["chunks"]
     ops, log, ndma, sent, at = [], {}, [0], [0], [-100.0]
     far = [d for d in range(N) if (me, d) in plan]
     near = [d for d in range(N) if d != me and d not in far]
@@ -305,7 +325,7 @@ def rank_program(g, core, T, topo):
             for (o, l, r, st, sp, _) in group:
                 ins = q.matmul(o, l, r, st, sp)
             return ins
-        op({"P": (run, 60.0 + sum(max(64, x[5]) for x in group) * CFG["pe"])}, reads, ["ps%d" % bank])
+        op({"P": (run, 60.0 + sum(max(64, x[5]) for x in group) * PEC)}, reads, ["ps%d" % bank])
 
     def dma(e, out, src, reads, writes, prio=0.0, lat=T_DMA):
         name = "d%d" % ndma[0]
@@ -363,7 +383,7 @@ def rank_program(g, core, T, topo):
                 n_in = len(theirs[piece, me]) + (len(theirs["t", me]) if piece == "l" else 0)
             else:
                 n_in = len(topo.engines(plan[(s, me)][piece in "cl"], core))
-            arrives("a%s%d" % (piece, s), n_in, CFG["direct" if s in near else "relayed"] + late, [],
+            arrives("a%s%d" % (piece, s), n_in, (T_NEAR if s in near else T_FAR) + late, [],
                     [("L" + x, s, s + 1) for x in ("lt" if piece == "l" else piece)])
     sources = [me] + near + far
     iota(T.cx3[:], [[64, 2], [0, 8], [1, 8]], 0, 0, 128, ["call", "cx3"])
@@ -389,14 +409,12 @@ def rank_program(g, core, T, topo):
     def tg(c):
         return T.tg[:, c:c + 1]
     GCB, GON, GE, GO8, GF, GP, GG, GT = range(8)
-    ts(tg(GF), pf(PI4), pf(PF64), None, A.add, None, 1, ["pf"], [("tg", GF, GF + 1)])
-    ts(tg(GCB), pf(PG16), 15.0, None, A.add, None, 1, ["pf"], [("tg", GCB, GCB + 1)])
-    ts(tg(GON), pf(PI), pf(PF64), None, A.add, None, 1, ["pf"], [("tg", GON, GON + 1)])
-    ts(tg(GE), pf(PI), 4.0, pf(PF64), A.mult, A.add, 1, ["pf"], [("tg", GE, GE + 1)])
-    ts(tg(GO8), pf(PI8), pf(PF64), None, A.add, None, 1, ["pf"], [("tg", GO8, GO8 + 1)])
-    ts(tg(GP), pf(PA), 16.0, tg(GF), A.mult, A.add, 1, ["pf", ("tg", GF, GF + 1)], [("tg", GP, GP + 1)])
-    ts(tg(GG), pf(PU), 8.0, pf(PG16), A.add, A.add, 1, ["pf"], [("tg", GG, GG + 1)])
-    ts(tg(GT), tg(GE), 3.0, None, A.add, None, 1, [("tg", GE, GE + 1)], [("tg", GT, GT + 1)])
+    for col, src, s1, s2, o0, o1, rd in (
+            (GF, pf(PI4), pf(PF64), None, A.add, None, []), (GCB, pf(PG16), 15.0, None, A.add, None, []),
+            (GON, pf(PI), pf(PF64), None, A.add, None, []), (GE, pf(PI), 4.0, pf(PF64), A.mult, A.add, []),
+            (GO8, pf(PI8), pf(PF64), None, A.add, None, []), (GP, pf(PA), 16.0, tg(GF), A.mult, A.add, [("tg", GF, GF + 1)]),
+            (GG, pf(PU), 8.0, pf(PG16), A.add, A.add, []), (GT, tg(GE), 3.0, None, A.add, None, [("tg", GE, GE + 1)])):
+        ts(tg(col), src, s1, s2, o0, o1, 1, ["pf"] + rd, [("tg", col, col + 1)])
     ts(T.tf0[:], T.cx[:, 0:4], pf(PA), 1000.0, A.not_equal, A.mult, 4, ["cx", "pf"], ["tf0"])
     ts(T.tf[:], T.tf0[:], tg(GF), None, A.add, None, 4, ["tf0", ("tg", GF, GF + 1)], ["tf"])
     ts(T.tf48[:], T.tf0[:], tg(GF), 48.0, A.add, A.add, 4, ["tf0", ("tg", GF, GF + 1)], ["tf48"])
@@ -408,18 +426,13 @@ def rank_program(g, core, T, topo):
     for a in range(4):
         pick(T.mr[:, a * 128:(a + 1) * 128], T.cx2[:], T.tf[:, a:a + 1], 1.0, 128, ["cx2", "tf"], [("mr", a, a + 1)])
         pick(T.mf[:, a * 176:(a + 1) * 176], T.cx[:], T.tf48[:, a:a + 1], 1.0, 176, ["cx", "tf48"], [("mf", a, a + 1)])
-    pick(T.mcb[:], T.cx[:, 0:144], tg(GCB), 1.0, 144, ["cx", "tg"], ["mcb"])
-    pick(T.mi1[:], T.cx[:, 0:128], pf(PP), 1.0, 128, ["cx", "pf"], ["mi1"])
-    pick(T.mon[:], T.cx2[:], tg(GON), 1.0, 128, ["cx2", "tg"], ["mon"])
-    pick(T.mo8[:], T.cx3[:], tg(GO8), 1.0, 128, ["cx3", "tg"], ["mo8"])
-    pick(T.me[:], T.cx[:, 0:132], tg(GT), 0.125, 132, ["cx", "tg"], ["me"])
-    pick(T.mp[:], T.cx[:, 0:128], tg(GP), 1.0, 128, ["cx", "tg"], ["mp"])
+    for name, cols, n, target, w in (("mcb", "cx", 144, tg(GCB), 1.0), ("mi1", "cx", 128, pf(PP), 1.0), ("mon", "cx2", 128, tg(GON), 1.0),
+                                     ("mo8", "cx3", 128, tg(GO8), 1.0), ("me", "cx", 132, tg(GT), 0.125), ("mp", "cx", 128, tg(GP), 1.0)):
+        pick(T[name][:], T[cols][:, 0:n], target, w, n, [cols, "tg", "pf"], [name])
     for jj in range(8):
         pick(T.mg[:, jj * 136:(jj + 1) * 136], T.cx[:, 0:136], T.tj[:, jj:jj + 1], K, 136, ["cx", "tj"], [("mg", jj, jj + 1)])
-    lin(T.mck[:], T.mcb[:], 4096.0, CZ, 144, ["mcb"], ["mck"])
-    lin(T.mch[:], T.mcb[:], 16384.0, CZ, 144, ["mcb"], ["mch"])
-    for name, src, w in (("mni", "mi1", -1.0), ("mn2", "mi1", -2.0), ("mnb", "mi1", -BIG), ("mi4", "mi1", 4096.0),
-                         ("mi8", "mi1", 8.0), ("msum", "mon", 0.125), ("monk", "mon", K / 2)):
+    for name, src, w in (("mck", "mcb", 4096.0), ("mch", "mcb", 16384.0), ("mni", "mi1", -1.0), ("mn2", "mi1", -2.0),
+                         ("mnb", "mi1", -BIG), ("mi4", "mi1", 4096.0), ("mi8", "mi1", 8.0), ("msum", "mon", 0.125), ("monk", "mon", K / 2)):
         lin(T[name][:], T[src][:], w, CZ, 128, [src], [name])
     tt(T.monp[:], T.mon[:], T.mi8[:], A.add, 128, ["mon", "mi8"], ["monp"])
     tt(T.mo8p[:], T.mo8[:], T.mi8[:], A.add, 128, ["mo8", "mi8"], ["mo8p"])
@@ -448,15 +461,11 @@ def rank_program(g, core, T, topo):
                  _slot(T, "x", s), True, True, 240) for b in range(2)], ["mr", ("Lx", s, s + 1)], hh)
             c0 = x0 + s * V + 480 * hh
             lin(T.win[:, c0:c0 + 480], ps(hh)[:, 0:480], 1.0, CM, 480, ["ps%d" % hh], [("win", c0, c0 + 480)], on="VA")
-        grp = []
+        ws = [T.mf[:, a * 176 + 48 - 16 * s:a * 176 + 176 - 16 * s] for a in range(4)]
+        mm([(ps(6)[:, 120 * a:120 * a + 120], ws[a], src[:, s * IB:s * IB + 120], False, lastsrc and a == 3 and b == 1, 120)
+            for a in range(4) for b, src in enumerate((T.lh, T.ll))], ["mf", ("lhc", s, s + 1), ("llc", s, s + 1)], 6)
         for a in range(4):
-            w = T.mf[:, a * 176 + 48 - 16 * s:a * 176 + 176 - 16 * s]
-            grp.append((ps(6)[:, 120 * a:120 * a + 120], w, T.lh[:, s * IB:s * IB + 120], False, False, 120))
-            grp.append((ps(6)[:, 120 * a:120 * a + 120], w, T.ll[:, s * IB:s * IB + 120], False, lastsrc and a == 3, 120))
-        mm(grp, ["mf", ("lhc", s, s + 1), ("llc", s, s + 1)], 6)
-        for a in range(4):
-            w = T.mf[:, a * 176 + 48 - 16 * s:a * 176 + 176 - 16 * s]
-            mm([(ps(2 + a)[:, 0:384], w, _slot(T, "h", s), k == 0, lastsrc, 384)], ["mf", ("Lh", s, s + 1)], 2 + a)
+            mm([(ps(2 + a)[:, 0:384], ws[a], _slot(T, "h", s), k == 0, lastsrc, 384)], ["mf", ("Lh", s, s + 1)], 2 + a)
     cp(T.cu[:], ps(6)[:, 0:480], 480, ["ps6"], ["cu"])
     for a in range(4):
         c0 = H0 + 384 * a
@@ -470,16 +479,12 @@ def rank_program(g, core, T, topo):
         for b, name in enumerate(("lh", "ll")):
             dma("S", T.lth[b, s], T[name][:, s * IB + 240:s * IB + 255], [(name + "l", s, s + 1)], [("lth", 4 * b + s, 4 * b + s + 1)],
                 lat=3000.0)
-        mm([(ps(7)[:, 120 * s:120 * s + 120], T.mp[:], T.lh[:, s * IB + 120:s * IB + 240], True, False, 120),
-            (ps(7)[:, 120 * s:120 * s + 120], T.mp[:], T.ll[:, s * IB + 120:s * IB + 240], False, True, 120)],
-           ["mp", ("lhl", s, s + 1), ("lll", s, s + 1)], 7)
-    k = 0
-    for b in range(2):
-        for gq in range(8):
-            f = gq // 4
-            dma("S" if k % 3 else "G", T.thw[16 * gq + b:16 * gq + b + 1, :], T.lth[b, :, 64 * f:64 * f + 64, :],
-                [("lth", 4 * b, 4 * b + 4), "thz"], [("thw", k, k + 1)])
-            k += 1
+        mm([(ps(7)[:, 120 * s:120 * s + 120], T.mp[:], src[:, s * IB + 120:s * IB + 240], b == 0, b == 1, 120)
+            for b, src in enumerate((T.lh, T.ll))], ["mp", ("lhl", s, s + 1), ("lll", s, s + 1)], 7)
+    for k in range(16):
+        b, gq = k // 8, k % 8
+        dma("S" if k % 3 else "G", T.thw[16 * gq + b:16 * gq + b + 1, :], T.lth[b, :, 64 * (gq // 4):64 * (gq // 4) + 64, :],
+            [("lth", 4 * b, 4 * b + 4), "thz"], [("thw", k, k + 1)])
     at[0] = 2.0
     cp(T.hli[:], ps(7)[:, 0:480], 480, ["ps7"], ["hli"])
     tt(T.hp0[:], ps(7)[:, 0:480], T.ki[:], A.add, 480, ["ps7", "ki"], ["hp0"], f=1.0)
@@ -512,11 +517,11 @@ def rank_program(g, core, T, topo):
         tt(T.ilo[:, a:b], T.idw[:, a:b], T.ihi[:, a:b], A.subtract, 384, [("idw", m, m + 1), ("ihi", m, m + 1)], [("ilo", m, m + 1)])
     for m in range(2):
         u0, u1 = 48 * m, 48 * m + 48
-        at[0] = CFG["tth"][m]
+        at[0] = (1.0, 13.0)[m]
         for c in range(C):
             a = 3840 * m + 768 * c
             lin(T.g5[:, a:a + 768], T.thw[:].indirect(T.cu[:, 96 * c + u0:96 * c + u1]), 1.0, CZ, 768,
-                ["thw", "thz", "cu"], [("g5", a, a + 768)], f=GATH, on="VA" if c >= CFG["thv"] else "A")
+                ["thw", "thz", "cu"], [("g5", a, a + 768)], f=GATH, on="VA" if c >= 2 else "A")
         mm([(ps(6)[:, 0:240], cb(j), T.g5[:, 3840 * m + j:3840 * m + 3840:16], j == 0, j == 15, 240) for j in range(16)],
            ["mcb", "g5" if m else ("g5", 0, 3840)], 6)
         lin(T.thc[:, :, u0:u1], ps(6)[:, 0:240], 1.0, CZ, 240, ["ps6"], [("thc", u0, u1)])
@@ -524,7 +529,31 @@ def rank_program(g, core, T, topo):
         tt(T.tlo[:, :, u0:u1], T.thc[:, :, u0:u1], T.thi[:, :, u0:u1], A.subtract, 240,
            [("thc", u0, u1), ("thi", u0, u1)], [("tlo", u0, u1)])
 
+    def sums(bank, col, name, o, wc, stop):
+        step, hc = -(-64 // wc), 16 * wc
+        for c in range(0, C, step):
+            d = min(C, c + step)
+            mm([(ps(bank)[:, col + c * wc:col + d * wc], cb(j, name), T.ab[:, o + c * hc + j:o + d * hc:16], False,
+                 stop and d == C and j == 15, (d - c) * wc) for j in range(16)], [name, ("ab", o + c * hc, o + d * hc)], bank)
+
     diff = [0]
+
+    def apart(o, hc, h0, name):
+        for a in range(0, 5 * hc, 512):
+            b = min(a + 512, 5 * hc)
+            bank = diff[0] % 3
+            diff[0] += 1
+            grp, u = [], a
+            while u < b:
+                v = min(b, (u // hc + 1) * hc)
+                grp.append((ps(bank)[:, u - a:v - a], T.mi1[:], T.dd[:, o + u:o + v], True, False, v - u))
+                grp.append((ps(bank)[:, u - a:v - a], T.mni[:], T[name][:, h0 + u % hc:h0 + u % hc + v - u], False, True, v - u))
+                u = v
+            mm(grp, ["mi1", "mni", ("dd", o + a, o + b), (name, h0, h0 + hc)], bank)
+            act(T.ab[:, o + a:o + b], ps(bank)[:, 0:b - a], F.Abs, b - a, ["ps%d" % bank], [("ab", o + a, o + b)])
+
+    at[0] = -2.0
+    lin(T.hb[:], T.win[:, H0:H0 + 384], 1.0, CN, 384, [("win", H0, H0 + 384)], ["hb"])
     for rnd in range(RO):
         blk = (RO - 1 - rnd) * BLK
         xs = blk + PAD
@@ -538,10 +567,13 @@ def rank_program(g, core, T, topo):
             a, v0, v1 = o + V * m, u0 + 60 * m, u0 + 60 * m + 60
             ur, vr = (lambda name: (name, u0, u1)), (lambda name: (name, v0, v1))
             fbank, nbank = 4 + k % 2 if m else 6, 7 - k % 2
-            at[0] = t0 + (30.0 + 1.8 * k if m else CFG["eq0"] + 1.3 * k)
-            tt(T.eq[:, a:a + V], T["ww%d" % m][:].indirect(T.hw[:, v0:v1]), T.iot[:, r * V:(r + 1) * V],
-               A.is_equal, V, ["ww%d" % m, "hw", ("iot", r, r + 1)], [("eq", a, a + V)], f=GATH)
-            at[0] += 1.0
+            at[0] = t0 + 21.0 + 0.5 * m + 1.3 * k
+            ne = V if m else 480
+            for b in range(0, V, ne):
+                tt(T.eq[:, a + b:a + b + ne], T["ww%d" % m][:].indirect(T.hw[:, v0 + b // 16:v0 + (b + ne) // 16]),
+                   T.iot[:, r * V + b:r * V + b + ne], A.is_equal, ne, ["ww%d" % m, "hw", ("iot", r, r + 1)],
+                   [("eq", a + b, a + b + ne)], f=GATH)
+            at[0] -= 30.0
             if last and m == 0:
                 return
             if last:
@@ -570,12 +602,12 @@ def rank_program(g, core, T, topo):
                     tt(T.t2[:, v0:v1], out, T.t1[:, v0:v1], A.min, 60, ["ps%d" % nbank, vr("t1")], [vr("t2")], f=1.0)
                     act(T[al][:, 60 * r:60 * r + 60], out, F.Sign, 60, ["ps%d" % nbank], [(al, r, r + 1)], scale=1.0, col=CS)
                     ts(T.ix[:, v0:v1], T.t2[:, v0:v1], OFF, None, A.subtract, None, 60, [vr("t2")], [vr("ix")])
-            n5 = V if k < CFG["big"] else 480
+            at[0] += 31.0
             for m2 in (range(2) if last else [m]):
-                for b in range(0, V, n5):
+                for b in (0, 480):
                     a, c0 = o + V * m2 + b, u0 + 60 * m2 + b // 16
-                    lin(T.g5[:, a:a + n5], whole.indirect(T.ix[:, c0:c0 + n5 // 16]), 1.0, CN, n5, [wholer, ("ix", c0, c0 + n5 // 16)],
-                        [("g5", a, a + n5)], f=GATH, on="VA" if (m2, k) in CFG["p5l" if last else "p5v"] else "A")
+                    lin(T.g5[:, a:a + 480], whole.indirect(T.ix[:, c0:c0 + 30]), 1.0, CN, 480, [wholer, ("ix", c0, c0 + 30)],
+                        [("g5", a, a + 480)], f=GATH, on="VA" if m2 and k >= (2 if last else 3) else "A")
 
         if last:
             at[0] = t0 + 10.0
@@ -593,63 +625,62 @@ def rank_program(g, core, T, topo):
             wr = lambda name: (name, w0, w1)
             for c in range(C):
                 a, b = o + c * hc, o + (c + 1) * hc
+                got = xw.indirect(T.cu[:, 96 * c + w0:96 * c + w1])
+                if k == 0:
+                    at[0] = t0 - 1.0 + 0.01 * c
+                    lin(T.dd[:, a:b], got, 1.0, CN, hc, [xr, "cu"], [("dd", a, b)], f=GATH)
+                    continue
                 at[0] = t0 + 14.0 * a / 7680
-                tt(T.dd[:, a:b], xw.indirect(T.cu[:, 96 * c + w0:96 * c + w1]), hits, A.subtract, hc, [xr, hr, "cu"],
-                   [("dd", a, b)], f=GATH)
+                tt(T.dd[:, a:b], got, hits, A.subtract, hc, [xr, hr, "cu"], [("dd", a, b)], f=GATH)
                 act(T.ab[:, a:b], T.dd[:, a:b], F.Abs, hc, [("dd", a, b)], [("ab", a, b)])
+            if k == 0:
+                apart(o, hc, h0, "hb")
             te = t0 + 14.0 * (o + 5 * hc) / 7680
             at[0] = te - 0.5
             kd = 3 + 4 * (k % 2)
             out = ps(kd)[:, 0:5 * wc]
             mm([(out, T.mnb[:], T.fl[:, :, w0:w1], True, False, 5 * wc), (out, T.mi1[:], T.chi[:, :, w0:w1], False, False, 5 * wc),
                 (out, T.mi1[:], T.clo[:, :, w0:w1], False, False, 5 * wc)], ["mnb", "mi1", "chi", "clo", wr("fl")], kd)
-            mm([(out, cb(j, "mck"), T.ab[:, o + j:o + 5 * hc:16], False, j == 15, 5 * wc) for j in range(16)],
-               ["mck", ("ab", o, o + 5 * hc)], kd)
-            lin(T.key[:, :, w0:w1], out, 1.0, CN, 5 * wc, ["ps%d" % kd], [wr("key")])
+            sums(kd, 0, "mck", o, wc, True)
+            lin(T.key[:, :, w0:w1], out, 1.0, CN, 5 * wc, ["ps%d" % kd], [wr("key")], on="V")
             at[0] = te + 0.8
             tt(T.m1[:, :, w0:w1], T.key[:, 0:2, w0:w1], T.key[:, 2:4, w0:w1], A.min, 2 * wc, [wr("key")], [wr("m1")])
-            at[0] += CFG["gap"]
+            at[0] += 0.3
             tt(T.m2[:, w0:w1], T.m1[:, 0, w0:w1], T.m1[:, 1, w0:w1], A.min, wc, [wr("m1")], [wr("m2")])
-            at[0] += CFG["gap"]
+            at[0] += 0.3
             tt(T.mi[:, w0:w1], T.m2[:, w0:w1], T.key[:, 4, w0:w1], A.min, wc, [wr("m2"), wr("key")], [wr("mi")])
-            at[0] += CFG["gap"]
+            at[0] += 0.3
             ts(T.ma[:, w0:w1], T.mi[:, w0:w1], 4095, None, A.bitwise_and, None, wc, [wr("mi")], [wr("ma")])
-            at[0] += CFG["gap"]
+            at[0] += 0.3
             ts(T.bi[:, w0:w1], T.ma[:, w0:w1], float(NT - 1), None, A.min, None, wc, [wr("ma")], [wr("bi")])
-            at[0] += CFG["gap"]
-            tt(T.db[:, h0:h0 + hc], xw.indirect(T.bi[:, w0:w1]), hits, A.subtract, hc, [xr, hr, wr("bi")],
-               [("db", h0, h0 + hc)], f=GATH)
-            for a in range(0, 5 * hc, 512):
-                b = min(a + 512, 5 * hc)
-                bank = diff[0] % 3
-                diff[0] += 1
-                grp, u = [], a
-                while u < b:
-                    v = min(b, (u // hc + 1) * hc)
-                    grp.append((ps(bank)[:, u - a:v - a], T.mi1[:], T.dd[:, o + u:o + v], True, False, v - u))
-                    grp.append((ps(bank)[:, u - a:v - a], T.mni[:], T.db[:, h0 + u % hc:h0 + u % hc + v - u], False, True, v - u))
-                    u = v
-                mm(grp, ["mi1", "mni", ("dd", o + a, o + b), ("db", h0, h0 + hc)], bank)
-                act(T.ab[:, o + a:o + b], ps(bank)[:, 0:b - a], F.Abs, b - a, ["ps%d" % bank], [("ab", o + a, o + b)])
+            at[0] += 0.3
+            got = xw.indirect(T.bi[:, w0:w1])
+            if k == 0:
+                lin(T.db[:, h0:h0 + hc], got, 1.0, CN, hc, [xr, wr("bi")], [("db", h0, h0 + hc)], f=GATH, on="VA")
+            else:
+                tt(T.db[:, h0:h0 + hc], got, hits, A.subtract, hc, [xr, hr, wr("bi")], [("db", h0, h0 + hc)], f=GATH)
+            at[0] = t0 + (9.0, 16.0)[m] + 0.1 * k
+            apart(o, hc, h0, "db")
             if w1 % 48 == 0:
-                at[0] += 0.5
+                at[0] = t0 - 5.0
                 u0, u1 = 48 * m, 48 * m + 48
                 for c in range(C):
                     tt(T.nb[:, c, u0:u1], T.key[:, c, u0:u1], T.mi[:, u0:u1], A.is_le, 48, [("key", u0, u1), ("mi", u0, u1)],
                        [("nb", 5 * m + c, 5 * m + c + 1)])
                 act(T.nl[:, :, u0:u1], T.key[:, :, u0:u1], F.Relu, 240, [("key", u0, u1)], [("nl", u0, u1)])
-                for (v0, v1) in CHUNKS:
-                    if v0 // 48 == m:
-                        vw, vo = v1 - v0, 80 * v0
-                        out = ps(4)[:, 5 * (v0 - u0):5 * (v1 - u0)]
-                        mm([(out, w, src[:, :, v0:v1], j == 0, False, 5 * vw) for j, (w, src) in
-                            enumerate(((T.mni[:], T.thi), (T.mni[:], T.tlo), (T.mn2[:], T.nl), (T.mi4[:], T.nb)))],
-                           ["mni", "mn2", "mi4", ("thi", v0, v1), ("tlo", v0, v1), ("nl", v0, v1), ("nb", 5 * m, 5 * m + 5)], 4)
-                        mm([(out, cb(j), T.ab[:, vo + j:vo + 80 * vw:16], False, j == 15, 5 * vw) for j in range(16)],
-                           ["mcb", ("ab", vo, vo + 80 * vw)], 4)
-                        act(T.fl[:, :, v0:v1], out, F.Sign, 5 * vw, ["ps4"], [("fl", v0, v1)], scale=1.0, col=CH)
-                mm([(ps(5)[:, 0:384], T.mi1[:], T.ihi[:, 384 * m:384 * m + 384], True, False, 384),
-                    (ps(5)[:, 0:384], T.mi1[:], T.ilo[:, 384 * m:384 * m + 384], False, False, 384)],
+                mine = [(v0, v1, ps(4)[:, 5 * (v0 - u0):5 * (v1 - u0)]) for (v0, v1) in CHUNKS if v0 // 48 == m]
+                mm([(ps(4)[:, 0:240], T.mz[:, 0:128], T.mz[:, 0:240], True, False, 240)]
+                   + [(o2, T.mni[:], src[:, :, v0:v1], False, False, 5 * (v1 - v0)) for v0, v1, o2 in mine for src in (T.thi, T.tlo)],
+                   ["mz", "mni", ("thi", u0, u1), ("tlo", u0, u1)], 4)
+                for v0, v1, _ in mine:
+                    if v1 == u1:
+                        mm([(o2, w, src[:, :, y0:y1], False, False, 5 * (y1 - y0)) for y0, y1, o2 in mine
+                            for w, src in ((T.mn2[:], T.nl), (T.mi4[:], T.nb))],
+                           ["mn2", "mi4", ("nl", u0, u1), ("nb", 5 * m, 5 * m + 5)], 4)
+                    sums(4, 5 * (v0 - u0), "mcb", 80 * v0, v1 - v0, v1 == u1)
+                for v0, v1, o2 in mine:
+                    act(T.fl[:, :, v0:v1], o2, F.Sign, 5 * (v1 - v0), ["ps4"], [("fl", v0, v1)], scale=1.0, col=CH)
+                mm([(ps(5)[:, 0:384], T.mi1[:], src[:, 384 * m:384 * m + 384], b == 0, False, 384) for b, src in enumerate((T.ihi, T.ilo))],
                    ["mi1", ("ihi", m, m + 1), ("ilo", m, m + 1)], 5)
                 spread([T.fl], m, [("fl", u0, u1)], own=False)
                 lin(T["ww%d" % m][:], ps(5)[:, 0:384], 1.0, CK, 384, ["ps5"], ["ww%d" % m])

@@ -1,44 +1,45 @@
 from concourse.bass import DstId, RemoteDMATransfer
 from concourse.mybir import AluOpType, ActivationFunctionType
 
-N, V, HQ, C, RO = 4, 960, 1536, 5, 3
+N, V, H, C, RO = 4, 960, 768, 5, 3
 NT = N * V
-XB, IB, OB = 624, 256, 360
-PAD = 16
-BLK = PAD + NT
-H0 = RO * BLK
-BIG = 2.0 ** 23
-K = 32768.0
-OFF = -1.5 * K
-CHUNKS = [(0, 24), (24, 48), (48, 72), (72, 96)]
-CYC, PEC, GATH, HOP, LOOK, T_DMA, T_NEAR, T_FAR = 0.83, 0.42, 1.5, 140.0, 200.0, 2200.0, 9000.0, 12500.0
-CFG = {"seeds": (1, 2, 3), "gits": 200, "its": 7000}
+XB, IB, OB = 624, 240, 192
+MAGIC = 1.5 * 2.0 ** 23
+CAP = 4095.0 * 4096.0
+STEP = 4096.0
+MARK = 64 * STEP
+CYC, PEC, GATH, HOP, LOOK, T_DMA, T_WIN, T_NEAR, T_FAR = 0.83, 0.42, 1.5, 140.0, 200.0, 2200.0, 4500.0, 9000.0, 12500.0
+ADD, T_ISSUE, T_ADD = 2, 900.0, 3000.0
+CFG = {"pfix": 60.0, "seed": 2, "shifts": 7500, "swaps": 12000, "passes": 4, "cut": (768, 960, 768, 960), "lag": 0.0, "w": "dp", "w0": "dd", "sets": ((0, 2), (2, 5)), "marks": ((0, 5),),
+       "ends": (((0, 2), (2, 4)), ((0, 2), (2, 4)))}
 
-F32, BF, I32, U16 = "float32", "bfloat16", "int32", "uint16"
+F32, BF, F16, I32, U16 = "float32", "bfloat16", "float16", "int32", "uint16"
 SCRATCH = {
-    "sx": ("dram", [N, 128, 240], BF), "sh": ("dram", [N, 128, 384], BF), "sc": ("dram", [N, 128, 120], I32),
-    "sl": ("dram", [N, 128, 120], I32), "st": ("dram", [N, 128, 15], I32),
-    "rx": ("dram", [128, 240], BF), "rh": ("dram", [128, 384], BF), "rc": ("dram", [128, 120], I32),
-    "ro": ("dram", [128, OB], BF), "lth": ("dram", [2, N, 128, 15], BF),
-    "m1": ("sbuf", [128, 2, 96], F32),
+    "sx": ("dram", [N, 128, 240], BF), "sh": ("dram", [N, 128, 384], BF),
+    "rx": ("dram", [128, 240], BF), "rh": ("dram", [128, 384], BF), "rc": ("dram", [128, IB], F16),
+    "rt": ("dram", [2, 128, 15], BF), "ro": ("dram", [128, 180], BF), "lt": ("dram", [2 * N, 128, 15], BF),
 }
 for _names, _shape, _dt in (
-        ("lb", [N * XB], BF), ("li", [N * IB], I32), ("lh ll", [N * IB], BF), ("lo res", [N * OB], BF), ("win", [H0 + HQ], F32),
-        ("dd ab eq g5", [7680], BF), ("db", [HQ], BF), ("hb", [384], BF), ("iot", [NT], F32), ("thw", [NT], BF), ("m2", [96], F32),
-        ("mi ma", [96], I32), ("bi", [96], U16), ("cu hw ix", [480], U16), ("idw", [768], F32), ("ihi ilo", [768], BF),
-        ("ww0 ww1", [384], F32), ("hli hls", [480], I32), ("xf", [V], F32), ("al0 al1 als alt", [240], F32),
-        ("cx", [176], F32), ("cx2 cx3", [128], F32), ("pc", [2], I32), ("pi", [8], I32), ("pf tg cc", [16], F32),
-        ("tf tf0 tf48", [4], F32), ("tj tj0", [8], F32), ("me", [132], BF), ("mf", [4 * 176], BF), ("mr", [4 * 128], BF),
-        ("mg", [8 * 136], BF), ("clf thc key", [C, 96], F32), ("nb nl fl chi clo thi tlo", [C, 96], BF),
-        ("ki si0 hp0 hp1 hp2 sfp home al2 t1 t2", [480], F32), ("mz shi slo fb fc", [480], BF), ("mcb mck mch", [144], BF),
-        ("mi1 mni mn2 mnb mi4 mi8 mon msum monp monk mo8 mo8p mp", [128], BF)):
+        ("lb", [N * XB], BF), ("li", [N, IB], I32), ("lf sf", [N, IB], F16), ("ti", [64], I32), ("tb", [128], BF), ("iot", [NT], F32),
+        ("cx", [48], F32), ("low pf", [4], F32), ("pc pi", [2], I32), ("thw", [NT], BF),
+        ("mw", [8 * 128], BF), ("mh", [4, 240], BF), ("ml", [2, 192], BF), ("mt", [2, 144], BF), ("mf", [8, 240], BF),
+        ("mr", [4 * 128], BF), ("mx md md7 md6", [2, 136], BF), ("me", [136], BF), ("mcb mck mcp mcf", [144], BF),
+        ("mbc", [16 * 128], BF), ("mal", [2 * 128], BF), ("mg", [8, 136], BF),
+        ("mi1 mni mnb mhf ck0 cc1", [128], BF), ("mnc one", [512], BF), ("hc", [48], F16)):
     for _n in _names.split():
         SCRATCH[_n] = ("sbuf", [128] + _shape, _dt)
+for _f in "AB":
+    for _names, _shape, _dt in (
+            ("win ab yy tmp dd", [NT], BF), ("hit db", [H], BF), ("ys", [3 * H], BF), ("idw", [384], F32), ("ns", [480], F32), ("cu hw pos", [240], U16), ("bi", [48], U16),
+            ("cf hf thf", [240], F16), ("nb fl", [240], BF), ("sa sb", [96], F32), ("sc mi", [48], F32),
+            ("xa xb xc rr mk xk xl", [480], BF), ("lo", [N * OB], BF), ("res", [N, OB], BF)):
+        for _n in _names.split():
+            SCRATCH[_n + _f] = ("sbuf", [128] + _shape, _dt)
 for _k in range(8):
     SCRATCH["ps%d" % _k] = ("psum", [128, 512], F32)
 
 SEMAPHORES = (["eV", "eA", "eP", "eG", "sent", "rin1", "rin2", "rout"]
-              + ["a%s%d" % (k, s) for k in "xhclo" for s in range(N)] + ["d%d" % k for k in range(52)])
+              + ["a%s%d" % (k, s) for k in "xhctop" for s in range(N)] + ["d%d" % k for k in range(56)])
 
 
 def _mask(engines):
@@ -67,19 +68,20 @@ def _lanes(T, topo, plan, s):
     off = topo.engines(T.cores[s], T.cores[near])
     rest = [e for e in topo.engines(T.cores[s], plan[(s, far[0])][0]) if e not in off]
     h, q = len(rest) // 2, len(off) // 4
-    lanes = {("x", near): off[2 * q:3 * q], ("c", near): off[3 * q:], ("h", near): off, ("l", near): off, ("t", near): off[:1]}
+    lanes = {("x", near): off, ("c", near): off, ("h", near): off, ("t", near): off[:2 * q], ("u", near): off[2 * q:]}
     for j, d in enumerate(far):
-        lanes["x", d] = lanes["h", d] = lanes["l", d] = rest[j * h:(j + 1) * h]
-        lanes["c", d] = off[j * q:(j + 1) * q]
-        lanes["t", d] = rest[j * h:j * h + 1]
+        lanes["x", d] = lanes["h", d] = lanes["c", d] = rest[j * h:(j + 1) * h]
+        lanes["t", d], lanes["u", d] = rest[j * h:j * h + h // 2], rest[j * h + h // 2:(j + 1) * h]
     return lanes
 
 
 def _slot(T, piece, s):
-    buf, c0, c1 = {"x": ("lb", 0, 240), "h": ("lb", 240, XB), "c": ("li", 0, 120), "l": ("li", 120, 240), "t": ("li", 240, 255),
-                   "lt": ("li", 120, 255)}[piece]
-    w = XB if buf == "lb" else IB
-    return T[buf][:, s * w + c0:s * w + c1]
+    if piece in "tu":
+        return T.lt[N * (piece == "u") + s]
+    if piece == "c":
+        return T.lf[:, s, :]
+    c0, c1 = {"x": (0, 240), "h": (240, XB)}[piece]
+    return T.lb[:, s * XB + c0:s * XB + c1]
 
 
 def _relay_program(g, core, T, topo, plan):
@@ -89,51 +91,25 @@ def _relay_program(g, core, T, topo, plan):
         lanes = _lanes(T, topo, plan, s)
         out = topo.engines(core, T.cores[d])
         rid, pid = topo.addr(T.cores[d], core)
-        if core == pair[0]:
-            steps = [(T.sem.rin1, len(lanes["x", d]), _slot(T, "x", s), T.rx[:], "ax"),
-                     (T.sem.rin2, len(lanes["h", d]), _slot(T, "h", s), T.rh[:], "ah"),
-                     (T.sem.rout, len(topo.engines(T.cores[s], core)), T.lo[:, s * OB:(s + 1) * OB], T.ro[:], "ao")]
+        f = int(core == pair[0])
+        if f:
+            steps = [(T.sem.rin1, len(lanes["x", d]), [(_slot(T, "x", s), T.rx[:])], "ax"),
+                     (T.sem.rin2, len(lanes["t", d]) + len(lanes["u", d]), [(_slot(T, "tu"[b], s), T.rt[b]) for b in range(2)], "at")]
         else:
-            steps = [(T.sem.rin1, len(lanes["c", d]), _slot(T, "c", s), T.rc[:], "ac"),
-                     (T.sem.rin2, len(lanes["l", d]) + len(lanes["t", d]), _slot(T, "lt", s), _slot(T, "lt", s), "al")]
-        for sem, n, land, src, name in steps:
+            steps = [(T.sem.rin1, len(lanes["c", d]), [(_slot(T, "c", s), T.rc[:])], "ac"),
+                     (T.sem.rin2, len(lanes["h", d]), [(_slot(T, "h", s), T.rh[:])], "ah")]
+        steps.append((T.sem.rout, len(topo.engines(T.cores[s], core)), [(T["lo" + "AB"[f]][:, s * OB:s * OB + 180], T.ro[:])],
+                      "a" + "op"[f]))
+        for sem, n, moves, name in steps:
             g.wait_ge(sem, n)
-            g.remote_dma(land, src, T.sem["%s%d" % (name, s)], T.sem.sent, pid, rid, _mask(out))
+            k = len(out) // len(moves)
+            g.remote_dma_fused([RemoteDMATransfer(dst_ids=[DstId(rid=rid, pnc=pid)], dma_engine_mask=_mask(out[j * k:(j + 1) * k]),
+                                                  remote_sem=T.sem["%s%d" % (name, s)], src=src, dst=land)
+                                for j, (land, src) in enumerate(moves)], local_sem=T.sem.sent)
         g.wait_ge(T.sem.sent, len(steps) * len(out))
 
 
 _ORDERS = {}
-
-
-def _place(seq, alts, before, first):
-    n = len(alts)
-    b0, b1 = {e: [] for e in "VAPGS"}, {e: [] for e in "VAPGS"}
-    start, end, eng = [0.0] * n, [0.0] * n, [None] * n
-    for k in seq:
-        best = None
-        for e, cost in alts[k]:
-            t = first[k]
-            for d, raw, wait in before[k]:
-                u = end[d] + wait + (HOP if raw or eng[d] != e else 0.0)
-                if u > t:
-                    t = u
-            j = 0
-            if e != "X":
-                s0, s1 = b0[e], b1[e]
-                j = len(s0)
-                while j > 0 and s1[j - 1] > t:
-                    j -= 1
-                while j < len(s0) and s0[j] < t + cost:
-                    if s1[j] > t:
-                        t = s1[j]
-                    j += 1
-            if best is None or t + cost < best[0]:
-                best = (t + cost, t, e, j)
-        end[k], start[k], eng[k], j = best
-        if eng[k] != "X":
-            b0[eng[k]].insert(j, start[k])
-            b1[eng[k]].insert(j, end[k])
-    return start, end, eng
 
 
 def _greedy(alts, pred, succ, pri):
@@ -141,83 +117,193 @@ def _greedy(alts, pred, succ, pri):
     free = {e: 0.0 for e in "VAPGSX"}
     start, end, eng, left = [0.0] * n, [0.0] * n, [None] * n, [len(p) for p in pred]
     ready = [k for k in range(n) if not left[k]]
-    when = {k: {e: 0.0 for e, _ in alts[k]} for k in ready}
+    when = {k: {e: 0.0 for e in alts[k]} for k in ready}
     while ready:
         t, e = min((max(when[k][e], free[e]), e != "A", e) for k in ready for e in when[k])[::2]
         k = min((k for k in ready if e in when[k] and when[k][e] <= t + (LOOK if len(when[k]) == 1 else 0.0)), key=lambda k: pri[k])
         ready.remove(k)
         start[k], eng[k] = max(when[k][e], free[e]), e
-        end[k] = start[k] + dict(alts[k])[e]
+        end[k] = start[k] + alts[k][e]
         if e != "X":
             free[e] = end[k]
         for s, _, _ in succ[k]:
             left[s] -= 1
             if not left[s]:
                 ready.append(s)
-                when[s] = {f: max(end[d] + w + (HOP if raw or eng[d] != f else 0.0) for d, raw, w in pred[s]) for f, _ in alts[s]}
-    return start, end
+                when[s] = {f: max(end[d] + w + (HOP if raw or eng[d] != f else 0.0) for d, raw, w in pred[s]) for f in alts[s]}
+    return start, end, eng
+
+
+def _shifts(ops, full, alts, pred, succ, lat, pri):
+    n, seed, its = len(ops), [CFG["seed"]], CFG["shifts"]
+    phase = [(o["fit"], o["rnd"], o["grp"]) for o in ops]
+    free = [k for k in range(n) if phase[k][2] != "first"]
+    names, both = sorted(set(phase[k] for k in free)), [k for k in free if len(full[k]) > 1]
+
+    def rand():
+        seed[0] = (seed[0] * 1103515245 + 12345) % 2147483648
+        return seed[0] / 2147483648.0
+    now = best = None
+    for it in range(its):
+        p, a, u = list(pri), alts, rand() if it else 1.0
+        if u < 0.3:
+            k, e = both[int(rand() * len(both))], "VAx"[int(rand() * 3)]
+            a = list(alts)
+            a[k] = full[k] if e == "x" else {e: full[k][e]}
+        elif u < 0.7:
+            name, d = names[int(rand() * len(names))], 6000.0 * (rand() - 0.5)
+            for k in free:
+                if phase[k] == name or (u >= 0.6 and phase[k][::2] == name[::2]):
+                    p[k] += d
+        elif it:
+            for _ in range(3):
+                p[free[int(rand() * len(free))]] += 5000.0 * (rand() - 0.5)
+        start, end, eng = _greedy(a, pred, succ, p)
+        span = max(end[k] + lat[k] for k in range(n))
+        if now is None or span <= now + 600.0 * rand() * (1.0 - it / its):
+            now, pri, alts = span, p, a
+            if best is None or span < best[0]:
+                best = (span, start, eng)
+    return best
+
+
+def _swaps(alts, pred, succ, lat, start, eng):
+    n, seed = len(alts), [1]
+    eng, prev, nxt = list(eng), [-1] * n, [-1] * n
+    for e in "VAPGS":
+        seq = sorted((k for k in range(n) if eng[k] == e), key=lambda k: (start[k], k))
+        for a, b in zip(seq, seq[1:]):
+            nxt[a], prev[b] = b, a
+    direct = [set(d for d, _, _ in p) for p in pred]
+
+    def rand():
+        seed[0] = (seed[0] * 1103515245 + 12345) % 2147483648
+        return seed[0] / 2147483648.0
+
+    def weights():
+        cost = [alts[k][eng[k]] for k in range(n)]
+        return (cost, [[(d, cost[d] + w + (HOP if raw or eng[d] != eng[k] else 0.0)) for d, raw, w in pred[k]] for k in range(n)],
+                [[(s, cost[k] + w + (HOP if raw or eng[s] != eng[k] else 0.0)) for s, raw, w in succ[k]] for k in range(n)])
+
+    def times():
+        left = [len(pred[k]) + (prev[k] >= 0) for k in range(n)]
+        r, q, order = [0.0] * n, [0.0] * n, [k for k in range(n) if not left[k]]
+        for k in order:
+            t = r[k]
+            for s, w in sw[k] + ([(nxt[k], cost[k])] if nxt[k] >= 0 else []):
+                if t + w > r[s]:
+                    r[s] = t + w
+                left[s] -= 1
+                if not left[s]:
+                    order.append(s)
+        if len(order) < n:
+            return None
+        for k in reversed(order):
+            b = cost[k] + max(lat[k], q[nxt[k]] if nxt[k] >= 0 else 0.0)
+            for s, w in sw[k]:
+                if w + q[s] > b:
+                    b = w + q[s]
+            q[k] = b
+        return r, q, order
+
+    def link(a, u, b):
+        prev[u], nxt[u] = a, b
+        if a >= 0:
+            nxt[a] = u
+        if b >= 0:
+            prev[b] = u
+    cost, pw, sw = weights()
+    best, barred, since = None, {}, 0
+    for it in range(1, CFG["swaps"] + 1):
+        r, q, order = times()
+        span, since = max(q), since + 1
+        if best is None or span < best[0] - 1e-6:
+            best, since = (span, r, list(eng), list(prev), list(nxt)), 0
+        if since > 3000:
+            eng[:], prev[:], nxt[:] = best[2:]
+            cost, pw, sw = weights()
+            since, barred = 0, {}
+            continue
+        moves = []
+        for u in order:
+            if r[u] + q[u] < span - 1e-3:
+                continue
+            v = nxt[u]
+            if v >= 0 and r[v] + q[v] > span - 1e-3 and abs(r[u] + cost[u] - r[v]) < 1e-3 and u not in direct[v]:
+                a, b = prev[u], nxt[v]
+                rv = max([r[a] + cost[a] if a >= 0 else 0.0] + [r[d] + w for d, w in pw[v]])
+                ru = max([rv + cost[v]] + [r[d] + w for d, w in pw[u]])
+                qu = max([cost[u] + max(lat[u], q[b] if b >= 0 else 0.0)] + [w + q[s] for s, w in sw[u]])
+                qv = max([cost[v] + qu] + [w + q[s] for s, w in sw[v]])
+                guess = max(rv + qv, ru + qu)
+                if barred.get((u, v), 0) < it or guess < best[0] - 1:
+                    moves.append((guess + 30 * rand(), u, v))
+            if len(alts[u]) > 1 and barred.get((u, -1), 0) < it:
+                e = [x for x in alts[u] if x != eng[u]][0]
+                t = max([r[d] + w for d, w in pw[u]] + [0.0])
+                seq = [k for k in order if eng[k] == e]
+                before = [k for k in seq if r[k] <= r[u] and (r[k] + cost[k] * 0.5 <= t or k in direct[u])]
+                a = before[-1] if before else -1
+                b, c = nxt[a] if before else seq[0], alts[u][e]
+                ru = max(t, r[a] + cost[a] if before else 0.0)
+                qu = max([c + lat[u], c + (q[b] if b >= 0 else 0.0)] + [w - cost[u] + c + q[s] for s, w in sw[u]])
+                moves.append((ru + qu + 200 + 30 * rand(), u, -1, e, a, b))
+        if not moves:
+            barred, since = {}, since + 50
+            continue
+        m = min(moves) if rand() > 0.03 else moves[int(rand() * len(moves))]
+        u, v = m[1:3]
+        if v >= 0:
+            a, b = prev[u], nxt[v]
+            link(a, v, u)
+            link(v, u, b)
+            barred[(v, u)] = it + 8 + int(14 * rand())
+            continue
+        was = (list(prev), list(nxt), eng[u])
+        if prev[u] >= 0:
+            nxt[prev[u]] = nxt[u]
+        if nxt[u] >= 0:
+            prev[nxt[u]] = prev[u]
+        link(m[4], u, m[5])
+        eng[u] = m[3]
+        cost, pw, sw = weights()
+        if times() is None:
+            prev[:], nxt[:], eng[u] = was
+            cost, pw, sw = weights()
+        barred[(u, -1)] = it + 40 + int(40 * rand())
+    return best[:3]
 
 
 def _schedule(ops):
     n = len(ops)
-    key = tuple(tuple(sorted(o["deps"].items())) for o in ops)
+    above, pred, succ = [0] * n, [], [[] for _ in range(n)]
+    lat = [o["lat"] for o in ops]
+    for k, o in enumerate(ops):
+        far = 0
+        for d in o["deps"]:
+            far |= above[d]
+        pred.append([(d, raw, lat[d]) for d, raw in sorted(o["deps"].items()) if not far >> d & 1])
+        above[k] = far | sum(1 << d for d, _, _ in pred[k])
+        for d, raw, _ in pred[k]:
+            succ[d].append((k, raw, lat[d]))
+    key = tuple(tuple(p) for p in pred)
     if key not in _ORDERS:
-        above, pred, succ = [0] * n, [], [[] for _ in range(n)]
-        lat = [o["lat"] for o in ops]
-        for k, o in enumerate(ops):
-            far = 0
-            for d in o["deps"]:
-                far |= above[d]
-            pred.append([(d, raw, lat[d]) for d, raw in o["deps"].items() if not far >> d & 1])
-            above[k] = far | sum(1 << d for d, _, _ in pred[k])
-            for d, raw, _ in pred[k]:
-                succ[d].append((k, raw, lat[d]))
-        alts = [[(e, c) for e, (_, c) in o["alts"].items()] for o in ops]
-        zero, prio = [0.0] * n, [o["prio"] for o in ops]
-        top, seed, its = None, [0], CFG["its"]
-
-        def rand():
-            seed[0] = (seed[0] * 1103515245 + 12345) % 2147483648
-            return seed[0] / 2147483648.0
-        for seed[0] in CFG["seeds"]:
-            best = keep = None
-            for it in range(CFG["gits"]):
-                pri = [o["at"] for o in ops] if keep is None else list(keep[1])
-                for _ in range(0 if keep is None else 4):
-                    pri[int(rand() * n)] += 6.0 * (rand() - 0.5)
-                start, end = _greedy(alts, pred, succ, pri)
-                span = max(end[k] + lat[k] for k in range(n))
-                if keep is None or span <= keep[0]:
-                    keep = (span, pri, start)
-            pri = list(keep[2])
-            for it in range(its):
-                for k in range(n):
-                    for d, _, _ in pred[k]:
-                        if pri[d] >= pri[k]:
-                            pri[k] = pri[d] + 1e-6
-                start, end, eng = _place(sorted(range(n), key=lambda k: pri[k]), alts, pred, zero)
-                span = max(end[k] + lat[k] for k in range(n))
-                if best is None or span <= best[0] + 100.0 * rand() * (1.0 - it / its):
-                    best = (span, start, end, eng)
-                    if top is None or span < top[0]:
-                        top = best
-                if it % 50 == 49:
-                    fixed = [[x for x in alts[k] if x[0] == best[3][k]] for k in range(n)]
-                    _, late, _ = _place(sorted(range(n), key=lambda k: (-best[2][k], -k)), fixed, succ, prio)
-                    pri = [-x for x in late]
-                else:
-                    pri, moved = list(best[1]), []
-                    for _ in range(1 + int(3 * rand())):
-                        k = int(rand() * n)
-                        pri[k] += 6000.0 * (rand() - 0.5) * rand()
-                        moved.append(k)
-                    if rand() < 0.5:
-                        for k in range(max(moved), -1, -1):
-                            for d, _, _ in pred[k]:
-                                if pri[d] >= pri[k]:
-                                    pri[d] = pri[k] - 1e-3
-        _, start, end, eng = top
-        _ORDERS[key] = (eng, {e: sorted((k for k in range(n) if eng[k] == e), key=lambda k: (start[k], k)) for e in "VAPGSX"}, top[0])
+        full = [{e: c for e, (_, c) in o["alts"].items()} for o in ops]
+        alts = [a if len(a) == 1 or o["grp"] in ("first", "land") or o["rnd"] + o["fit"] == RO else {"A": a["A"]} for a, o in zip(full, ops)]
+        way = [0.0] * n
+        for k in range(n - 1, -1, -1):
+            way[k] = min(alts[k].values()) + lat[k] + max([way[s] + HOP for s, _, _ in succ[k]] + [0.0])
+        pri, top = [-way[k] - ops[k]["prio"] for k in range(n)], None
+        for _ in range(CFG["passes"]):
+            start, end, eng = _greedy(alts, pred, succ, pri)
+            span = max(end[k] + lat[k] for k in range(n))
+            if top is None or span < top[0]:
+                top = (span, start, eng)
+            _, late, _ = _greedy([{eng[k]: alts[k][eng[k]]} for k in range(n)], succ, pred, [-end[k] - lat[k] for k in range(n)])
+            pri = [-late[k] - ops[k]["prio"] for k in range(n)]
+        top = _shifts(ops, full, alts, pred, succ, lat, [top[1][k] - (o["prio"] if o["grp"] == "first" else 0.0) for k, o in enumerate(ops)])
+        span, start, eng = _swaps(full, pred, succ, lat, top[1], top[2])
+        _ORDERS[key] = (eng, {e: sorted((k for k in range(n) if eng[k] == e), key=lambda k: (start[k], k)) for e in "VAPGSX"}, span)
     return _ORDERS[key]
 
 
@@ -255,8 +341,6 @@ def _emit(ops, queues, T):
             ins = ops[k]["alts"][e][0](q)
             if k in marked:
                 ins.then_inc(T.sem["e" + e], 1)
-            elif ops[k]["dma"]:
-                ins.then_inc(T.sem[ops[k]["sem"][0]], 16)
     waited = set(d for w in waits for kind, d in w if kind == "sem")
     return [ops[k]["sem"] for k in range(n) if ops[k]["dma"] and k not in waited]
 
@@ -268,10 +352,10 @@ def rank_program(g, core, T, topo):
         _relay_program(g, core, T, topo, plan)
         return
     A, F = AluOpType, ActivationFunctionType
-    ops, log, ndma, sent, at = [], {}, [0], [0], [-100.0]
+    ops, log, ndma, sent, ahead = [], {}, [0], [0], [1e5, 0, "first", -1]
     far = [d for d in range(N) if (me, d) in plan]
     near = [d for d in range(N) if d != me and d not in far]
-    dests = far + near + [me]
+    sources = [me] + near + far
 
     def op(alts, reads, writes, lat=0.0, prio=0.0, sem=None, dma=False):
         k, deps = len(ops), {}
@@ -287,34 +371,26 @@ def rank_program(g, core, T, topo):
                 if w:
                     old[:] = [x for x in old if not (lo <= x[1] and x[2] <= hi)]
                 old.append((k, lo, hi, w))
-        ops.append({"alts": alts, "deps": deps, "lat": lat, "prio": prio, "sem": sem, "dma": dma, "at": at[0] + 1e-4 * k})
+        ops.append({"alts": alts, "deps": deps, "lat": lat, "prio": prio + ahead[0], "fit": ahead[1], "grp": ahead[2], "rnd": ahead[3], "name": str(writes[-1:]), "sem": sem, "dma": dma})
 
     def vc(n, f=1.0):
         return 60.0 + max(64.0, n * f) * CYC
 
-    def tt(out, a, b, o, n, reads, writes, f=2.0):
+    def tt(out, a, b, o, n, reads, writes, f=1.0):
         op({"V": (lambda q: q.tensor_tensor(out, a, b, o), vc(n, f))}, reads, writes)
 
-    def ts(out, a, s1, s2, o0, o1, n, reads, writes, f=1.0):
+    def ts(out, a, s1, s2, o0, o1, n, reads, writes, prio=0.0):
         if o1 is None:
-            op({"V": (lambda q: q.tensor_scalar(out, a, s1, None, o0), vc(n, f))}, reads, writes)
+            op({"V": (lambda q: q.tensor_scalar(out, a, s1, None, o0), vc(n))}, reads, writes, prio=prio)
         else:
-            op({"V": (lambda q: q.tensor_scalar(out, a, s1, s2, o0, o1), vc(n, f))}, reads, writes)
+            op({"V": (lambda q: q.tensor_scalar(out, a, s1, s2, o0, o1), vc(n))}, reads, writes, prio=prio)
 
-    def cp(out, a, n, reads, writes):
-        op({"V": (lambda q: q.tensor_copy(out, a), vc(n))}, reads, writes)
+    def cp(out, a, n, reads, writes, f=1.0, on="V", prio=0.0):
+        alts = {"V": (lambda q: q.tensor_copy(out, a), vc(n, f)), "A": (lambda q: q.activation(out, a, F.Copy), vc(n, f))}
+        op({e: alts[e] for e in on}, reads, writes, prio=prio)
 
-    def lin(out, a, scale, col, n, reads, writes, f=1.0, on="A"):
-        bias = T.cc[:, col:col + 1]
-        alts = {"V": (lambda q: q.tensor_scalar(out, a, scale, bias, A.mult, A.add), vc(n, f)),
-                "A": (lambda q: q.activation(out, a, F.Identity, bias=bias, scale=scale), vc(n, f))}
-        op({e: alts[e] for e in on}, reads + ["cc"], writes)
-
-    def act(out, a, func, n, reads, writes, scale=None, col=None):
-        if col is None:
-            op({"A": (lambda q: q.activation(out, a, func), vc(n))}, reads, writes)
-        else:
-            op({"A": (lambda q: q.activation(out, a, func, bias=T.cc[:, col:col + 1], scale=scale), vc(n))}, reads + ["cc"], writes)
+    def act(out, a, func, n, reads, writes, scale=1.0):
+        op({"A": (lambda q: q.activation(out, a, func, scale=scale), vc(n))}, reads, writes)
 
     def fill(ap, val, n, writes):
         op({"V": (lambda q: q.memset(ap, val), vc(n))}, [], writes)
@@ -325,19 +401,22 @@ def rank_program(g, core, T, topo):
             for (o, l, r, st, sp, _) in group:
                 ins = q.matmul(o, l, r, st, sp)
             return ins
-        op({"P": (run, 60.0 + sum(max(64, x[5]) for x in group) * PEC)}, reads, ["ps%d" % bank])
+        op({"P": (run, CFG["pfix"] + sum(max(64, x[5]) for x in group) * PEC)}, reads, ["ps%d" % bank])
 
-    def dma(e, out, src, reads, writes, prio=0.0, lat=T_DMA):
+    def dma(e, moves, reads, writes, prio=0.0, lat=T_DMA):
         name = "d%d" % ndma[0]
         ndma[0] += 1
-        op({e: (lambda q: q.dma_start(out, src), 900.0 if e == "G" else 150.0)}, reads, writes, lat=lat, prio=prio,
-           sem=(name, 16), dma=True)
 
-    def iota(out, pattern, base, mult, n, writes, flag=True, prio=0.0):
-        if flag:
-            fn = lambda q: q.iota(out, pattern, base, mult, allow_small_or_imprecise_dtypes=True)
-        else:
+        def run(q):
+            for out, src in moves:
+                q.dma_start(out, src).then_inc(T.sem[name], 16)
+        op({e: (run, 100.0 * len(moves))}, reads, writes, lat=lat, prio=prio, sem=(name, 16 * len(moves)), dma=True)
+
+    def iota(out, pattern, base, mult, n, writes, prio=0.0):
+        if "pc" in writes:
             fn = lambda q: q.iota(out, pattern, base, mult)
+        else:
+            fn = lambda q: q.iota(out, pattern, base, mult, allow_small_or_imprecise_dtypes=True)
         op({"G": (fn, 130.0 + 2 * n * CYC)}, [], writes, prio=prio)
 
     def arrives(name, val, t, reads, writes):
@@ -347,387 +426,406 @@ def rank_program(g, core, T, topo):
         return T["ps%d" % k]
 
     top = 2e5
-    dma("S", T.sx[:], T.fx[:], [], ["sx"], prio=top + 200)
-    dma("A", T.sc[:], T.cl[:], [], ["sc"], prio=top + 200)
-    dma("S", T.sh[:], T.hv[:], [], ["sh"], prio=top + 100)
-    dma("A", T.sl[:], T.hl[:], [], ["sl"], prio=top)
-    dma("S", T.st[:], T.th[:], [], ["st"], prio=top)
-    iota(T.pc[:, 0:1], [[0, 1]], 0, 1, 1, ["call", "pc"], flag=False, prio=top)
-    iota(T.cx[:], [[1, 176]], 0, 0, 176, ["call", "cx"], prio=top)
-    iota(T.cx2[:], [[64, 2], [0, 4], [1, 16]], 0, 0, 128, ["call", "cx2"], prio=top)
+    dma("S", [(T.sx[:], T.fx[:])], [], ["sx"], prio=top + 200)
+    dma("A", [(T.li[:, d, 0:120], T.cl[32 * d:32 * d + 32, :]) for d in range(N)], [], [("li", 0, 1)], prio=top + 200)
+    dma("S", [(T.li[:, d, 120:240], T.hl[32 * d:32 * d + 32, :]) for d in range(N)], [], [("li", 1, 2)], prio=top + 150)
+    dma("S", [(T.sh[:], T.hv[:])], [], ["sh"], prio=top + 100)
+    ts(T.sf[:, :, 0:120], T.li[:, :, 0:120], -NT / 2.0, None, A.add, None, 480, [("li", 0, 1)], [("sc", 0, 1)], prio=top)
+    cp(T.sf[:, :, 120:240], T.li[:, :, 120:240], 480, [("li", 1, 2)], [("sc", 1, 2)], prio=top)
+    dma("A", [(T.ti[:, 16 * d:16 * d + 15], T.th[2 * d:2 * d + 2, :]) for d in range(N)], ["ti"], ["tl"], prio=top)
+    iota(T.pc[:, 0:1], [[0, 1]], 0, 1, 1, ["call", "pc"], prio=top)
+    iota(T.cx[:], [[1, 48]], 0, 0, 48, ["call", "cx"], prio=top)
+
+    def select(name, out, pattern, base=0, mult=1, test=A.is_equal, own=False):
+        n = 1
+        for _, count in pattern:
+            n *= count
+        src = out if own else T.one[:, 0:n]
+        op({"G": (lambda q: q.affine_select(out, src, pattern, test, 0.0, base, mult), 170.0 + 2 * n * CYC)}, ["one", name], ["call", name])
+
+    def within(name, out, pattern, size):
+        select(name, out, pattern, 0, 1, A.is_ge)
+        select(name, out, [[-s, c] for s, c in pattern], size - 1, -1, A.is_ge, True)
+    for name, val, n in (("one", 1.0, 512), ("mf", 0.0, 1920), ("mh", 0.0, 960), ("mx", 0.0, 272), ("ml", 0.0, 384), ("mcb", 0.0, 144),
+                         ("mt", 0.0, 288), ("mg", 0.0, 1088), ("thw", 0.0, NT), ("me", 0.0, 136), ("md", 0.0, 272), ("mcf", 0.0, 144),
+                         ("mbc", -MARK, 2048), ("mw", 1.0, 1024)):
+        fill(T[name][:], val, n / 2, ["thz" if name == "thw" else name])
+    select("mr", T.mr[:], [[-1, 4], [0, 8], [-4, 16]])
+    select("mf", T.mf[:, :, 112:128], [[-64, 2], [-1, 4], [-4, 16]])
+    for m in range(2):
+        select("mh", T.mh[:, :, 112 + 64 * m:128 + 64 * m], [[-64, 2], [-1, 2], [-4, 16]], -2 * m)
+    select("mi1", T.mi1[:], [[-1, 128]])
+    for d in range(N):
+        a, b = 16 * d, 16 * d + 15
+        cp(T.tb[:, a:b], T.ti[:, a:b], 15, ["tl"], [("tb", a, b)], prio=top)
+        op({"V": (lambda q, a=a, b=b: q.tensor_tensor(T.tb[:, 64 + a:64 + b], T.ti[:, a:b], T.tb[:, a:b], A.subtract), vc(15))},
+           ["tl", ("tb", a, b)], [("tb", 64 + a, 64 + b)], prio=top)
     lanes = _lanes(T, topo, plan, me)
-    for pieces in ("xc", "h", "l", "t"):
+    for pieces in ("x", "c", "h", "tu"):
         tr = []
         for piece in pieces:
             for d in far + near:
-                if d in near:
-                    c, land, rsem = T.cores[d], _slot(T, piece, me), T.sem["a%s%d" % ("l" if piece == "t" else piece, me)]
+                if piece in "tu":
+                    src = T.tb[:, 64 * (piece == "u") + 16 * d:64 * (piece == "u") + 16 * d + 15]
                 else:
-                    c = plan[(me, d)][piece in "clt"]
-                    land = T["r" + piece][:] if piece in "xhc" else _slot(T, piece, me)
-                    rsem = T.sem.rin1 if piece in "xc" else T.sem.rin2
+                    src = T.sf[:, d, :] if piece == "c" else T["s" + piece][d]
+                if d in near:
+                    c, land, rsem = T.cores[d], _slot(T, piece, me), T.sem["a%s%d" % (pieces[0], me)]
+                else:
+                    c = plan[(me, d)][piece in "ch"]
+                    land = T.rt[int(piece == "u")] if piece in "tu" else T["r" + piece][:]
+                    rsem = T.sem["rin%d" % (1 if piece in "xc" else 2)]
                 rid, pid = topo.addr(c, core)
                 tr.append(RemoteDMATransfer(dst_ids=[DstId(rid=rid, pnc=pid)], dma_engine_mask=_mask(lanes[piece, d]),
-                                            remote_sem=rsem, src=T["s" + piece][d], dst=land))
+                                            remote_sem=rsem, src=src, dst=land))
                 sent[0] += len(lanes[piece, d])
-        op({"G": (lambda q, tr=tr: q.remote_dma_fused(tr, local_sem=T.sem.sent), 1000.0)}, ["s" + x for x in pieces], ["call"],
-           prio=top)
+        op({"G": (lambda q, tr=tr: q.remote_dma_fused(tr, local_sem=T.sem.sent), 1000.0)},
+           ["tb"] if pieces == "tu" else ["s" + x for x in pieces], ["call"], prio=top)
     rows = slice(32 * me, 32 * me + 32)
-    for piece, src in (("x", T.fx[rows, :]), ("c", T.cl[rows, :]), ("h", T.hv[rows, :]), ("l", T.hl[rows, :]),
-                       ("t", T.th[2 * me:2 * me + 2, :])):
-        dma("S", _slot(T, piece, me), src, ["st"], [("L" + piece, me, me + 1)])
+    for piece, src in (("x", T.fx[rows, :]), ("h", T.hv[rows, :])):
+        dma("S", [(_slot(T, piece, me), src)], ["sh"], [("L" + piece, me, me + 1)])
+    dma("S", [(_slot(T, "tu"[b], me), T.tb[:, 64 * b + 16 * me:64 * b + 16 * me + 15]) for b in range(2)], ["tb"], [("Lt", me, me + 1)])
     for s in near + far:
         theirs = _lanes(T, topo, plan, s)
-        for piece, late in (("x", 0.0), ("c", 0.0), ("h", 1000.0), ("l", 2500.0)):
+        for piece, late in (("x", 0.0), ("c", 1000.0), ("h", 2000.0), ("t", 3000.0)):
             if s in near:
-                n_in = len(theirs[piece, me]) + (len(theirs["t", me]) if piece == "l" else 0)
+                n_in = len(theirs[piece, me]) + (len(theirs["u", me]) if piece == "t" else 0)
             else:
-                n_in = len(topo.engines(plan[(s, me)][piece in "cl"], core))
-            arrives("a%s%d" % (piece, s), n_in, (T_NEAR if s in near else T_FAR) + late, [],
-                    [("L" + x, s, s + 1) for x in ("lt" if piece == "l" else piece)])
-    sources = [me] + near + far
-    iota(T.cx3[:], [[64, 2], [0, 8], [1, 8]], 0, 0, 128, ["call", "cx3"])
-    iota(T.si0[:], [[960, 4], [0, 2], [16, 60]], PAD + int(OFF), 1, 480, ["call", "si0"])
-    iota(T.ki[:], [[0, 4], [768, 2], [0, 60]], BLK + int(OFF), 0, 480, ["call", "ki"])
-    for r in dests:
-        iota(T.iot[:, r * V:(r + 1) * V], [[1, V]], r * V + 16384, 0, V, ["call", ("iot", r, r + 1)])
-
-    CZ, CM, CN, CFL, CB, CR, CS, CL, CH, CK, CF = range(11)
-    for col, val in ((CZ, 0.0), (CM, BIG + 1), (CN, -BIG), (CFL, BIG - 0.5), (CB, 16384.0), (CR, float(BLK)), (CS, -OFF),
-                     (CL, -10.5 * K), (CH, 0.5), (CK, -K), (CF, -OFF - 8192.0)):
-        fill(T.cc[:, col:col + 1], val, 1, [("cc", col, col + 1)])
-    p = T.pc[:, 0:1]
-    PF64, PI, PG16, PI4, PA, PI8, PU, PJ, PP = range(9)
-    for col, sh, m in ((PF64, 0, 64), (PI, 0, 15), (PG16, 0, 112), (PI4, 2, 15), (PA, 0, 3), (PI8, 0, 7), (PU, 0, 1), (PJ, 1, 7)):
-        ts(T.pi[:, col:col + 1], p, sh, m, A.arith_shift_right, A.bitwise_and, 1, ["pc"], [("pi", col, col + 1)])
-    cp(T.pf[:, 0:8], T.pi[:], 8, ["pi"], [("pf", 0, 8)])
-    cp(T.pf[:, PP:PP + 1], p, 1, ["pc"], [("pf", PP, PP + 1)])
-
-    def pf(c):
-        return T.pf[:, c:c + 1]
-
-    def tg(c):
-        return T.tg[:, c:c + 1]
-    GCB, GON, GE, GO8, GF, GP, GG, GT = range(8)
-    for col, src, s1, s2, o0, o1, rd in (
-            (GF, pf(PI4), pf(PF64), None, A.add, None, []), (GCB, pf(PG16), 15.0, None, A.add, None, []),
-            (GON, pf(PI), pf(PF64), None, A.add, None, []), (GE, pf(PI), 4.0, pf(PF64), A.mult, A.add, []),
-            (GO8, pf(PI8), pf(PF64), None, A.add, None, []), (GP, pf(PA), 16.0, tg(GF), A.mult, A.add, [("tg", GF, GF + 1)]),
-            (GG, pf(PU), 8.0, pf(PG16), A.add, A.add, []), (GT, tg(GE), 3.0, None, A.add, None, [("tg", GE, GE + 1)])):
-        ts(tg(col), src, s1, s2, o0, o1, 1, ["pf"] + rd, [("tg", col, col + 1)])
-    ts(T.tf0[:], T.cx[:, 0:4], pf(PA), 1000.0, A.not_equal, A.mult, 4, ["cx", "pf"], ["tf0"])
-    ts(T.tf[:], T.tf0[:], tg(GF), None, A.add, None, 4, ["tf0", ("tg", GF, GF + 1)], ["tf"])
-    ts(T.tf48[:], T.tf0[:], tg(GF), 48.0, A.add, A.add, 4, ["tf0", ("tg", GF, GF + 1)], ["tf48"])
-    ts(T.tj0[:], T.cx[:, 0:8], pf(PJ), 1000.0, A.not_equal, A.mult, 8, ["cx", "pf"], ["tj0"])
-    ts(T.tj[:], T.tj0[:], tg(GG), None, A.add, None, 8, ["tj0", ("tg", GG, GG + 1)], ["tj"])
-
-    def pick(out, cols, target, weight, n, reads, writes):
-        ts(out, cols, target, weight, A.is_equal, A.mult, n, reads, writes)
+                n_in = len(topo.engines(plan[(s, me)][piece in "ch"], core))
+            arrives("a%s%d" % (piece, s), n_in, (T_NEAR if s in near else T_FAR) + late, [], [("L" + piece, s, s + 1)])
     for a in range(4):
-        pick(T.mr[:, a * 128:(a + 1) * 128], T.cx2[:], T.tf[:, a:a + 1], 1.0, 128, ["cx2", "tf"], [("mr", a, a + 1)])
-        pick(T.mf[:, a * 176:(a + 1) * 176], T.cx[:], T.tf48[:, a:a + 1], 1.0, 176, ["cx", "tf48"], [("mf", a, a + 1)])
-    for name, cols, n, target, w in (("mcb", "cx", 144, tg(GCB), 1.0), ("mi1", "cx", 128, pf(PP), 1.0), ("mon", "cx2", 128, tg(GON), 1.0),
-                                     ("mo8", "cx3", 128, tg(GO8), 1.0), ("me", "cx", 132, tg(GT), 0.125), ("mp", "cx", 128, tg(GP), 1.0)):
-        pick(T[name][:], T[cols][:, 0:n], target, w, n, [cols, "tg", "pf"], [name])
-    for jj in range(8):
-        pick(T.mg[:, jj * 136:(jj + 1) * 136], T.cx[:, 0:136], T.tj[:, jj:jj + 1], K, 136, ["cx", "tj"], [("mg", jj, jj + 1)])
-    for name, src, w in (("mck", "mcb", 4096.0), ("mch", "mcb", 16384.0), ("mni", "mi1", -1.0), ("mn2", "mi1", -2.0),
-                         ("mnb", "mi1", -BIG), ("mi4", "mi1", 4096.0), ("mi8", "mi1", 8.0), ("msum", "mon", 0.125), ("monk", "mon", K / 2)):
-        lin(T[name][:], T[src][:], w, CZ, 128, [src], [name])
-    tt(T.monp[:], T.mon[:], T.mi8[:], A.add, 128, ["mon", "mi8"], ["monp"])
-    tt(T.mo8p[:], T.mo8[:], T.mi8[:], A.add, 128, ["mo8", "mi8"], ["mo8p"])
-    fill(T.mz[:], 0.0, 240, ["mz"])
-    fill(T.fl[:], 1.0, 240, ["fl"])
-    for b in range(RO):
-        fill(T.win[:, b * BLK:b * BLK + PAD], BIG + 1153.0, 16, [("win", b * BLK, b * BLK + PAD)])
-    for hh in range(4):
-        fill(T.thw[:, hh * V:(hh + 1) * V], 0.0, V // 2, [("thz", hh, hh + 1)])
+        select("mx", T.mx[:, :, 4 + a:132:8], [[-64, 2], [-4, 16]], -a)
+    select("ml", T.ml[:, :, 64:128], [[-64, 2], [-1, 4], [-4, 16]])
+    within("mcb", T.mcb[:, 15:143:16], [[-16, 8]], 16)
+    within("mt", T.mt[:, :, 15:143:16], [[-2, 2], [-16, 8]], 2)
+    for u in range(2):
+        select("mg", T.mg[:, :, 8 + u:136:16], [[-2, 8], [-16, 8]], -u)
+    for r in range(N):
+        iota(T.iot[:, r * V:(r + 1) * V], [[1, V]], r * V - NT // 2, 0, V, ["call", ("iot", r, r + 1)])
+    select("mbc", T.mbc[:], [[-1, 16], [-16, 8], [0, 16]], own=True)
+    select("mw", T.mw[:], [[-1, 8], [0, 8], [-8, 16]], own=True)
+    select("md", T.md[:, :, 1:129:2], [[-4, 2], [-8, 16], [-1, 4]])
+    select("mal", T.mal[:], [[-1, 2], [0, 8], [1, 16]], mult=-2)
+    within("mcf", T.mcf[:, 15:143:16], [[-16, 4], [-64, 2]], 16)
+
+    p = T.pc[:, 0:1]
+    for col, sh, m in ((0, 0, 15), (1, 1, 7)):
+        ts(T.pi[:, col:col + 1], p, sh, m, A.arith_shift_right, A.bitwise_and, 1, ["pc"], [("pi", col, col + 1)])
+    cp(T.pf[:, 0:2], T.pi[:], 2, ["pi"], [("pf", 0, 2)])
+    ts(T.pf[:, 2:3], T.pf[:, 1:2], float(C), T.pf[:, 1:2], A.is_lt, A.mult, 1, [("pf", 0, 2)], [("pf", 2, 3)])
+    ts(T.pf[:, 3:4], T.pf[:, 2:3], float(H), None, A.mult, None, 1, [("pf", 2, 3)], [("pf", 3, 4)])
+    ts(T.me[:, 7:135:8], T.cx[:, 0:16], T.pf[:, 0:1], -0.125, A.is_equal, A.mult, 16, ["cx", ("pf", 0, 2), "me"], ["me"])
+    ts(T.hc[:], T.cx[:], 16.0, T.pf[:, 0:1], A.mult, A.add, 48, ["cx", ("pf", 0, 2)], ["hc"])
+    fill(T.low[:, 0:1], -2047.5, 1, [("low", 0, 1)])
+    fill(T.low[:, 1:2], 192.0 * STEP - 0.5, 1, [("low", 1, 2)])
+    for name, src, w in (("mck", "mcb", 4096.0), ("mni", "mi1", -1.0), ("mnb", "mi1", 8192.0), ("mhf", "mi1", 0.5), ("mcp", "mcb", T.pf[:, 3:4]),
+                         ("md7", "md", 7.0), ("md6", "md", -6.0), ("mcf", "mcf", -1.0 / 64)):
+        act(T[name][:], T[src][:], F.Identity, 272 if src == "md" else 144, [src, "pf"], [name], scale=w)
+    for c in range(1, C):
+        act(T.mnc[:, 128 * c - 128:128 * c], T.mi1[:], F.Identity, 128, ["mi1"], [("mnc", c, c + 1)], scale=float(H * c))
+    for name, part in (("ck0", NT / 256.0), ("cc1", -7.0 / 2048)):
+        fill(T[name][:], part, 64, [name])
+    ahead[0] = CFG["lag"]
+    for f in range(2):
+        dma("S", [(T.thw[16 * k + 2 * f:16 * k + 2 * f + 2, :], T.lt[:, 64 * f:64 * f + 64, :]) for k in range(8)], ["Lt", "thz"],
+            [("thw", f, f + 1)], lat=3000.0)
+
+    def lists(s, a, b):
+        return (T.sf if s == me else T.lf)[:, s, a:b]
+
+    def listed(s):
+        return "sc" if s == me else ("Lc", s, s + 1)
 
     def cb(j, name="mcb"):
         return T[name][:, 15 - j:143 - j]
 
-    def parts(s, c0, c1, names, tag):
-        a, b, rd = s * IB + c0, s * IB + c1, [("L" + x, s, s + 1) for x in names]
-        cp(T.lh[:, a:b], T.li[:, a:b], c1 - c0, rd, [("lh" + tag, s, s + 1)])
-        tt(T.ll[:, a:b], T.li[:, a:b], T.lh[:, a:b], A.subtract, c1 - c0, rd + [("lh" + tag, s, s + 1)], [("ll" + tag, s, s + 1)])
+    def fit(f):
+        def B(name):
+            return T[name + "AB"[f]]
 
-    x0 = (RO - 1) * BLK + PAD
-    mm([(ps(6)[:, 0:480], T.mz[:, 0:128], T.mz[:, 0:480], True, False, 480)], ["mz"], 6)
-    for k, s in enumerate(sources):
-        lastsrc = k == N - 1
-        parts(s, 0, 120, "c", "c")
-        for hh in range(2):
-            mm([(ps(hh)[:, 240 * b:240 * b + 240], T.mr[:, (2 * hh + b) * 128:(2 * hh + b + 1) * 128],
-                 _slot(T, "x", s), True, True, 240) for b in range(2)], ["mr", ("Lx", s, s + 1)], hh)
-            c0 = x0 + s * V + 480 * hh
-            lin(T.win[:, c0:c0 + 480], ps(hh)[:, 0:480], 1.0, CM, 480, ["ps%d" % hh], [("win", c0, c0 + 480)], on="VA")
-        ws = [T.mf[:, a * 176 + 48 - 16 * s:a * 176 + 176 - 16 * s] for a in range(4)]
-        mm([(ps(6)[:, 120 * a:120 * a + 120], ws[a], src[:, s * IB:s * IB + 120], False, lastsrc and a == 3 and b == 1, 120)
-            for a in range(4) for b, src in enumerate((T.lh, T.ll))], ["mf", ("lhc", s, s + 1), ("llc", s, s + 1)], 6)
-        for a in range(4):
-            mm([(ps(2 + a)[:, 0:384], ws[a], _slot(T, "h", s), k == 0, lastsrc, 384)], ["mf", ("Lh", s, s + 1)], 2 + a)
-    cp(T.cu[:], ps(6)[:, 0:480], 480, ["ps6"], ["cu"])
-    for a in range(4):
-        c0 = H0 + 384 * a
-        lin(T.win[:, c0:c0 + 384], ps(2 + a)[:, 0:384], 1.0, CM, 384, ["ps%d" % (2 + a)], [("win", c0, c0 + 384)], on="VA")
-    lin(T.clf[:], ps(6)[:, 0:480], 1.0, CB, 480, ["ps6"], ["clf"])
-    lin(T.chi[:], T.clf[:], 1.0, CZ, 480, ["clf"], ["chi"])
-    tt(T.clo[:], T.clf[:], T.chi[:], A.subtract, 480, ["clf", "chi"], ["clo"])
-    at[0] = -1.0
-    for s in sources:
-        parts(s, 120, 255, "lt", "l")
-        for b, name in enumerate(("lh", "ll")):
-            dma("S", T.lth[b, s], T[name][:, s * IB + 240:s * IB + 255], [(name + "l", s, s + 1)], [("lth", 4 * b + s, 4 * b + s + 1)],
-                lat=3000.0)
-        mm([(ps(7)[:, 120 * s:120 * s + 120], T.mp[:], src[:, s * IB + 120:s * IB + 240], b == 0, b == 1, 120)
-            for b, src in enumerate((T.lh, T.ll))], ["mp", ("lhl", s, s + 1), ("lll", s, s + 1)], 7)
-    for k in range(16):
-        b, gq = k // 8, k % 8
-        dma("S" if k % 3 else "G", T.thw[16 * gq + b:16 * gq + b + 1, :], T.lth[b, :, 64 * (gq // 4):64 * (gq // 4) + 64, :],
-            [("lth", 4 * b, 4 * b + 4), "thz"], [("thw", k, k + 1)])
-    at[0] = 2.0
-    cp(T.hli[:], ps(7)[:, 0:480], 480, ["ps7"], ["hli"])
-    tt(T.hp0[:], ps(7)[:, 0:480], T.ki[:], A.add, 480, ["ps7", "ki"], ["hp0"], f=1.0)
-    at[0] = 6.0
-    ts(T.hls[:], T.hli[:], 1, None, A.arith_shift_right, None, 480, ["hli"], ["hls"])
-    cp(T.hw[:], T.hls[:], 480, ["hls"], ["hw"])
-    ts(T.sfp[:], T.si0[:], pf(PG16), None, A.subtract, None, 480, ["si0", "pf"], ["sfp"])
-    lin(T.shi[:], T.sfp[:], 1.0, CZ, 480, ["sfp"], ["shi"])
-    tt(T.slo[:], T.sfp[:], T.shi[:], A.subtract, 480, ["sfp", "shi"], ["slo"])
-    lin(T.hp1[:], T.hp0[:], 1.0, CR, 480, ["hp0"], ["hp1"])
-    lin(T.hp2[:], T.hp1[:], 1.0, CR, 480, ["hp1"], ["hp2"])
+        def R(name, lo=0, hi=1 << 30):
+            return (name + "AB"[f], lo, hi)
+        KE, TR, R0 = f, 2 + f, 4 + 2 * f
+        turn = [0, 0, 0]
 
-    def spread(srcs, m, reads, own=True):
-        grp = []
-        for jj in range(8):
-            for c in range(C):
-                for b, src in enumerate(srcs):
-                    grp.append((ps(5)[:, jj:384:8], T.mg[:, jj * 136 + 8 - 2 * c:jj * 136 + 136 - 2 * c],
-                                src[:, c, 48 * m:48 * m + 48], own and c == 0 and b == 0,
-                                (own or jj == 7) and c == C - 1 and b == len(srcs) - 1, 48))
-        for j in range(0, len(grp), 20):
-            mm(grp[j:j + 20], ["mg"] + reads, 5)
+        def phase(name):
+            ahead[2] = name
+        phase("land")
 
-    at[0] = 3.0
-    for m in range(2):
-        a, b = 384 * m, 384 * m + 384
-        spread([T.chi, T.clo], m, ["chi", "clo"])
-        lin(T.idw[:, a:b], ps(5)[:, 0:384], 1.0 / K, CZ, 384, ["ps5"], [("idw", m, m + 1)])
-        lin(T.ihi[:, a:b], T.idw[:, a:b], 1.0, CZ, 384, [("idw", m, m + 1)], [("ihi", m, m + 1)])
-        tt(T.ilo[:, a:b], T.idw[:, a:b], T.ihi[:, a:b], A.subtract, 384, [("idw", m, m + 1), ("ihi", m, m + 1)], [("ilo", m, m + 1)])
-    for m in range(2):
-        u0, u1 = 48 * m, 48 * m + 48
-        at[0] = (1.0, 13.0)[m]
-        for c in range(C):
-            a = 3840 * m + 768 * c
-            lin(T.g5[:, a:a + 768], T.thw[:].indirect(T.cu[:, 96 * c + u0:96 * c + u1]), 1.0, CZ, 768,
-                ["thw", "thz", "cu"], [("g5", a, a + 768)], f=GATH, on="VA" if c >= 2 else "A")
-        mm([(ps(6)[:, 0:240], cb(j), T.g5[:, 3840 * m + j:3840 * m + 3840:16], j == 0, j == 15, 240) for j in range(16)],
-           ["mcb", "g5" if m else ("g5", 0, 3840)], 6)
-        lin(T.thc[:, :, u0:u1], ps(6)[:, 0:240], 1.0, CZ, 240, ["ps6"], [("thc", u0, u1)])
-        lin(T.thi[:, :, u0:u1], T.thc[:, :, u0:u1], 1.0, CZ, 240, [("thc", u0, u1)], [("thi", u0, u1)])
-        tt(T.tlo[:, :, u0:u1], T.thc[:, :, u0:u1], T.thi[:, :, u0:u1], A.subtract, 240,
-           [("thc", u0, u1), ("thi", u0, u1)], [("tlo", u0, u1)])
+        def rot():
+            turn[0] += 1
+            return (KE, TR)[turn[0] % 2]
 
-    def sums(bank, col, name, o, wc, stop):
-        step, hc = -(-64 // wc), 16 * wc
-        for c in range(0, C, step):
-            d = min(C, c + step)
-            mm([(ps(bank)[:, col + c * wc:col + d * wc], cb(j, name), T.ab[:, o + c * hc + j:o + d * hc:16], False,
-                 stop and d == C and j == 15, (d - c) * wc) for j in range(16)], [name, ("ab", o + c * hc, o + d * hc)], bank)
+        def place(a, q, m):
+            c0 = 112 - 64 * m - 16 * q
+            return T.mf[:, 4 * f + a, c0:c0 + 128]
 
-    diff = [0]
+        def const(out, name, n, start):
+            return (out, T[name][:], T.one[:, 0:n], start, False, n)
 
-    def apart(o, hc, h0, name):
-        for a in range(0, 5 * hc, 512):
-            b = min(a + 512, 5 * hc)
-            bank = diff[0] % 3
-            diff[0] += 1
-            grp, u = [], a
-            while u < b:
-                v = min(b, (u // hc + 1) * hc)
-                grp.append((ps(bank)[:, u - a:v - a], T.mi1[:], T.dd[:, o + u:o + v], True, False, v - u))
-                grp.append((ps(bank)[:, u - a:v - a], T.mni[:], T[name][:, h0 + u % hc:h0 + u % hc + v - u], False, True, v - u))
-                u = v
-            mm(grp, ["mi1", "mni", ("dd", o + a, o + b), (name, h0, h0 + hc)], bank)
-            act(T.ab[:, o + a:o + b], ps(bank)[:, 0:b - a], F.Abs, b - a, ["ps%d" % bank], [("ab", o + a, o + b)])
-
-    at[0] = -2.0
-    lin(T.hb[:], T.win[:, H0:H0 + 384], 1.0, CN, 384, [("win", H0, H0 + 384)], ["hb"])
-    for rnd in range(RO):
-        blk = (RO - 1 - rnd) * BLK
-        xs = blk + PAD
-        xw, xr = T.win[:, xs:xs + NT], ("win", xs, xs + NT)
-        whole, wholer = T.win[:, blk:H0 + HQ], ("win", blk, H0 + HQ)
-        last, t0 = rnd == RO - 1, 100.0 * rnd
-        al, hp = "al%d" % rnd, "hp%d" % rnd
-
-        def claims(m, k, r):
-            o, u0, u1 = 1920 * k, 120 * r, 120 * r + 120
-            a, v0, v1 = o + V * m, u0 + 60 * m, u0 + 60 * m + 60
-            ur, vr = (lambda name: (name, u0, u1)), (lambda name: (name, v0, v1))
-            fbank, nbank = 4 + k % 2 if m else 6, 7 - k % 2
-            at[0] = t0 + 21.0 + 0.5 * m + 1.3 * k
-            ne = V if m else 480
-            for b in range(0, V, ne):
-                tt(T.eq[:, a + b:a + b + ne], T["ww%d" % m][:].indirect(T.hw[:, v0 + b // 16:v0 + (b + ne) // 16]),
-                   T.iot[:, r * V + b:r * V + b + ne], A.is_equal, ne, ["ww%d" % m, "hw", ("iot", r, r + 1)],
-                   [("eq", a + b, a + b + ne)], f=GATH)
-            at[0] -= 30.0
-            if last and m == 0:
+        def spread_window(tile, h, way):
+            src = B(tile)[:, 240 * h:240 * h + 240]
+            if way == "d":
+                dma("S", [(B("win")[16 * k:16 * k + 16, 1920 * h:1920 * h + 1920], src) for k in range(8)],
+                    [R(tile, h, h + 1)], [R("win", 1920 * h, 1920 * h + 1920)], lat=T_WIN)
                 return
-            if last:
-                mm([(ps(7)[:, 0:120], cb(j), T.eq[:, o + j:o + 1920:16], j == 0, j == 15, 120) for j in range(16)],
-                   ["mcb", ("eq", o, o + 1920)], 7)
-                lin(T.fb[:, u0:u1], ps(7)[:, 0:120], 1.0, CZ, 120, ["ps7"], [ur("fb")])
-                mm([(ps(5)[:, 60 * m1:60 * m1 + 60], T.monp[:] if m1 == m2 else T.mon[:], T.fb[:, u0 + 60 * m2:u0 + 60 * m2 + 60],
-                     m2 == 0, m2 == 1, 60) for m1 in range(2) for m2 in range(2)], ["mon", "monp", ur("fb")], 5)
-                act(T[al][:, u0:u1], ps(5)[:, 0:120], F.Relu, 120, ["ps5"], [ur(al)], scale=K, col=CL)
-                tt(T.t1[:, u0:u1], T[al][:, u0:u1], T.home[:, u0:u1], A.add, 120, [ur(al), "home"], [ur("t1")])
-                tt(T.t2[:, u0:u1], T.t1[:, u0:u1], T[hp][:, u0:u1], A.min, 120, [ur("t1"), hp], [ur("t2")])
-                ts(T.ix[:, u0:u1], T.t2[:, u0:u1], OFF, None, A.subtract, None, 120, [ur("t2")], [ur("ix")])
-            else:
-                out = ps(fbank)[:, 0:60]
-                mm([(out, T.mi1[:], T.shi[:, v0:v1], True, False, 60), (out, T.mi1[:], T.slo[:, v0:v1], False, False, 60)]
-                   + [(out, cb(j, "mch"), T.eq[:, a + j:a + V:16], False, j == 15, 60) for j in range(16)],
-                   ["mi1", "mch", "shi", "slo", ("eq", a, a + V)], fbank)
-                tt(T.t1[:, v0:v1], out, T[hp][:, v0:v1], A.min, 60, ["ps%d" % fbank, hp], [vr("t1")], f=1.0)
-                act(T.fb[:, v0:v1], out, F.Sign, 60, ["ps%d" % fbank], [vr("fb")], scale=1.0, col=CF)
-                if m == 0:
-                    ts(T.ix[:, v0:v1], T.t1[:, v0:v1], OFF, None, A.subtract, None, 60, [vr("t1")], [vr("ix")])
-                else:
-                    out = ps(nbank)[:, 0:60]
-                    mm([(out, T.monk[:], T.fb[:, u0 + 60 * m2:u0 + 60 * m2 + 60], m2 == 0, m2 == 1, 60) for m2 in range(2)],
-                       ["monk", ur("fb")], nbank)
-                    tt(T.t2[:, v0:v1], out, T.t1[:, v0:v1], A.min, 60, ["ps%d" % nbank, vr("t1")], [vr("t2")], f=1.0)
-                    act(T[al][:, 60 * r:60 * r + 60], out, F.Sign, 60, ["ps%d" % nbank], [(al, r, r + 1)], scale=1.0, col=CS)
-                    ts(T.ix[:, v0:v1], T.t2[:, v0:v1], OFF, None, A.subtract, None, 60, [vr("t2")], [vr("ix")])
-            at[0] += 31.0
-            for m2 in (range(2) if last else [m]):
-                for b in (0, 480):
-                    a, c0 = o + V * m2 + b, u0 + 60 * m2 + b // 16
-                    lin(T.g5[:, a:a + 480], whole.indirect(T.ix[:, c0:c0 + 30]), 1.0, CN, 480, [wholer, ("ix", c0, c0 + 30)],
-                        [("g5", a, a + 480)], f=GATH, on="VA" if m2 and k >= (2 if last else 3) else "A")
+            for b in range(4):
+                bank, c0 = rot(), 1920 * h + 480 * b
+                mm([(ps(bank)[:, 240 * u:240 * u + 240], T.mw[:, (2 * b + u) * 128:(2 * b + u + 1) * 128], src, True, True, 240)
+                    for u in range(2)], ["mw", R(tile, h, h + 1)], bank)
+                cp(B("win")[:, c0:c0 + 480], ps(bank)[:, 0:480], 480, ["ps%d" % bank], [R("win", c0, c0 + 480)], on="VA")
 
-        if last:
-            at[0] = t0 + 10.0
-            tt(T.als[:], T.al0[:], T.al1[:], A.add, 240, ["al0", "al1"], ["als"])
-            lin(T.alt[:], T.als[:], -BLK / 2.0, CR, 240, ["als"], ["alt"])
-            for r in dests:
-                for m in range(2):
-                    c0 = 120 * r + 60 * m
-                    tt(T.home[:, c0:c0 + 60], T.alt[:, 60 * r:60 * r + 60], T.sfp[:, c0:c0 + 60], A.add, 60, ["alt", "sfp"],
-                       [("home", c0, c0 + 60)])
-        for k, (w0, w1) in enumerate(CHUNKS):
-            wc, hc, h0, o, m = w1 - w0, 16 * (w1 - w0), 16 * w0, 80 * w0, w0 // 48
-            hits = T.win[:, H0 + h0:H0 + h0 + hc]
-            hr = ("win", H0 + h0, H0 + h0 + hc)
-            wr = lambda name: (name, w0, w1)
-            for c in range(C):
-                a, b = o + c * hc, o + (c + 1) * hc
-                got = xw.indirect(T.cu[:, 96 * c + w0:96 * c + w1])
-                if k == 0:
-                    at[0] = t0 - 1.0 + 0.01 * c
-                    lin(T.dd[:, a:b], got, 1.0, CN, hc, [xr, "cu"], [("dd", a, b)], f=GATH)
-                    continue
-                at[0] = t0 + 14.0 * a / 7680
-                tt(T.dd[:, a:b], got, hits, A.subtract, hc, [xr, hr, "cu"], [("dd", a, b)], f=GATH)
-                act(T.ab[:, a:b], T.dd[:, a:b], F.Abs, hc, [("dd", a, b)], [("ab", a, b)])
-            if k == 0:
-                apart(o, hc, h0, "hb")
-            te = t0 + 14.0 * (o + 5 * hc) / 7680
-            at[0] = te - 0.5
-            kd = 3 + 4 * (k % 2)
-            out = ps(kd)[:, 0:5 * wc]
-            mm([(out, T.mnb[:], T.fl[:, :, w0:w1], True, False, 5 * wc), (out, T.mi1[:], T.chi[:, :, w0:w1], False, False, 5 * wc),
-                (out, T.mi1[:], T.clo[:, :, w0:w1], False, False, 5 * wc)], ["mnb", "mi1", "chi", "clo", wr("fl")], kd)
-            sums(kd, 0, "mck", o, wc, True)
-            lin(T.key[:, :, w0:w1], out, 1.0, CN, 5 * wc, ["ps%d" % kd], [wr("key")], on="V")
-            at[0] = te + 0.8
-            tt(T.m1[:, :, w0:w1], T.key[:, 0:2, w0:w1], T.key[:, 2:4, w0:w1], A.min, 2 * wc, [wr("key")], [wr("m1")])
-            at[0] += 0.3
-            tt(T.m2[:, w0:w1], T.m1[:, 0, w0:w1], T.m1[:, 1, w0:w1], A.min, wc, [wr("m1")], [wr("m2")])
-            at[0] += 0.3
-            tt(T.mi[:, w0:w1], T.m2[:, w0:w1], T.key[:, 4, w0:w1], A.min, wc, [wr("m2"), wr("key")], [wr("mi")])
-            at[0] += 0.3
-            ts(T.ma[:, w0:w1], T.mi[:, w0:w1], 4095, None, A.bitwise_and, None, wc, [wr("mi")], [wr("ma")])
-            at[0] += 0.3
-            ts(T.bi[:, w0:w1], T.ma[:, w0:w1], float(NT - 1), None, A.min, None, wc, [wr("ma")], [wr("bi")])
-            at[0] += 0.3
-            got = xw.indirect(T.bi[:, w0:w1])
-            if k == 0:
-                lin(T.db[:, h0:h0 + hc], got, 1.0, CN, hc, [xr, wr("bi")], [("db", h0, h0 + hc)], f=GATH, on="VA")
-            else:
-                tt(T.db[:, h0:h0 + hc], got, hits, A.subtract, hc, [xr, hr, wr("bi")], [("db", h0, h0 + hc)], f=GATH)
-            at[0] = t0 + (9.0, 16.0)[m] + 0.1 * k
-            apart(o, hc, h0, "db")
-            if w1 % 48 == 0:
-                at[0] = t0 - 5.0
-                u0, u1 = 48 * m, 48 * m + 48
-                for c in range(C):
-                    tt(T.nb[:, c, u0:u1], T.key[:, c, u0:u1], T.mi[:, u0:u1], A.is_le, 48, [("key", u0, u1), ("mi", u0, u1)],
-                       [("nb", 5 * m + c, 5 * m + c + 1)])
-                act(T.nl[:, :, u0:u1], T.key[:, :, u0:u1], F.Relu, 240, [("key", u0, u1)], [("nl", u0, u1)])
-                mine = [(v0, v1, ps(4)[:, 5 * (v0 - u0):5 * (v1 - u0)]) for (v0, v1) in CHUNKS if v0 // 48 == m]
-                mm([(ps(4)[:, 0:240], T.mz[:, 0:128], T.mz[:, 0:240], True, False, 240)]
-                   + [(o2, T.mni[:], src[:, :, v0:v1], False, False, 5 * (v1 - v0)) for v0, v1, o2 in mine for src in (T.thi, T.tlo)],
-                   ["mz", "mni", ("thi", u0, u1), ("tlo", u0, u1)], 4)
-                for v0, v1, _ in mine:
-                    if v1 == u1:
-                        mm([(o2, w, src[:, :, y0:y1], False, False, 5 * (y1 - y0)) for y0, y1, o2 in mine
-                            for w, src in ((T.mn2[:], T.nl), (T.mi4[:], T.nb))],
-                           ["mn2", "mi4", ("nl", u0, u1), ("nb", 5 * m, 5 * m + 5)], 4)
-                    sums(4, 5 * (v0 - u0), "mcb", 80 * v0, v1 - v0, v1 == u1)
-                for v0, v1, o2 in mine:
-                    act(T.fl[:, :, v0:v1], o2, F.Sign, 5 * (v1 - v0), ["ps4"], [("fl", v0, v1)], scale=1.0, col=CH)
-                mm([(ps(5)[:, 0:384], T.mi1[:], src[:, 384 * m:384 * m + 384], b == 0, False, 384) for b, src in enumerate((T.ihi, T.ilo))],
-                   ["mi1", ("ihi", m, m + 1), ("ilo", m, m + 1)], 5)
-                spread([T.fl], m, [("fl", u0, u1)], own=False)
-                lin(T["ww%d" % m][:], ps(5)[:, 0:384], 1.0, CK, 384, ["ps5"], ["ww%d" % m])
-                if m == 0:
-                    for k2, r in enumerate(dests):
-                        claims(0, k2, r)
-        for k, r in enumerate(dests):
-            o, u0, u1 = 1920 * k, 120 * r, 120 * r + 120
-            claims(1, k, r)
-            if not last:
+        banks = [2, 3, 6, 7]
+        mm([const(ps(KE)[:, 0:240], "ck0", 240, True)], ["ck0", "one"], KE)
+        cuts = sorted(set(range(0, 481, 48)) | set(range(0, 481, 120)))
+        for k, s in enumerate(sources):
+            lastsrc = k == N - 1
+            mm([(ps(KE)[:, 48 * (u // 96) + u % 48:48 * (u // 96) + u % 48 + v - u], place(u // 120, s, u % 96 // 48),
+                 lists(s, u % 120, u % 120 + v - u), False, lastsrc and v == 480, v - u)
+                for u, v in zip(cuts, cuts[1:])], ["mf", listed(s)], KE)
+            if f == 0:
                 for hh in range(2):
-                    bank, a = (2 * k + hh) % 4, o + 480 * hh
-                    mm([(ps(bank)[:, 0:480], T.msum[:], T.g5[:, a + V * m:a + V * m + 480], m == 0, m == 1, 480) for m in range(2)],
-                       ["msum"] + [("g5", a + V * m, a + V * m + 480) for m in range(2)], bank)
-                    c0 = xs - BLK + r * V + 480 * hh
-                    lin(T.win[:, c0:c0 + 480], ps(bank)[:, 0:480], 1.0 + 2.0 ** -12, CFL, 480, ["ps%d" % bank],
-                        [("win", c0, c0 + 480)], on="VA")
+                    bank = banks[(2 * k + hh) % 4]
+                    mm([(ps(bank)[:, 240 * b:240 * b + 240], T.mr[:, (2 * hh + b) * 128:(2 * hh + b + 1) * 128],
+                         _slot(T, "x", s), True, True, 240) for b in range(2)], ["mr", ("Lx", s, s + 1)], bank)
+                    c0 = s * V + 480 * hh
+                    cp(B("win")[:, c0:c0 + 480], ps(bank)[:, 0:480], 480, ["ps%d" % bank], [R("win", c0, c0 + 480)], on="VA")
+            for b in range(2):
+                c0 = 112 - 16 * s
+                mm([(ps(R0 + b)[:, 0:384], T.mh[:, 2 * f + b, c0:c0 + 128], _slot(T, "h", s), k == 0, lastsrc, 384)], ["mh", ("Lh", s, s + 1)], R0 + b)
+        cp(B("cu")[:], ps(KE)[:, 0:240], 240, ["ps%d" % KE], [R("cu")])
+        ts(B("cf")[:], ps(KE)[:, 0:240], -NT / 2.0, None, A.add, None, 240, ["ps%d" % KE], [R("cf")])
+        for b in range(2):
+            cp(B("hit")[:, 384 * b:384 * b + 384], ps(R0 + b)[:, 0:384], 384, ["ps%d" % (R0 + b)], [R("hit", 384 * b, 384 * b + 384)], on="VA")
+        for h in range(2):
+            mm([(ps(TR)[:, 240 * h:240 * h + 240], T.mx[:, f, 4 - 4 * u:132 - 4 * u], _slot(T, "x", 2 * h + u),
+                 u == 0, u == 1, 240) for u in range(2)], ["mx", "Lx"], TR)
+            cp(B("xa")[:, 240 * h:240 * h + 240], ps(TR)[:, 240 * h:240 * h + 240], 240, ["ps%d" % TR], [R("xa", h, h + 1)], on="VA")
+            if f == 1:
+                spread_window("xa", h, CFG["w0"][h])
+        phase("th")
+        n = CFG["cut"][0]
+        for a in range(0, NT, n):
+            cp(B("tmp")[:, a:a + n], T.thw[:].indirect(B("cu")[:, a // 16:(a + n) // 16]), n, ["thw", "thz", R("cu")],
+               [R("tmp", a, a + n)], f=GATH, on="VA")
+
+        def thresholds():
+            mm([(ps(TR)[:, 0:240], T.mt[:, f, 15 - j:143 - j], B("tmp")[:, j:NT:16], j == 0, j == 15, 240) for j in range(16)],
+               ["mt", R("tmp")], TR)
+            ts(B("thf")[:], ps(TR)[:, 0:240], -2048.0, None, A.add, None, 240, ["ps%d" % TR], [R("thf")])
+
+        def positions():
+            mm([(ps(TR)[:, 60 * s:60 * s + 60], T.ml[:, f, 64 - 64 * m:192 - 64 * m], lists(s, 120 + 60 * m, 180 + 60 * m),
+                 m == 0, m == 1, 60) for s in sources for m in range(2)], ["ml", "sc", "Lc"], TR)
+            cp(B("hf")[:], ps(TR)[:, 0:240], 240, ["ps%d" % TR], [R("hf")])
+            mm([const(ps(TR)[:, 0:240], "cc1", 240, True), (ps(TR)[:, 0:240], T.mhf[:], B("hf")[:], False, True, 240)],
+               ["cc1", "one", "mhf", R("hf")], TR)
+            ts(B("hw")[:], ps(TR)[:, 0:240], MAGIC, MAGIC, A.add, A.subtract, 240, ["ps%d" % TR], [R("hw")])
+            grp = [(ps(TR)[:, jj:384:8], T.mg[:, jj, 8 - 2 * c:136 - 2 * c], B("cf")[:, 48 * c:48 * c + 48],
+                    c == 0, c == C - 1, 48) for jj in range(8) for c in range(C)]
+            for j in range(0, 40, 20):
+                mm(grp[j:j + 20], ["mg", R("cf")], TR)
+            cp(B("idw")[:], ps(TR)[:, 0:384], 384, ["ps%d" % TR], [R("idw")], on="VA")
+            n = CFG["cut"][1]
+            for a in range(0, NT, n):
+                tt(B("yy")[:, a:a + n], B("idw")[:].indirect(B("hw")[:, a // 16:(a + n) // 16]), T.iot[:, a:a + n],
+                   A.is_equal, n, [R("idw"), R("hw"), ("iot", a // V, a // V + 1)], [R("yy", a, a + n)], f=GATH)
+
+        def positions_end():
+            mm([(ps(KE)[:, 0:240], T.mi1[:], B("hf")[:], True, False, 240)]
+               + [(ps(KE)[:, 0:240], cb(j, "mcp"), B("yy")[:, j:NT:16], False, j == 15, 240) for j in range(16)],
+               ["mi1", "mcp", R("hf"), R("yy")], KE)
+            cp(B("pos")[:], ps(KE)[:, 0:240], 240, ["ps%d" % KE], [R("pos")])
+
+        def keys(c, d):
+            out, n = ps(KE)[:, 48 * c:48 * d], 48 * (d - c)
+            mm([(out, T.mi1[:], B("cf")[:, 48 * c:48 * d], True, False, n)]
+               + [(out, cb(j, "mck"), B("ab")[:, H * c + j:H * d:16], False, j == 15, n) for j in range(16)],
+               ["mi1", "mck", R("cf"), R("ab", H * c, H * d)], KE)
+
+        def refit(bank, n, parts, old, tile, c0, reads, tag):
+            out, rr, rest = ps(bank)[:, 0:n], B("rr")[:, c0:c0 + n], B("ns")[:, c0:c0 + n]
+            mm([const(out, "cc1", n, True)] + old, ["cc1", "one"] + reads, bank)
+            for grp, rd in parts:
+                mm([x[:4] + (x is parts[-1][0][-1],) + x[5:] for x in grp], ["me"] + rd, bank)
+            ts(rr, out, -192.0 * STEP, -232.0 * STEP, A.add, A.max, n, ["ps%d" % bank], [R("rr", c0, c0 + n)])
+            tt(rest, out, rr, A.subtract, n, ["ps%d" % bank, R("rr", c0, c0 + n)], [R("ns", c0, c0 + n)])
+            ts(B(tile)[:, c0:c0 + n], rest, MAGIC - 192.0 * STEP, MAGIC, A.add, A.subtract, n, [R("ns", c0, c0 + n)], [tag])
+
+        phase("pos")
+        positions()
+        phase("th")
+        thresholds()
+        key, kr = ps(KE), "ps%d" % KE
+        for rnd in range(RO):
+            yield
+            last = rnd == RO - 1
+            old, new = ("xa", "xb", "xc")[rnd], ("xb", "xc", "xl")[rnd]
+            phase("far")
+            for c in range(C):
+                n = CFG["cut"][2]
+                for a in range(H * c, H * c + H, n):
+                    rows = B("dd")[:, a:a + n]
+                    tt(rows, B("win")[:].indirect(B("cu")[:, a // 16:(a + n) // 16]), rows if rnd else B("hit")[:, a % H:a % H + n],
+                       A.add if rnd else A.subtract, n, [R("win"), R("cu"), R("hit"), R("wd"), R("dd", a, a + n)], [R("dd", a, a + n)], f=GATH)
+                a, b = H * c, H * c + H
+                act(B("ab")[:, a:b], B("dd")[:, a:b], F.Abs, H, [R("dd", a, b)], [R("ab", a, b)])
+            if ADD:
+                dma("S", [(B("ys")[:, 0:H * ADD], B("dd")[:, H * (C - ADD):NT])], [R("dd", H * (C - ADD), NT)], [R("ys")], lat=3000.0)
+            keys(0, 2)
+            ts(B("sa")[:], key[:, 0:96], CAP, None, A.min, None, 96, [kr], [R("sa")])
+            keys(2, 4)
+            tt(B("sb")[:], key[:, 96:192], B("sa")[:], A.min, 96, [kr, R("sa")], [R("sb")])
+            tt(B("sc")[:], B("sb")[:, 0:48], B("sb")[:, 48:96], A.min, 96, [R("sb")], [R("sc")])
+            keys(4, 5)
+            phase("best")
+            tt(B("mi")[:], key[:, 192:240], B("sc")[:], A.min, 48, [kr, R("sc")], [R("mi")])
+            for c in (1, 2, 3, 4, 0):
+                tt(B("nb")[:, 48 * c:48 * c + 48], key[:, 48 * c:48 * c + 48], B("mi")[:], A.is_le, 48, [kr, R("mi")], [R("nb", c, c + 1)])
+                if c == C - 1:
+                    out = ps(TR)[:, 0:48]
+                    mm([(out, T.mi1[:], T.hc[:], True, False, 48)]
+                       + [(out, T.mnc[:, 128 * k - 128:128 * k], B("nb")[:, 48 * k:48 * k + 48], False, k == c, 48) for k in range(1, C)],
+                       ["mi1", "hc", "mnc", R("nb", 1, C)], TR)
+                    cp(B("bi")[:], out, 48, ["ps%d" % TR], [R("bi")])
+            best = B("dd")[:].indirect(B("bi")[:])
+            op({"V": (lambda q, best=best: q.tensor_scalar(B("db")[:], best, -1.0, None, A.mult), vc(H, GATH)),
+                "A": (lambda q, best=best: q.activation(B("db")[:], best, F.Identity, scale=-1.0), vc(H, GATH))}, [R("dd"), R("bi")], [R("db")])
+
+            def added(c):
+                a, name = H * (c - C + ADD), "d%d" % ndma[0]
+                ndma[0] += 1
+                op({"G": (lambda q: q.dma_start(B("ys")[:, a:a + H], B("db")[:], accum_op=A.add).then_inc(T.sem[name], 16), T_ISSUE)},
+                   [R("db"), R("ys", a, a + H)], [R("ys", a, a + H)], lat=T_ADD, sem=(name, 16), dma=True)
+                act(B("ab")[:, H * c:H * c + H], B("ys")[:, a:a + H], F.Abs, H, [R("ys", a, a + H)], [R("ab", H * c, H * c + H)])
+
+            def apart(c, d):
+                for k in range(max(c, C - ADD), d):
+                    added(k)
+                d = min(d, C - ADD)
+                for a in range(H * c, H * d, 512):
+                    b, bank, grp, u = min(a + 512, H * d), 4 + turn[1] % 2, [], a
+                    turn[1] += 1
+                    while u < b:
+                        v = min(b, (u // H + 1) * H)
+                        grp.append((ps(bank)[:, u - a:v - a], T.mi1[:], B("dd")[:, u:v], True, False, v - u))
+                        grp.append((ps(bank)[:, u - a:v - a], T.mi1[:], B("db")[:, u % H:u % H + v - u], False, True, v - u))
+                        u = v
+                    mm(grp, ["mi1", R("dd", a, b), R("db")], bank)
+                    act(B("ab")[:, a:b], ps(bank)[:, 0:b - a], F.Abs, b - a, ["ps%d" % bank], [R("ab", a, b)])
+
+            def flags(c, d):
+                u, v = 48 * c, 48 * d
+                out = key[:, 240 + u:240 + v]
+                mm([(out, T.mni[:], B("thf")[:, u:v], True, False, v - u), (out, T.mnb[:], B("nb")[:, u:v], False, False, v - u)]
+                   + [(out, cb(j), B("ab")[:, H * c + j:H * d:16], False, j == 15, v - u) for j in range(16)],
+                   ["mni", "mnb", "mcb", R("thf"), R("nb", c, d), R("ab", H * c, H * d)], KE)
+                op({"A": (lambda q: q.activation(B("fl")[:, u:v], out, F.Sign, bias=T.low[:, 0:1]), vc(v - u))}, [kr, "low"], [R("fl", c, d)])
+
+            def marks(c, d):
+                n, per = 48 * (d - c), 512 // (48 * (d - c))
+                for j0 in range(0, 16, per):
+                    js, bank = range(j0, min(16, j0 + per)), 6 + turn[2] % 2
+                    turn[2] += 1
+                    mm([(ps(bank)[:, n * (j - j0):n * (j - j0 + 1)], T.mbc[:, j * 128:(j + 1) * 128], B("fl")[:, 48 * c:48 * d], True, True, n)
+                        for j in js], ["mbc", R("fl", c, d)], bank)
+                    for j in js:
+                        view = B("dd")[:, H * c + j:H * d:16]
+                        tt(view, view, ps(bank)[:, n * (j - j0):n * (j - j0 + 1)], A.max, n,
+                           ["ps%d" % bank, R("ab", H * c, H * d), R("dd", H * c, H * d)], [R("wd", 16 * c + j, 16 * c + j + 1)])
+            phase("apart")
+            for c, d in CFG["sets"]:
+                apart(c, d)
+                flags(c, d)
+            phase("mark")
+            for c, d in CFG["marks"]:
+                marks(c, d)
+            if rnd == 0:
+                phase("pos2")
+                positions_end()
+
+            phase("back")
+
+            def gather(r):
+                n = CFG["cut"][3]
+                for a in range(r * V, r * V + V, n):
+                    cp(B("yy")[:, a:a + n], B("dd")[:].indirect(B("pos")[:, a // 16:(a + n) // 16]), n, [R("dd"), R("wd"), R("pos")],
+                       [R("yy", a, a + n)], f=GATH, on="VA")
+            if not last:
+                for h in range(2):
+                    bank, parts = KE if h else TR, []
+                    for u in range(2):
+                        r = 2 * h + u
+                        gather(r)
+                        parts.append(([(ps(bank)[:, 0:240], T.me[:, 7 - k:135 - k], B("yy")[:, 1920 * h + 240 * k:1920 * h + 240 * k + 240],
+                                        False, False, 240) for k in range(4 * u, 4 * u + 4)], [R("yy", r * V, r * V + V)]))
+                    refit(bank, 240, parts, [], "xl", 240 * h, [], R("xl", h, h + 1))
+                    spread_window("xl", h, CFG["w"][h])
+                phase("keep")
+                kept = "xk" if rnd else "xa"
+                bank = TR
+                mm([(ps(bank)[:, 0:480], T.mni[:], B(x)[:], x == old, x != old, 480) for x in (old, "xl")], ["mni", R(old), R("xl")], bank)
+                act(B(new)[:], ps(bank)[:, 0:480], F.Identity, 480, ["ps%d" % bank], [R(new)], scale=-1.0)
+                tt(B("mk")[:], ps(bank)[:, 0:480], B(kept)[:], A.min, 480, ["ps%d" % bank, R(kept)], [R("mk")])
+                tt(B("xk")[:], B(new)[:], B("mk")[:], A.max, 480, [R(new), R("mk")], [R("xk")])
                 continue
-            mm([(ps(k)[:, 0:240], T.me[:, 3 - a:131 - a], T.g5[:, o + V * m + 240 * a:o + V * m + 240 * a + 240],
-                 a == 0 and m == 0, a == 3 and m == 1, 240) for a in range(4) for m in range(2)], ["me", ("g5", o, o + 1920)], k)
-            xf = T.xf[:, 240 * r:240 * r + 240]
-            lin(xf, ps(k)[:, 0:240], 1.0 + 2.0 ** -12, CFL, 240, ["ps%d" % k], [("xf", r, r + 1)], on="VA")
-            ts(T.res[:, OB * r:OB * r + 240], xf, BIG + 1, None, A.subtract, None, 240, [("xf", r, r + 1)], [("res", 2 * r, 2 * r + 1)])
-            mm([(ps(4)[:, 0:120], cb(j), T.eq[:, o + 120 * j:o + 120 * j + 120], j == 0, j == 15, 120) for j in range(16)],
-               ["mcb", ("eq", o, o + 1920)], 4)
-            lin(T.fc[:, u0:u1], ps(4)[:, 0:120], 1.0, CZ, 120, ["ps4"], [("fc", u0, u1)], on="VA")
-            mm([(ps(6)[:, 0:120], T.mo8p[:], T.fc[:, u0:u1], True, True, 120)], ["mo8p", ("fc", u0, u1)], 6)
-            ts(T.res[:, OB * r + 240:OB * r + OB], ps(6)[:, 0:120], 11.0, None, A.is_ge, None, 120, ["ps6"],
-               [("res", 2 * r + 1, 2 * r + 2)])
-            piece = T.res[:, OB * r:OB * r + OB]
-            if r == me:
-                dma("S", T.yx[32 * r:32 * r + 32, :], T.res[:, OB * r:OB * r + 240], [("res", 2 * r, 2 * r + 1)], [])
-                dma("S", T.yl[2 * r:2 * r + 2, :], T.res[:, OB * r + 240:OB * r + OB], [("res", 2 * r + 1, 2 * r + 2)], [])
-                continue
-            if r in far:
-                dst, land, rsem, tail, via = plan[(me, r)][0], T.ro[:], T.sem.rout, 6500.0, plan[(r, me)][0]
-            else:
-                dst, land, rsem, tail, via = T.cores[r], T.lo[:, me * OB:(me + 1) * OB], T.sem["ao%d" % me], 3500.0, T.cores[r]
-            on = topo.engines(core, dst)
-            rid, pid = topo.addr(dst, core)
-            sent[0] += len(on)
-            op({"G": (lambda q, land=land, piece=piece, rsem=rsem, pid=pid, rid=rid, on=on:
-                      q.remote_dma(land, piece, rsem, T.sem.sent, pid, rid, _mask(on)), 800.0)},
-               [("res", 2 * r, 2 * r + 2)], [])
-            arrives("ao%d" % r, len(topo.engines(via, core)), tail, [("res", 2 * r, 2 * r + 2)], [("lo", r, r + 1)])
-            dma("S", T.yx[32 * r:32 * r + 32, :], T.lo[:, OB * r:OB * r + 240], [("lo", r, r + 1)], [])
-            dma("S", T.yl[2 * r:2 * r + 2, :], T.lo[:, OB * r + 240:OB * r + OB], [("lo", r, r + 1)], [])
+            dests = far + near + [me]
+
+            def turned(out, k, tile, name, alone=False):
+                h, u = dests[k] // 2, dests[k] % 2
+                return [(out, T[name][:, u, 1 - a:129 - a], B(tile)[:, 240 * h + 120 * a:240 * h + 120 * a + 120],
+                         alone and a == 0, alone and a == 1, 120) for a in range(2)]
+            for name, terms in (("xa", (("xk", "md"),)), ("xb", ((old, "md7"), ("xk", "md6")))):
+                mm([x[:3] + (j == 0 and x[3], j == len(terms) - 1 and x[4]) + x[5:] for k in range(N) for j, (tile, mat) in enumerate(terms)
+                    for x in turned(ps(TR)[:, 120 * k:120 * k + 120], k, tile, mat, True)], ["md", "md7", "md6", R(old), R("xk")], TR)
+                cp(B(name)[:], ps(TR)[:, 0:480], 480, ["ps%d" % TR], [R(name)], on="VA")
+            for k0, k1 in CFG["ends"][f]:
+                bank, c0, n = (TR, 4)[k0 % 2 * f], 120 * k0, 120 * (k1 - k0)
+                parts = []
+                mm([const(key[:, 0:n // 2], "cc1", n // 2, True)], ["cc1", "one"], KE)
+                for k in range(k0, k1):
+                    r = dests[k]
+                    gather(r)
+                    out = ps(bank)[:, 120 * (k - k0):120 * (k - k0 + 1)]
+                    parts.append(([(out, T.me[:, 7 - b:135 - b], B("yy")[:, r * V + 120 * b:r * V + 120 * b + 120], False, False, 120)
+                                   for b in range(8)], [R("yy", r * V, r * V + V)]))
+                    mm([(key[:, 60 * (k - k0):60 * (k - k0 + 1)], cb(j, "mcf"), B("yy")[:, r * V + 60 * j:r * V + 60 * j + 60],
+                         False, False, 60) for j in range(16)], ["mcf", R("yy", r * V, r * V + V)], KE)
+                cols = R(new, c0, c0 + n)
+                refit(bank, n, parts, [(ps(bank)[:, 0:n], T.mi1[:], B("xb")[:, c0:c0 + n], False, False, n)], new, c0, ["mi1", R("xb")], cols)
+                op({"A": (lambda q, c0=c0, n=n: q.activation(B("rr")[:, c0:c0 + n], B("ns")[:, c0:c0 + n], F.Identity, bias=T.low[:, 1:2],
+                                                           scale=-1.0), vc(n))}, [R("ns", c0, c0 + n), "low"], [R("rr", c0, c0 + n)])
+                tt(B("mk")[:, c0:c0 + n], B("xa")[:, c0:c0 + n], B("rr")[:, c0:c0 + n], A.min, n, [R("xa"), R("rr", c0, c0 + n)],
+                   [R("mk", c0, c0 + n)])
+                tt(B("res")[:, k0:k1, 0:120], B(new)[:, c0:c0 + n], B("mk")[:, c0:c0 + n], A.max, n, [cols, R("mk", c0, c0 + n)],
+                   [R("rx", k0, k1)])
+                mm([(key[:, 60 * (k - k0):60 * (k - k0 + 1)], T.mal[:, 128 * a:128 * a + 128], B(new)[:, 120 * k + 60 * a:120 * k + 60 * a + 60],
+                     False, a == 1 and k == k1 - 1, 60) for k in range(k0, k1) for a in range(2)], ["mal", cols], KE)
+                ts(B("res")[:, k0:k1, 120:180], key[:, 0:n // 2], -1000.0, None, A.is_gt, None, n // 2, [kr], [R("rf", k0, k1)])
+            for k, r in enumerate(dests):
+                gq, o, done = 2 * r + f, OB * r, [R("rx", k, k + 1), R("rf", k, k + 1)]
+                if r == me:
+                    dma("S", [(T.yx[16 * gq:16 * gq + 16, :], B("res")[:, k, 0:120]), (T.yl[gq:gq + 1, :], B("res")[:, k, 120:180])], done, [])
+                    continue
+                name = "a" + "op"[f]
+                if r in far:
+                    dst, land, rsem, tail, via = plan[(me, r)][1 - f], T.ro[:], T.sem.rout, 6500.0, plan[(r, me)][1 - f]
+                else:
+                    dst, land, rsem, tail, via = (T.cores[r], B("lo")[:, me * OB:me * OB + 180], T.sem["%s%d" % (name, me)], 3500.0,
+                                                  T.cores[r])
+                on = topo.engines(core, dst)
+                rid, pid = topo.addr(dst, core)
+                sent[0] += len(on)
+                op({"G": (lambda q, land=land, piece=B("res")[:, k, 0:180], rsem=rsem, pid=pid, rid=rid, on=on:
+                          q.remote_dma(land, piece, rsem, T.sem.sent, pid, rid, _mask(on)), 800.0)}, done, [R("out", k, k + 1)])
+                arrives("%s%d" % (name, r), len(topo.engines(via, core)), tail, done, [R("lo", r, r + 1)])
+                dma("S", [(T.yx[16 * gq:16 * gq + 16, :], B("lo")[:, o:o + 120]), (T.yl[gq:gq + 1, :], B("lo")[:, o + 120:o + 180])],
+                    [R("lo", r, r + 1)], [])
+    fits = [fit(0), fit(1)]
+    for rnd in range(-1, RO):
+        for f in range(2):
+            ahead[0], ahead[1], ahead[3] = CFG["lag"] * (1 - f), f, rnd
+            next(fits[f], None)
 
     for sem in _emit(ops, {"V": g.vector, "A": g.scalar, "P": g.tensor, "G": g, "S": g.sync}, T):
         g.wait_ge(T.sem[sem[0]], sem[1])

from concourse.bass import DstId, RemoteDMATransfer
from concourse.mybir import AluOpType, ActivationFunctionType

N, V, H, C, RO = 4, 960, 768, 5, 3
NT = N * V
XB, IB, OB = 624, 240, 192
MAGIC = 1.5 * 2.0 ** 23
CAP = 4095.0 * 4096.0
STEP = 4096.0
MARK = 64 * STEP
CYC, PEC, GATH, HOP, LOOK, T_DMA, T_WIN, T_NEAR, T_FAR = 0.83, 0.42, 1.5, 140.0, 200.0, 2200.0, 4500.0, 9000.0, 12500.0
ADD, T_ISSUE, T_ADD = 2, 900.0, 3000.0
CFG = {"pfix": 60.0, "seed": 2, "shifts": 7500, "swaps": 12000, "passes": 4, "cut": (768, 960, 768, 960), "lag": 0.0, "w": "dp", "w0": "dd", "sets": ((0, 2), (2, 5)), "marks": ((0, 5),),
       "ends": (((0, 2), (2, 4)), ((0, 2), (2, 4)))}

F32, BF, F16, I32, U16 = "float32", "bfloat16", "float16", "int32", "uint16"
SCRATCH = {
    "sx": ("dram", [N, 128, 240], BF), "sh": ("dram", [N, 128, 384], BF),
    "rx": ("dram", [128, 240], BF), "rh": ("dram", [128, 384], BF), "rc": ("dram", [128, IB], F16),
    "rt": ("dram", [2, 128, 15], BF), "ro": ("dram", [128, 180], BF), "lt": ("dram", [2 * N, 128, 15], BF),
}
for _names, _shape, _dt in (
        ("lb", [N * XB], BF), ("li", [N, IB], I32), ("lf sf", [N, IB], F16), ("ti", [64], I32), ("tb", [128], BF), ("iot", [NT], F32),
        ("cx", [48], F32), ("low pf", [4], F32), ("pc pi", [2], I32), ("thw", [NT], BF),
        ("mw", [8 * 128], BF), ("mh", [4, 240], BF), ("ml", [2, 192], BF), ("mt", [2, 144], BF), ("mf", [8, 240], BF),
        ("mr", [4 * 128], BF), ("mx md md7 md6", [2, 136], BF), ("me", [136], BF), ("mcb mck mcp mcf", [144], BF),
        ("mbc", [16 * 128], BF), ("mal", [2 * 128], BF), ("mg", [8, 136], BF),
        ("mi1 mni mnb mhf ck0 cc1", [128], BF), ("mnc one", [512], BF), ("hc", [48], F16)):
    for _n in _names.split():
        SCRATCH[_n] = ("sbuf", [128] + _shape, _dt)
for _f in "AB":
    for _names, _shape, _dt in (
            ("win ab yy tmp dd", [NT], BF), ("hit db", [H], BF), ("ys", [3 * H], BF), ("idw", [384], F32), ("ns", [480], F32), ("cu hw pos", [240], U16), ("bi", [48], U16),
            ("cf hf thf", [240], F16), ("nb fl", [240], BF), ("sa sb", [96], F32), ("sc mi", [48], F32),
            ("xa xb xc rr mk xk xl", [480], BF), ("lo", [N * OB], BF), ("res", [N, OB], BF)):
        for _n in _names.split():
            SCRATCH[_n + _f] = ("sbuf", [128] + _shape, _dt)
for _k in range(8):
    SCRATCH["ps%d" % _k] = ("psum", [128, 512], F32)

SEMAPHORES = (["eV", "eA", "eP", "eG", "sent", "rin1", "rin2", "rout"]
              + ["a%s%d" % (k, s) for k in "xhctop" for s in range(N)] + ["d%d" % k for k in range(56)])


def _mask(engines):
    return sum(1 << e for e in engines)


def _relays(T, topo):
    plan = {}
    for s, cs in enumerate(T.cores):
        far = [d for d, cd in enumerate(T.cores) if d != s and not topo.may_write(cs, cd)]
        free = sorted((c for c in topo.cores_of(cs) if T.rank_of(c) is None), key=lambda c: (topo.die(c) != topo.die(cs), c))
        got = {d: [] for d in far}
        for _ in range(2):
            for d in far:
                c = [c for c in free if topo.may_write(c, T.cores[d])][0]
                free.remove(c)
                got[d].append(c)
        for d in far:
            plan[(s, d)] = tuple(got[d])
    return plan


def _lanes(T, topo, plan, s):
    far = [d for d in range(N) if (s, d) in plan]
    near = [d for d in range(N) if d != s and d not in far][0]
    off = topo.engines(T.cores[s], T.cores[near])
    rest = [e for e in topo.engines(T.cores[s], plan[(s, far[0])][0]) if e not in off]
    h, q = len(rest) // 2, len(off) // 4
    lanes = {("x", near): off, ("c", near): off, ("h", near): off, ("t", near): off[:2 * q], ("u", near): off[2 * q:]}
    for j, d in enumerate(far):
        lanes["x", d] = lanes["h", d] = lanes["c", d] = rest[j * h:(j + 1) * h]
        lanes["t", d], lanes["u", d] = rest[j * h:j * h + h // 2], rest[j * h + h // 2:(j + 1) * h]
    return lanes


def _slot(T, piece, s):
    if piece in "tu":
        return T.lt[N * (piece == "u") + s]
    if piece == "c":
        return T.lf[:, s, :]
    c0, c1 = {"x": (0, 240), "h": (240, XB)}[piece]
    return T.lb[:, s * XB + c0:s * XB + c1]


def _relay_program(g, core, T, topo, plan):
    for (s, d), pair in plan.items():
        if core not in pair:
            continue
        lanes = _lanes(T, topo, plan, s)
        out = topo.engines(core, T.cores[d])
        rid, pid = topo.addr(T.cores[d], core)
        f = int(core == pair[0])
        if f:
            steps = [(T.sem.rin1, len(lanes["x", d]), [(_slot(T, "x", s), T.rx[:])], "ax"),
                     (T.sem.rin2, len(lanes["t", d]) + len(lanes["u", d]), [(_slot(T, "tu"[b], s), T.rt[b]) for b in range(2)], "at")]
        else:
            steps = [(T.sem.rin1, len(lanes["c", d]), [(_slot(T, "c", s), T.rc[:])], "ac"),
                     (T.sem.rin2, len(lanes["h", d]), [(_slot(T, "h", s), T.rh[:])], "ah")]
        steps.append((T.sem.rout, len(topo.engines(T.cores[s], core)), [(T["lo" + "AB"[f]][:, s * OB:s * OB + 180], T.ro[:])],
                      "a" + "op"[f]))
        for sem, n, moves, name in steps:
            g.wait_ge(sem, n)
            k = len(out) // len(moves)
            g.remote_dma_fused([RemoteDMATransfer(dst_ids=[DstId(rid=rid, pnc=pid)], dma_engine_mask=_mask(out[j * k:(j + 1) * k]),
                                                  remote_sem=T.sem["%s%d" % (name, s)], src=src, dst=land)
                                for j, (land, src) in enumerate(moves)], local_sem=T.sem.sent)
        g.wait_ge(T.sem.sent, len(steps) * len(out))


_ORDERS = {}


def _greedy(alts, pred, succ, pri):
    n = len(alts)
    free = {e: 0.0 for e in "VAPGSX"}
    start, end, eng, left = [0.0] * n, [0.0] * n, [None] * n, [len(p) for p in pred]
    ready = [k for k in range(n) if not left[k]]
    when = {k: {e: 0.0 for e in alts[k]} for k in ready}
    while ready:
        t, e = min((max(when[k][e], free[e]), e != "A", e) for k in ready for e in when[k])[::2]
        k = min((k for k in ready if e in when[k] and when[k][e] <= t + (LOOK if len(when[k]) == 1 else 0.0)), key=lambda k: pri[k])
        ready.remove(k)
        start[k], eng[k] = max(when[k][e], free[e]), e
        end[k] = start[k] + alts[k][e]
        if e != "X":
            free[e] = end[k]
        for s, _, _ in succ[k]:
            left[s] -= 1
            if not left[s]:
                ready.append(s)
                when[s] = {f: max(end[d] + w + (HOP if raw or eng[d] != f else 0.0) for d, raw, w in pred[s]) for f in alts[s]}
    return start, end, eng


def _shifts(ops, full, alts, pred, succ, lat, pri):
    n, seed, its = len(ops), [CFG["seed"]], CFG["shifts"]
    phase = [(o["fit"], o["rnd"], o["grp"]) for o in ops]
    free = [k for k in range(n) if phase[k][2] != "first"]
    names, both = sorted(set(phase[k] for k in free)), [k for k in free if len(full[k]) > 1]

    def rand():
        seed[0] = (seed[0] * 1103515245 + 12345) % 2147483648
        return seed[0] / 2147483648.0
    now = best = None
    for it in range(its):
        p, a, u = list(pri), alts, rand() if it else 1.0
        if u < 0.3:
            k, e = both[int(rand() * len(both))], "VAx"[int(rand() * 3)]
            a = list(alts)
            a[k] = full[k] if e == "x" else {e: full[k][e]}
        elif u < 0.7:
            name, d = names[int(rand() * len(names))], 6000.0 * (rand() - 0.5)
            for k in free:
                if phase[k] == name or (u >= 0.6 and phase[k][::2] == name[::2]):
                    p[k] += d
        elif it:
            for _ in range(3):
                p[free[int(rand() * len(free))]] += 5000.0 * (rand() - 0.5)
        start, end, eng = _greedy(a, pred, succ, p)
        span = max(end[k] + lat[k] for k in range(n))
        if now is None or span <= now + 600.0 * rand() * (1.0 - it / its):
            now, pri, alts = span, p, a
            if best is None or span < best[0]:
                best = (span, start, eng)
    return best


def _swaps(alts, pred, succ, lat, start, eng):
    n, seed = len(alts), [1]
    eng, prev, nxt = list(eng), [-1] * n, [-1] * n
    for e in "VAPGS":
        seq = sorted((k for k in range(n) if eng[k] == e), key=lambda k: (start[k], k))
        for a, b in zip(seq, seq[1:]):
            nxt[a], prev[b] = b, a
    direct = [set(d for d, _, _ in p) for p in pred]

    def rand():
        seed[0] = (seed[0] * 1103515245 + 12345) % 2147483648
        return seed[0] / 2147483648.0

    def weights():
        cost = [alts[k][eng[k]] for k in range(n)]
        return (cost, [[(d, cost[d] + w + (HOP if raw or eng[d] != eng[k] else 0.0)) for d, raw, w in pred[k]] for k in range(n)],
                [[(s, cost[k] + w + (HOP if raw or eng[s] != eng[k] else 0.0)) for s, raw, w in succ[k]] for k in range(n)])

    def times():
        left = [len(pred[k]) + (prev[k] >= 0) for k in range(n)]
        r, q, order = [0.0] * n, [0.0] * n, [k for k in range(n) if not left[k]]
        for k in order:
            t = r[k]
            for s, w in sw[k] + ([(nxt[k], cost[k])] if nxt[k] >= 0 else []):
                if t + w > r[s]:
                    r[s] = t + w
                left[s] -= 1
                if not left[s]:
                    order.append(s)
        if len(order) < n:
            return None
        for k in reversed(order):
            b = cost[k] + max(lat[k], q[nxt[k]] if nxt[k] >= 0 else 0.0)
            for s, w in sw[k]:
                if w + q[s] > b:
                    b = w + q[s]
            q[k] = b
        return r, q, order

    def link(a, u, b):
        prev[u], nxt[u] = a, b
        if a >= 0:
            nxt[a] = u
        if b >= 0:
            prev[b] = u
    cost, pw, sw = weights()
    best, barred, since = None, {}, 0
    for it in range(1, CFG["swaps"] + 1):
        r, q, order = times()
        span, since = max(q), since + 1
        if best is None or span < best[0] - 1e-6:
            best, since = (span, r, list(eng), list(prev), list(nxt)), 0
        if since > 3000:
            eng[:], prev[:], nxt[:] = best[2:]
            cost, pw, sw = weights()
            since, barred = 0, {}
            continue
        moves = []
        for u in order:
            if r[u] + q[u] < span - 1e-3:
                continue
            v = nxt[u]
            if v >= 0 and r[v] + q[v] > span - 1e-3 and abs(r[u] + cost[u] - r[v]) < 1e-3 and u not in direct[v]:
                a, b = prev[u], nxt[v]
                rv = max([r[a] + cost[a] if a >= 0 else 0.0] + [r[d] + w for d, w in pw[v]])
                ru = max([rv + cost[v]] + [r[d] + w for d, w in pw[u]])
                qu = max([cost[u] + max(lat[u], q[b] if b >= 0 else 0.0)] + [w + q[s] for s, w in sw[u]])
                qv = max([cost[v] + qu] + [w + q[s] for s, w in sw[v]])
                guess = max(rv + qv, ru + qu)
                if barred.get((u, v), 0) < it or guess < best[0] - 1:
                    moves.append((guess + 30 * rand(), u, v))
            if len(alts[u]) > 1 and barred.get((u, -1), 0) < it:
                e = [x for x in alts[u] if x != eng[u]][0]
                t = max([r[d] + w for d, w in pw[u]] + [0.0])
                seq = [k for k in order if eng[k] == e]
                before = [k for k in seq if r[k] <= r[u] and (r[k] + cost[k] * 0.5 <= t or k in direct[u])]
                a = before[-1] if before else -1
                b, c = nxt[a] if before else seq[0], alts[u][e]
                ru = max(t, r[a] + cost[a] if before else 0.0)
                qu = max([c + lat[u], c + (q[b] if b >= 0 else 0.0)] + [w - cost[u] + c + q[s] for s, w in sw[u]])
                moves.append((ru + qu + 200 + 30 * rand(), u, -1, e, a, b))
        if not moves:
            barred, since = {}, since + 50
            continue
        m = min(moves) if rand() > 0.03 else moves[int(rand() * len(moves))]
        u, v = m[1:3]
        if v >= 0:
            a, b = prev[u], nxt[v]
            link(a, v, u)
            link(v, u, b)
            barred[(v, u)] = it + 8 + int(14 * rand())
            continue
        was = (list(prev), list(nxt), eng[u])
        if prev[u] >= 0:
            nxt[prev[u]] = nxt[u]
        if nxt[u] >= 0:
            prev[nxt[u]] = prev[u]
        link(m[4], u, m[5])
        eng[u] = m[3]
        cost, pw, sw = weights()
        if times() is None:
            prev[:], nxt[:], eng[u] = was
            cost, pw, sw = weights()
        barred[(u, -1)] = it + 40 + int(40 * rand())
    return best[:3]


def _schedule(ops):
    n = len(ops)
    above, pred, succ = [0] * n, [], [[] for _ in range(n)]
    lat = [o["lat"] for o in ops]
    for k, o in enumerate(ops):
        far = 0
        for d in o["deps"]:
            far |= above[d]
        pred.append([(d, raw, lat[d]) for d, raw in sorted(o["deps"].items()) if not far >> d & 1])
        above[k] = far | sum(1 << d for d, _, _ in pred[k])
        for d, raw, _ in pred[k]:
            succ[d].append((k, raw, lat[d]))
    key = tuple(tuple(p) for p in pred)
    if key not in _ORDERS:
        full = [{e: c for e, (_, c) in o["alts"].items()} for o in ops]
        alts = [a if len(a) == 1 or o["grp"] in ("first", "land") or o["rnd"] + o["fit"] == RO else {"A": a["A"]} for a, o in zip(full, ops)]
        way = [0.0] * n
        for k in range(n - 1, -1, -1):
            way[k] = min(alts[k].values()) + lat[k] + max([way[s] + HOP for s, _, _ in succ[k]] + [0.0])
        pri, top = [-way[k] - ops[k]["prio"] for k in range(n)], None
        for _ in range(CFG["passes"]):
            start, end, eng = _greedy(alts, pred, succ, pri)
            span = max(end[k] + lat[k] for k in range(n))
            if top is None or span < top[0]:
                top = (span, start, eng)
            _, late, _ = _greedy([{eng[k]: alts[k][eng[k]]} for k in range(n)], succ, pred, [-end[k] - lat[k] for k in range(n)])
            pri = [-late[k] - ops[k]["prio"] for k in range(n)]
        top = _shifts(ops, full, alts, pred, succ, lat, [top[1][k] - (o["prio"] if o["grp"] == "first" else 0.0) for k, o in enumerate(ops)])
        span, start, eng = _swaps(full, pred, succ, lat, top[1], top[2])
        _ORDERS[key] = (eng, {e: sorted((k for k in range(n) if eng[k] == e), key=lambda k: (start[k], k)) for e in "VAPGSX"}, span)
    return _ORDERS[key]


def _emit(ops, queues, T):
    n = len(ops)
    eng, order, _ = _schedule(ops)
    pos = {k: j for e in order for j, k in enumerate(order[e])}
    waits = [[] for _ in range(n)]
    marked = set()
    for e in "VAPGS":
        seen = {}
        for k in order[e]:
            need = {}
            for d, raw in ops[k]["deps"].items():
                if ops[d]["sem"] is not None:
                    if d not in seen:
                        seen[d] = 1
                        waits[k].append(("sem", d))
                elif eng[d] != e or raw or ops[k]["sem"] is not None:
                    need[eng[d]] = max(need.get(eng[d], -1), pos[d])
            for f, j in need.items():
                if seen.get(f, -1) < j:
                    seen[f] = j
                    waits[k].append(("eng", order[f][j]))
                    marked.add(order[f][j])
    count = {k: j + 1 for e in "VAPG" for j, k in enumerate(x for x in order[e] if x in marked)}
    for e in "VAPGS":
        q = queues[e]
        for k in order[e]:
            for kind, d in waits[k]:
                if kind == "sem":
                    q.wait_ge(T.sem[ops[d]["sem"][0]], ops[d]["sem"][1])
                else:
                    q.wait_ge(T.sem["e" + eng[d]], count[d])
            ins = ops[k]["alts"][e][0](q)
            if k in marked:
                ins.then_inc(T.sem["e" + e], 1)
    waited = set(d for w in waits for kind, d in w if kind == "sem")
    return [ops[k]["sem"] for k in range(n) if ops[k]["dma"] and k not in waited]


def rank_program(g, core, T, topo):
    plan = _relays(T, topo)
    me = T.rank_of(core)
    if me is None:
        _relay_program(g, core, T, topo, plan)
        return
    A, F = AluOpType, ActivationFunctionType
    ops, log, ndma, sent, ahead = [], {}, [0], [0], [1e5, 0, "first", -1]
    far = [d for d in range(N) if (me, d) in plan]
    near = [d for d in range(N) if d != me and d not in far]
    sources = [me] + near + far

    def op(alts, reads, writes, lat=0.0, prio=0.0, sem=None, dma=False):
        k, deps = len(ops), {}
        for acc, isw in ((reads, False), (writes, True)):
            for r in acc:
                name, lo, hi = r if isinstance(r, tuple) else (r, 0, 1 << 30)
                bank = name.startswith("ps")
                w = isw or bank
                old = log.setdefault(name, [])
                for (d, a, b, dw) in old:
                    if d != k and a < hi and lo < b and (w or dw):
                        deps[d] = deps.get(d, False) or (dw and not isw and not bank)
                if w:
                    old[:] = [x for x in old if not (lo <= x[1] and x[2] <= hi)]
                old.append((k, lo, hi, w))
        ops.append({"alts": alts, "deps": deps, "lat": lat, "prio": prio + ahead[0], "fit": ahead[1], "grp": ahead[2], "rnd": ahead[3], "name": str(writes[-1:]), "sem": sem, "dma": dma})

    def vc(n, f=1.0):
        return 60.0 + max(64.0, n * f) * CYC

    def tt(out, a, b, o, n, reads, writes, f=1.0):
        op({"V": (lambda q: q.tensor_tensor(out, a, b, o), vc(n, f))}, reads, writes)

    def ts(out, a, s1, s2, o0, o1, n, reads, writes, prio=0.0):
        if o1 is None:
            op({"V": (lambda q: q.tensor_scalar(out, a, s1, None, o0), vc(n))}, reads, writes, prio=prio)
        else:
            op({"V": (lambda q: q.tensor_scalar(out, a, s1, s2, o0, o1), vc(n))}, reads, writes, prio=prio)

    def cp(out, a, n, reads, writes, f=1.0, on="V", prio=0.0):
        alts = {"V": (lambda q: q.tensor_copy(out, a), vc(n, f)), "A": (lambda q: q.activation(out, a, F.Copy), vc(n, f))}
        op({e: alts[e] for e in on}, reads, writes, prio=prio)

    def act(out, a, func, n, reads, writes, scale=1.0):
        op({"A": (lambda q: q.activation(out, a, func, scale=scale), vc(n))}, reads, writes)

    def fill(ap, val, n, writes):
        op({"V": (lambda q: q.memset(ap, val), vc(n))}, [], writes)

    def mm(group, reads, bank):
        def run(q):
            ins = None
            for (o, l, r, st, sp, _) in group:
                ins = q.matmul(o, l, r, st, sp)
            return ins
        op({"P": (run, CFG["pfix"] + sum(max(64, x[5]) for x in group) * PEC)}, reads, ["ps%d" % bank])

    def dma(e, moves, reads, writes, prio=0.0, lat=T_DMA):
        name = "d%d" % ndma[0]
        ndma[0] += 1

        def run(q):
            for out, src in moves:
                q.dma_start(out, src).then_inc(T.sem[name], 16)
        op({e: (run, 100.0 * len(moves))}, reads, writes, lat=lat, prio=prio, sem=(name, 16 * len(moves)), dma=True)

    def iota(out, pattern, base, mult, n, writes, prio=0.0):
        if "pc" in writes:
            fn = lambda q: q.iota(out, pattern, base, mult)
        else:
            fn = lambda q: q.iota(out, pattern, base, mult, allow_small_or_imprecise_dtypes=True)
        op({"G": (fn, 130.0 + 2 * n * CYC)}, [], writes, prio=prio)

    def arrives(name, val, t, reads, writes):
        op({"X": (None, t)}, reads, writes, sem=(name, val))

    def ps(k):
        return T["ps%d" % k]

    top = 2e5
    dma("S", [(T.sx[:], T.fx[:])], [], ["sx"], prio=top + 200)
    dma("A", [(T.li[:, d, 0:120], T.cl[32 * d:32 * d + 32, :]) for d in range(N)], [], [("li", 0, 1)], prio=top + 200)
    dma("S", [(T.li[:, d, 120:240], T.hl[32 * d:32 * d + 32, :]) for d in range(N)], [], [("li", 1, 2)], prio=top + 150)
    dma("S", [(T.sh[:], T.hv[:])], [], ["sh"], prio=top + 100)
    ts(T.sf[:, :, 0:120], T.li[:, :, 0:120], -NT / 2.0, None, A.add, None, 480, [("li", 0, 1)], [("sc", 0, 1)], prio=top)
    cp(T.sf[:, :, 120:240], T.li[:, :, 120:240], 480, [("li", 1, 2)], [("sc", 1, 2)], prio=top)
    dma("A", [(T.ti[:, 16 * d:16 * d + 15], T.th[2 * d:2 * d + 2, :]) for d in range(N)], ["ti"], ["tl"], prio=top)
    iota(T.pc[:, 0:1], [[0, 1]], 0, 1, 1, ["call", "pc"], prio=top)
    iota(T.cx[:], [[1, 48]], 0, 0, 48, ["call", "cx"], prio=top)

    def select(name, out, pattern, base=0, mult=1, test=A.is_equal, own=False):
        n = 1
        for _, count in pattern:
            n *= count
        src = out if own else T.one[:, 0:n]
        op({"G": (lambda q: q.affine_select(out, src, pattern, test, 0.0, base, mult), 170.0 + 2 * n * CYC)}, ["one", name], ["call", name])

    def within(name, out, pattern, size):
        select(name, out, pattern, 0, 1, A.is_ge)
        select(name, out, [[-s, c] for s, c in pattern], size - 1, -1, A.is_ge, True)
    for name, val, n in (("one", 1.0, 512), ("mf", 0.0, 1920), ("mh", 0.0, 960), ("mx", 0.0, 272), ("ml", 0.0, 384), ("mcb", 0.0, 144),
                         ("mt", 0.0, 288), ("mg", 0.0, 1088), ("thw", 0.0, NT), ("me", 0.0, 136), ("md", 0.0, 272), ("mcf", 0.0, 144),
                         ("mbc", -MARK, 2048), ("mw", 1.0, 1024)):
        fill(T[name][:], val, n / 2, ["thz" if name == "thw" else name])
    select("mr", T.mr[:], [[-1, 4], [0, 8], [-4, 16]])
    select("mf", T.mf[:, :, 112:128], [[-64, 2], [-1, 4], [-4, 16]])
    for m in range(2):
        select("mh", T.mh[:, :, 112 + 64 * m:128 + 64 * m], [[-64, 2], [-1, 2], [-4, 16]], -2 * m)
    select("mi1", T.mi1[:], [[-1, 128]])
    for d in range(N):
        a, b = 16 * d, 16 * d + 15
        cp(T.tb[:, a:b], T.ti[:, a:b], 15, ["tl"], [("tb", a, b)], prio=top)
        op({"V": (lambda q, a=a, b=b: q.tensor_tensor(T.tb[:, 64 + a:64 + b], T.ti[:, a:b], T.tb[:, a:b], A.subtract), vc(15))},
           ["tl", ("tb", a, b)], [("tb", 64 + a, 64 + b)], prio=top)
    lanes = _lanes(T, topo, plan, me)
    for pieces in ("x", "c", "h", "tu"):
        tr = []
        for piece in pieces:
            for d in far + near:
                if piece in "tu":
                    src = T.tb[:, 64 * (piece == "u") + 16 * d:64 * (piece == "u") + 16 * d + 15]
                else:
                    src = T.sf[:, d, :] if piece == "c" else T["s" + piece][d]
                if d in near:
                    c, land, rsem = T.cores[d], _slot(T, piece, me), T.sem["a%s%d" % (pieces[0], me)]
                else:
                    c = plan[(me, d)][piece in "ch"]
                    land = T.rt[int(piece == "u")] if piece in "tu" else T["r" + piece][:]
                    rsem = T.sem["rin%d" % (1 if piece in "xc" else 2)]
                rid, pid = topo.addr(c, core)
                tr.append(RemoteDMATransfer(dst_ids=[DstId(rid=rid, pnc=pid)], dma_engine_mask=_mask(lanes[piece, d]),
                                            remote_sem=rsem, src=src, dst=land))
                sent[0] += len(lanes[piece, d])
        op({"G": (lambda q, tr=tr: q.remote_dma_fused(tr, local_sem=T.sem.sent), 1000.0)},
           ["tb"] if pieces == "tu" else ["s" + x for x in pieces], ["call"], prio=top)
    rows = slice(32 * me, 32 * me + 32)
    for piece, src in (("x", T.fx[rows, :]), ("h", T.hv[rows, :])):
        dma("S", [(_slot(T, piece, me), src)], ["sh"], [("L" + piece, me, me + 1)])
    dma("S", [(_slot(T, "tu"[b], me), T.tb[:, 64 * b + 16 * me:64 * b + 16 * me + 15]) for b in range(2)], ["tb"], [("Lt", me, me + 1)])
    for s in near + far:
        theirs = _lanes(T, topo, plan, s)
        for piece, late in (("x", 0.0), ("c", 1000.0), ("h", 2000.0), ("t", 3000.0)):
            if s in near:
                n_in = len(theirs[piece, me]) + (len(theirs["u", me]) if piece == "t" else 0)
            else:
                n_in = len(topo.engines(plan[(s, me)][piece in "ch"], core))
            arrives("a%s%d" % (piece, s), n_in, (T_NEAR if s in near else T_FAR) + late, [], [("L" + piece, s, s + 1)])
    for a in range(4):
        select("mx", T.mx[:, :, 4 + a:132:8], [[-64, 2], [-4, 16]], -a)
    select("ml", T.ml[:, :, 64:128], [[-64, 2], [-1, 4], [-4, 16]])
    within("mcb", T.mcb[:, 15:143:16], [[-16, 8]], 16)
    within("mt", T.mt[:, :, 15:143:16], [[-2, 2], [-16, 8]], 2)
    for u in range(2):
        select("mg", T.mg[:, :, 8 + u:136:16], [[-2, 8], [-16, 8]], -u)
    for r in range(N):
        iota(T.iot[:, r * V:(r + 1) * V], [[1, V]], r * V - NT // 2, 0, V, ["call", ("iot", r, r + 1)])
    select("mbc", T.mbc[:], [[-1, 16], [-16, 8], [0, 16]], own=True)
    select("mw", T.mw[:], [[-1, 8], [0, 8], [-8, 16]], own=True)
    select("md", T.md[:, :, 1:129:2], [[-4, 2], [-8, 16], [-1, 4]])
    select("mal", T.mal[:], [[-1, 2], [0, 8], [1, 16]], mult=-2)
    within("mcf", T.mcf[:, 15:143:16], [[-16, 4], [-64, 2]], 16)

    p = T.pc[:, 0:1]
    for col, sh, m in ((0, 0, 15), (1, 1, 7)):
        ts(T.pi[:, col:col + 1], p, sh, m, A.arith_shift_right, A.bitwise_and, 1, ["pc"], [("pi", col, col + 1)])
    cp(T.pf[:, 0:2], T.pi[:], 2, ["pi"], [("pf", 0, 2)])
    ts(T.pf[:, 2:3], T.pf[:, 1:2], float(C), T.pf[:, 1:2], A.is_lt, A.mult, 1, [("pf", 0, 2)], [("pf", 2, 3)])
    ts(T.pf[:, 3:4], T.pf[:, 2:3], float(H), None, A.mult, None, 1, [("pf", 2, 3)], [("pf", 3, 4)])
    ts(T.me[:, 7:135:8], T.cx[:, 0:16], T.pf[:, 0:1], -0.125, A.is_equal, A.mult, 16, ["cx", ("pf", 0, 2), "me"], ["me"])
    ts(T.hc[:], T.cx[:], 16.0, T.pf[:, 0:1], A.mult, A.add, 48, ["cx", ("pf", 0, 2)], ["hc"])
    fill(T.low[:, 0:1], -2047.5, 1, [("low", 0, 1)])
    fill(T.low[:, 1:2], 192.0 * STEP - 0.5, 1, [("low", 1, 2)])
    for name, src, w in (("mck", "mcb", 4096.0), ("mni", "mi1", -1.0), ("mnb", "mi1", 8192.0), ("mhf", "mi1", 0.5), ("mcp", "mcb", T.pf[:, 3:4]),
                         ("md7", "md", 7.0), ("md6", "md", -6.0), ("mcf", "mcf", -1.0 / 64)):
        act(T[name][:], T[src][:], F.Identity, 272 if src == "md" else 144, [src, "pf"], [name], scale=w)
    for c in range(1, C):
        act(T.mnc[:, 128 * c - 128:128 * c], T.mi1[:], F.Identity, 128, ["mi1"], [("mnc", c, c + 1)], scale=float(H * c))
    for name, part in (("ck0", NT / 256.0), ("cc1", -7.0 / 2048)):
        fill(T[name][:], part, 64, [name])
    ahead[0] = CFG["lag"]
    for f in range(2):
        dma("S", [(T.thw[16 * k + 2 * f:16 * k + 2 * f + 2, :], T.lt[:, 64 * f:64 * f + 64, :]) for k in range(8)], ["Lt", "thz"],
            [("thw", f, f + 1)], lat=3000.0)

    def lists(s, a, b):
        return (T.sf if s == me else T.lf)[:, s, a:b]

    def listed(s):
        return "sc" if s == me else ("Lc", s, s + 1)

    def cb(j, name="mcb"):
        return T[name][:, 15 - j:143 - j]

    def fit(f):
        def B(name):
            return T[name + "AB"[f]]

        def R(name, lo=0, hi=1 << 30):
            return (name + "AB"[f], lo, hi)
        KE, TR, R0 = f, 2 + f, 4 + 2 * f
        turn = [0, 0, 0]

        def phase(name):
            ahead[2] = name
        phase("land")

        def rot():
            turn[0] += 1
            return (KE, TR)[turn[0] % 2]

        def place(a, q, m):
            c0 = 112 - 64 * m - 16 * q
            return T.mf[:, 4 * f + a, c0:c0 + 128]

        def const(out, name, n, start):
            return (out, T[name][:], T.one[:, 0:n], start, False, n)

        def spread_window(tile, h, way):
            src = B(tile)[:, 240 * h:240 * h + 240]
            if way == "d":
                dma("S", [(B("win")[16 * k:16 * k + 16, 1920 * h:1920 * h + 1920], src) for k in range(8)],
                    [R(tile, h, h + 1)], [R("win", 1920 * h, 1920 * h + 1920)], lat=T_WIN)
                return
            for b in range(4):
                bank, c0 = rot(), 1920 * h + 480 * b
                mm([(ps(bank)[:, 240 * u:240 * u + 240], T.mw[:, (2 * b + u) * 128:(2 * b + u + 1) * 128], src, True, True, 240)
                    for u in range(2)], ["mw", R(tile, h, h + 1)], bank)
                cp(B("win")[:, c0:c0 + 480], ps(bank)[:, 0:480], 480, ["ps%d" % bank], [R("win", c0, c0 + 480)], on="VA")

        banks = [2, 3, 6, 7]
        mm([const(ps(KE)[:, 0:240], "ck0", 240, True)], ["ck0", "one"], KE)
        cuts = sorted(set(range(0, 481, 48)) | set(range(0, 481, 120)))
        for k, s in enumerate(sources):
            lastsrc = k == N - 1
            mm([(ps(KE)[:, 48 * (u // 96) + u % 48:48 * (u // 96) + u % 48 + v - u], place(u // 120, s, u % 96 // 48),
                 lists(s, u % 120, u % 120 + v - u), False, lastsrc and v == 480, v - u)
                for u, v in zip(cuts, cuts[1:])], ["mf", listed(s)], KE)
            if f == 0:
                for hh in range(2):
                    bank = banks[(2 * k + hh) % 4]
                    mm([(ps(bank)[:, 240 * b:240 * b + 240], T.mr[:, (2 * hh + b) * 128:(2 * hh + b + 1) * 128],
                         _slot(T, "x", s), True, True, 240) for b in range(2)], ["mr", ("Lx", s, s + 1)], bank)
                    c0 = s * V + 480 * hh
                    cp(B("win")[:, c0:c0 + 480], ps(bank)[:, 0:480], 480, ["ps%d" % bank], [R("win", c0, c0 + 480)], on="VA")
            for b in range(2):
                c0 = 112 - 16 * s
                mm([(ps(R0 + b)[:, 0:384], T.mh[:, 2 * f + b, c0:c0 + 128], _slot(T, "h", s), k == 0, lastsrc, 384)], ["mh", ("Lh", s, s + 1)], R0 + b)
        cp(B("cu")[:], ps(KE)[:, 0:240], 240, ["ps%d" % KE], [R("cu")])
        ts(B("cf")[:], ps(KE)[:, 0:240], -NT / 2.0, None, A.add, None, 240, ["ps%d" % KE], [R("cf")])
        for b in range(2):
            cp(B("hit")[:, 384 * b:384 * b + 384], ps(R0 + b)[:, 0:384], 384, ["ps%d" % (R0 + b)], [R("hit", 384 * b, 384 * b + 384)], on="VA")
        for h in range(2):
            mm([(ps(TR)[:, 240 * h:240 * h + 240], T.mx[:, f, 4 - 4 * u:132 - 4 * u], _slot(T, "x", 2 * h + u),
                 u == 0, u == 1, 240) for u in range(2)], ["mx", "Lx"], TR)
            cp(B("xa")[:, 240 * h:240 * h + 240], ps(TR)[:, 240 * h:240 * h + 240], 240, ["ps%d" % TR], [R("xa", h, h + 1)], on="VA")
            if f == 1:
                spread_window("xa", h, CFG["w0"][h])
        phase("th")
        n = CFG["cut"][0]
        for a in range(0, NT, n):
            cp(B("tmp")[:, a:a + n], T.thw[:].indirect(B("cu")[:, a // 16:(a + n) // 16]), n, ["thw", "thz", R("cu")],
               [R("tmp", a, a + n)], f=GATH, on="VA")

        def thresholds():
            mm([(ps(TR)[:, 0:240], T.mt[:, f, 15 - j:143 - j], B("tmp")[:, j:NT:16], j == 0, j == 15, 240) for j in range(16)],
               ["mt", R("tmp")], TR)
            ts(B("thf")[:], ps(TR)[:, 0:240], -2048.0, None, A.add, None, 240, ["ps%d" % TR], [R("thf")])

        def positions():
            mm([(ps(TR)[:, 60 * s:60 * s + 60], T.ml[:, f, 64 - 64 * m:192 - 64 * m], lists(s, 120 + 60 * m, 180 + 60 * m),
                 m == 0, m == 1, 60) for s in sources for m in range(2)], ["ml", "sc", "Lc"], TR)
            cp(B("hf")[:], ps(TR)[:, 0:240], 240, ["ps%d" % TR], [R("hf")])
            mm([const(ps(TR)[:, 0:240], "cc1", 240, True), (ps(TR)[:, 0:240], T.mhf[:], B("hf")[:], False, True, 240)],
               ["cc1", "one", "mhf", R("hf")], TR)
            ts(B("hw")[:], ps(TR)[:, 0:240], MAGIC, MAGIC, A.add, A.subtract, 240, ["ps%d" % TR], [R("hw")])
            grp = [(ps(TR)[:, jj:384:8], T.mg[:, jj, 8 - 2 * c:136 - 2 * c], B("cf")[:, 48 * c:48 * c + 48],
                    c == 0, c == C - 1, 48) for jj in range(8) for c in range(C)]
            for j in range(0, 40, 20):
                mm(grp[j:j + 20], ["mg", R("cf")], TR)
            cp(B("idw")[:], ps(TR)[:, 0:384], 384, ["ps%d" % TR], [R("idw")], on="VA")
            n = CFG["cut"][1]
            for a in range(0, NT, n):
                tt(B("yy")[:, a:a + n], B("idw")[:].indirect(B("hw")[:, a // 16:(a + n) // 16]), T.iot[:, a:a + n],
                   A.is_equal, n, [R("idw"), R("hw"), ("iot", a // V, a // V + 1)], [R("yy", a, a + n)], f=GATH)

        def positions_end():
            mm([(ps(KE)[:, 0:240], T.mi1[:], B("hf")[:], True, False, 240)]
               + [(ps(KE)[:, 0:240], cb(j, "mcp"), B("yy")[:, j:NT:16], False, j == 15, 240) for j in range(16)],
               ["mi1", "mcp", R("hf"), R("yy")], KE)
            cp(B("pos")[:], ps(KE)[:, 0:240], 240, ["ps%d" % KE], [R("pos")])

        def keys(c, d):
            out, n = ps(KE)[:, 48 * c:48 * d], 48 * (d - c)
            mm([(out, T.mi1[:], B("cf")[:, 48 * c:48 * d], True, False, n)]
               + [(out, cb(j, "mck"), B("ab")[:, H * c + j:H * d:16], False, j == 15, n) for j in range(16)],
               ["mi1", "mck", R("cf"), R("ab", H * c, H * d)], KE)

        def refit(bank, n, parts, old, tile, c0, reads, tag):
            out, rr, rest = ps(bank)[:, 0:n], B("rr")[:, c0:c0 + n], B("ns")[:, c0:c0 + n]
            mm([const(out, "cc1", n, True)] + old, ["cc1", "one"] + reads, bank)
            for grp, rd in parts:
                mm([x[:4] + (x is parts[-1][0][-1],) + x[5:] for x in grp], ["me"] + rd, bank)
            ts(rr, out, -192.0 * STEP, -232.0 * STEP, A.add, A.max, n, ["ps%d" % bank], [R("rr", c0, c0 + n)])
            tt(rest, out, rr, A.subtract, n, ["ps%d" % bank, R("rr", c0, c0 + n)], [R("ns", c0, c0 + n)])
            ts(B(tile)[:, c0:c0 + n], rest, MAGIC - 192.0 * STEP, MAGIC, A.add, A.subtract, n, [R("ns", c0, c0 + n)], [tag])

        phase("pos")
        positions()
        phase("th")
        thresholds()
        key, kr = ps(KE), "ps%d" % KE
        for rnd in range(RO):
            yield
            last = rnd == RO - 1
            old, new = ("xa", "xb", "xc")[rnd], ("xb", "xc", "xl")[rnd]
            phase("far")
            for c in range(C):
                n = CFG["cut"][2]
                for a in range(H * c, H * c + H, n):
                    rows = B("dd")[:, a:a + n]
                    tt(rows, B("win")[:].indirect(B("cu")[:, a // 16:(a + n) // 16]), rows if rnd else B("hit")[:, a % H:a % H + n],
                       A.add if rnd else A.subtract, n, [R("win"), R("cu"), R("hit"), R("wd"), R("dd", a, a + n)], [R("dd", a, a + n)], f=GATH)
                a, b = H * c, H * c + H
                act(B("ab")[:, a:b], B("dd")[:, a:b], F.Abs, H, [R("dd", a, b)], [R("ab", a, b)])
            if ADD:
                dma("S", [(B("ys")[:, 0:H * ADD], B("dd")[:, H * (C - ADD):NT])], [R("dd", H * (C - ADD), NT)], [R("ys")], lat=3000.0)
            keys(0, 2)
            ts(B("sa")[:], key[:, 0:96], CAP, None, A.min, None, 96, [kr], [R("sa")])
            keys(2, 4)
            tt(B("sb")[:], key[:, 96:192], B("sa")[:], A.min, 96, [kr, R("sa")], [R("sb")])
            tt(B("sc")[:], B("sb")[:, 0:48], B("sb")[:, 48:96], A.min, 96, [R("sb")], [R("sc")])
            keys(4, 5)
            phase("best")
            tt(B("mi")[:], key[:, 192:240], B("sc")[:], A.min, 48, [kr, R("sc")], [R("mi")])
            for c in (1, 2, 3, 4, 0):
                tt(B("nb")[:, 48 * c:48 * c + 48], key[:, 48 * c:48 * c + 48], B("mi")[:], A.is_le, 48, [kr, R("mi")], [R("nb", c, c + 1)])
                if c == C - 1:
                    out = ps(TR)[:, 0:48]
                    mm([(out, T.mi1[:], T.hc[:], True, False, 48)]
                       + [(out, T.mnc[:, 128 * k - 128:128 * k], B("nb")[:, 48 * k:48 * k + 48], False, k == c, 48) for k in range(1, C)],
                       ["mi1", "hc", "mnc", R("nb", 1, C)], TR)
                    cp(B("bi")[:], out, 48, ["ps%d" % TR], [R("bi")])
            best = B("dd")[:].indirect(B("bi")[:])
            op({"V": (lambda q, best=best: q.tensor_scalar(B("db")[:], best, -1.0, None, A.mult), vc(H, GATH)),
                "A": (lambda q, best=best: q.activation(B("db")[:], best, F.Identity, scale=-1.0), vc(H, GATH))}, [R("dd"), R("bi")], [R("db")])

            def added(c):
                a, name = H * (c - C + ADD), "d%d" % ndma[0]
                ndma[0] += 1
                op({"G": (lambda q: q.dma_start(B("ys")[:, a:a + H], B("db")[:], accum_op=A.add).then_inc(T.sem[name], 16), T_ISSUE)},
                   [R("db"), R("ys", a, a + H)], [R("ys", a, a + H)], lat=T_ADD, sem=(name, 16), dma=True)
                act(B("ab")[:, H * c:H * c + H], B("ys")[:, a:a + H], F.Abs, H, [R("ys", a, a + H)], [R("ab", H * c, H * c + H)])

            def apart(c, d):
                for k in range(max(c, C - ADD), d):
                    added(k)
                d = min(d, C - ADD)
                for a in range(H * c, H * d, 512):
                    b, bank, grp, u = min(a + 512, H * d), 4 + turn[1] % 2, [], a
                    turn[1] += 1
                    while u < b:
                        v = min(b, (u // H + 1) * H)
                        grp.append((ps(bank)[:, u - a:v - a], T.mi1[:], B("dd")[:, u:v], True, False, v - u))
                        grp.append((ps(bank)[:, u - a:v - a], T.mi1[:], B("db")[:, u % H:u % H + v - u], False, True, v - u))
                        u = v
                    mm(grp, ["mi1", R("dd", a, b), R("db")], bank)
                    act(B("ab")[:, a:b], ps(bank)[:, 0:b - a], F.Abs, b - a, ["ps%d" % bank], [R("ab", a, b)])

            def flags(c, d):
                u, v = 48 * c, 48 * d
                out = key[:, 240 + u:240 + v]
                mm([(out, T.mni[:], B("thf")[:, u:v], True, False, v - u), (out, T.mnb[:], B("nb")[:, u:v], False, False, v - u)]
                   + [(out, cb(j), B("ab")[:, H * c + j:H * d:16], False, j == 15, v - u) for j in range(16)],
                   ["mni", "mnb", "mcb", R("thf"), R("nb", c, d), R("ab", H * c, H * d)], KE)
                op({"A": (lambda q: q.activation(B("fl")[:, u:v], out, F.Sign, bias=T.low[:, 0:1]), vc(v - u))}, [kr, "low"], [R("fl", c, d)])

            def marks(c, d):
                n, per = 48 * (d - c), 512 // (48 * (d - c))
                for j0 in range(0, 16, per):
                    js, bank = range(j0, min(16, j0 + per)), 6 + turn[2] % 2
                    turn[2] += 1
                    mm([(ps(bank)[:, n * (j - j0):n * (j - j0 + 1)], T.mbc[:, j * 128:(j + 1) * 128], B("fl")[:, 48 * c:48 * d], True, True, n)
                        for j in js], ["mbc", R("fl", c, d)], bank)
                    for j in js:
                        view = B("dd")[:, H * c + j:H * d:16]
                        tt(view, view, ps(bank)[:, n * (j - j0):n * (j - j0 + 1)], A.max, n,
                           ["ps%d" % bank, R("ab", H * c, H * d), R("dd", H * c, H * d)], [R("wd", 16 * c + j, 16 * c + j + 1)])
            phase("apart")
            for c, d in CFG["sets"]:
                apart(c, d)
                flags(c, d)
            phase("mark")
            for c, d in CFG["marks"]:
                marks(c, d)
            if rnd == 0:
                phase("pos2")
                positions_end()

            phase("back")

            def gather(r):
                n = CFG["cut"][3]
                for a in range(r * V, r * V + V, n):
                    cp(B("yy")[:, a:a + n], B("dd")[:].indirect(B("pos")[:, a // 16:(a + n) // 16]), n, [R("dd"), R("wd"), R("pos")],
                       [R("yy", a, a + n)], f=GATH, on="VA")
            if not last:
                for h in range(2):
                    bank, parts = KE if h else TR, []
                    for u in range(2):
                        r = 2 * h + u
                        gather(r)
                        parts.append(([(ps(bank)[:, 0:240], T.me[:, 7 - k:135 - k], B("yy")[:, 1920 * h + 240 * k:1920 * h + 240 * k + 240],
                                        False, False, 240) for k in range(4 * u, 4 * u + 4)], [R("yy", r * V, r * V + V)]))
                    refit(bank, 240, parts, [], "xl", 240 * h, [], R("xl", h, h + 1))
                    spread_window("xl", h, CFG["w"][h])
                phase("keep")
                kept = "xk" if rnd else "xa"
                bank = TR
                mm([(ps(bank)[:, 0:480], T.mni[:], B(x)[:], x == old, x != old, 480) for x in (old, "xl")], ["mni", R(old), R("xl")], bank)
                act(B(new)[:], ps(bank)[:, 0:480], F.Identity, 480, ["ps%d" % bank], [R(new)], scale=-1.0)
                tt(B("mk")[:], ps(bank)[:, 0:480], B(kept)[:], A.min, 480, ["ps%d" % bank, R(kept)], [R("mk")])
                tt(B("xk")[:], B(new)[:], B("mk")[:], A.max, 480, [R(new), R("mk")], [R("xk")])
                continue
            dests = far + near + [me]

            def turned(out, k, tile, name, alone=False):
                h, u = dests[k] // 2, dests[k] % 2
                return [(out, T[name][:, u, 1 - a:129 - a], B(tile)[:, 240 * h + 120 * a:240 * h + 120 * a + 120],
                         alone and a == 0, alone and a == 1, 120) for a in range(2)]
            for name, terms in (("xa", (("xk", "md"),)), ("xb", ((old, "md7"), ("xk", "md6")))):
                mm([x[:3] + (j == 0 and x[3], j == len(terms) - 1 and x[4]) + x[5:] for k in range(N) for j, (tile, mat) in enumerate(terms)
                    for x in turned(ps(TR)[:, 120 * k:120 * k + 120], k, tile, mat, True)], ["md", "md7", "md6", R(old), R("xk")], TR)
                cp(B(name)[:], ps(TR)[:, 0:480], 480, ["ps%d" % TR], [R(name)], on="VA")
            for k0, k1 in CFG["ends"][f]:
                bank, c0, n = (TR, 4)[k0 % 2 * f], 120 * k0, 120 * (k1 - k0)
                parts = []
                mm([const(key[:, 0:n // 2], "cc1", n // 2, True)], ["cc1", "one"], KE)
                for k in range(k0, k1):
                    r = dests[k]
                    gather(r)
                    out = ps(bank)[:, 120 * (k - k0):120 * (k - k0 + 1)]
                    parts.append(([(out, T.me[:, 7 - b:135 - b], B("yy")[:, r * V + 120 * b:r * V + 120 * b + 120], False, False, 120)
                                   for b in range(8)], [R("yy", r * V, r * V + V)]))
                    mm([(key[:, 60 * (k - k0):60 * (k - k0 + 1)], cb(j, "mcf"), B("yy")[:, r * V + 60 * j:r * V + 60 * j + 60],
                         False, False, 60) for j in range(16)], ["mcf", R("yy", r * V, r * V + V)], KE)
                cols = R(new, c0, c0 + n)
                refit(bank, n, parts, [(ps(bank)[:, 0:n], T.mi1[:], B("xb")[:, c0:c0 + n], False, False, n)], new, c0, ["mi1", R("xb")], cols)
                op({"A": (lambda q, c0=c0, n=n: q.activation(B("rr")[:, c0:c0 + n], B("ns")[:, c0:c0 + n], F.Identity, bias=T.low[:, 1:2],
                                                           scale=-1.0), vc(n))}, [R("ns", c0, c0 + n), "low"], [R("rr", c0, c0 + n)])
                tt(B("mk")[:, c0:c0 + n], B("xa")[:, c0:c0 + n], B("rr")[:, c0:c0 + n], A.min, n, [R("xa"), R("rr", c0, c0 + n)],
                   [R("mk", c0, c0 + n)])
                tt(B("res")[:, k0:k1, 0:120], B(new)[:, c0:c0 + n], B("mk")[:, c0:c0 + n], A.max, n, [cols, R("mk", c0, c0 + n)],
                   [R("rx", k0, k1)])
                mm([(key[:, 60 * (k - k0):60 * (k - k0 + 1)], T.mal[:, 128 * a:128 * a + 128], B(new)[:, 120 * k + 60 * a:120 * k + 60 * a + 60],
                     False, a == 1 and k == k1 - 1, 60) for k in range(k0, k1) for a in range(2)], ["mal", cols], KE)
                ts(B("res")[:, k0:k1, 120:180], key[:, 0:n // 2], -1000.0, None, A.is_gt, None, n // 2, [kr], [R("rf", k0, k1)])
            for k, r in enumerate(dests):
                gq, o, done = 2 * r + f, OB * r, [R("rx", k, k + 1), R("rf", k, k + 1)]
                if r == me:
                    dma("S", [(T.yx[16 * gq:16 * gq + 16, :], B("res")[:, k, 0:120]), (T.yl[gq:gq + 1, :], B("res")[:, k, 120:180])], done, [])
                    continue
                name = "a" + "op"[f]
                if r in far:
                    dst, land, rsem, tail, via = plan[(me, r)][1 - f], T.ro[:], T.sem.rout, 6500.0, plan[(r, me)][1 - f]
                else:
                    dst, land, rsem, tail, via = (T.cores[r], B("lo")[:, me * OB:me * OB + 180], T.sem["%s%d" % (name, me)], 3500.0,
                                                  T.cores[r])
                on = topo.engines(core, dst)
                rid, pid = topo.addr(dst, core)
                sent[0] += len(on)
                op({"G": (lambda q, land=land, piece=B("res")[:, k, 0:180], rsem=rsem, pid=pid, rid=rid, on=on:
                          q.remote_dma(land, piece, rsem, T.sem.sent, pid, rid, _mask(on)), 800.0)}, done, [R("out", k, k + 1)])
                arrives("%s%d" % (name, r), len(topo.engines(via, core)), tail, done, [R("lo", r, r + 1)])
                dma("S", [(T.yx[16 * gq:16 * gq + 16, :], B("lo")[:, o:o + 120]), (T.yl[gq:gq + 1, :], B("lo")[:, o + 120:o + 180])],
                    [R("lo", r, r + 1)], [])
    fits = [fit(0), fit(1)]
    for rnd in range(-1, RO):
        for f in range(2):
            ahead[0], ahead[1], ahead[3] = CFG["lag"] * (1 - f), f, rnd
            next(fits[f], None)

    for sem in _emit(ops, {"V": g.vector, "A": g.scalar, "P": g.tensor, "G": g, "S": g.sync}, T):
        g.wait_ge(T.sem[sem[0]], sem[1])
    g.wait_ge(T.sem.sent, sent[0])
